import numpy as np
import ml_dtypes


def mxq(x, axis, fmt="e4m3"):
    dtype, down = {"e4m3": (ml_dtypes.float8_e4m3fn, 7), "e5m2": (ml_dtypes.float8_e5m2, 14)}[fmt]
    v = np.moveaxis(np.asarray(x, np.float32).astype(ml_dtypes.bfloat16).astype(np.float64), axis, -1)
    blocks = v.reshape(v.shape[:-1] + (-1, 32))
    amax = np.abs(blocks).max(-1, keepdims=True)
    byte = np.maximum(np.where(amax > 0, np.frexp(amax)[1] - 1 + 127, 0) - down, 1)
    scale = np.exp2(byte - 127.0)
    codes = (blocks / scale).astype(np.float32).astype(dtype).astype(np.float64)
    return np.moveaxis((codes * scale).reshape(v.shape), -1, axis)


WIDE = False


def mx_kscale(k):
    if not WIDE:
        return np.ones(k)
    levels = np.array([24, -24, 12, -12, 0])
    if k % 512:
        return np.exp2(np.random.permutation(np.resize(levels, k // 32))).repeat(32)
    a = np.empty((k // 512, 16))
    for p in range(k // 512):
        a[p, :8] = np.random.permutation(np.resize(levels, 8))
        for g in range(8):
            far = levels[np.abs(levels - a[p, g]) >= 10]
            a[p, g + 8] = far[np.random.randint(len(far))]
    return np.exp2(a.ravel()).repeat(32)


def f64(x):
    return np.asarray(x).astype(np.float64)


def striped(idx):
    return np.tile(idx.reshape(-1, 16).T, (8, 1)).astype(np.uint16)


def unstriped(offs):
    return offs[:16].T.reshape(-1).astype(np.int64)


E2M1 = np.array([0.0, 0.5, 1.0, 1.5, 2.0, 3.0, 4.0, 6.0, -0.0, -0.5, -1.0, -1.5, -2.0, -3.0, -4.0, -6.0])


def pack_weight(w, fmt):
    k, n = w.shape
    w = f64(np.asarray(w, np.float32).astype(ml_dtypes.bfloat16)).reshape(k // 32, 32, n)
    amax = np.abs(w).max(1)
    if fmt == "e4m3":
        byte = np.frexp(amax)[1] - 1 + 127 - 7
    else:
        mant, ex = np.frexp(amax / 6.0)
        byte = np.where(mant > 0.5, ex, ex - 1) + 127
    byte = np.clip(np.where(amax > 0, byte, 1), 1, 254)
    scaled = (w * np.exp2(127.0 - byte)[:, None, :]).reshape(k, n).astype(np.float32)
    by_word = np.ascontiguousarray(scaled.reshape(k // 512, 128, 4, n).transpose(0, 1, 3, 2))
    if fmt == "e4m3":
        words = by_word.astype(ml_dtypes.float8_e4m3fn).view(np.uint8)
    else:
        c = by_word.astype(ml_dtypes.float4_e2m1fn).view(np.uint8) & 0xF
        words = (c[..., 0::2] | (c[..., 1::2] << 4)).reshape(k // 512, 128, 2 * n)
    return np.ascontiguousarray(words), np.ascontiguousarray(byte.astype(np.uint8).reshape(k // 512, 16, n))


def unpack_weight(words, scales, fmt):
    g, _, n = scales.shape
    words = np.ascontiguousarray(words).reshape(g, 128, n, -1)
    if fmt == "e4m3":
        vals = words.view(ml_dtypes.float8_e4m3fn).astype(np.float64)
    else:
        nib = np.empty((g, 128, n, 4), np.uint8)
        nib[..., 0::2] = words & 0xF
        nib[..., 1::2] = words >> 4
        vals = E2M1[nib]
    vals = vals * np.repeat(np.exp2(scales.astype(np.float64) - 127.0), 8, axis=1)[..., None]
    return vals.transpose(0, 1, 3, 2).reshape(g * 512, n)


def pack_table4(v):
    words, scales = pack_weight(v, "e2m1")
    g, t = words.shape[0] // 2, v.shape[1]
    return np.ascontiguousarray(words.reshape(g, 2, 128, t, 2).transpose(0, 2, 3, 1, 4).reshape(g, 128, t, 4)), scales


def unpack_table4(words, scales):
    g, _, t, _ = words.shape
    return unpack_weight(words.reshape(g, 128, t, 2, 2).transpose(0, 3, 1, 2, 4).reshape(2 * g, 128, 2 * t), scales, "e2m1")


K, L, R, N, T, J = 1024, 512, 512, 256, 4096, 1024


def setup_inputs():
    n = np.random.standard_normal
    s = mx_kscale(K)[:, None]
    s2 = mx_kscale(L)[:, None]
    u = mx_kscale(R)[:, None]
    p_tab = pack_table4(n((K, T)) * s)
    p_tab2 = pack_weight(n((L, T)) * s2, "e4m3")
    p_wer = pack_weight(n((K, R)) / np.sqrt(K) / s * u.T, "e2m1")
    p_wei = pack_weight(n((K, R)) / np.sqrt(K) / s * u.T, "e2m1")
    p_wrr = pack_weight(n((L, R)) / np.sqrt(L) / s2, "e4m3")
    p_wri = pack_weight(n((L, R)) / np.sqrt(L) / s2, "e4m3")
    p_nr = pack_weight(n((R, N)) / np.sqrt(R) / u, "e4m3")
    p_ni = pack_weight(n((R, N)) / np.sqrt(R) / u, "e2m1")
    return {
        "tab_words": p_tab[0],
        "tab_scales": p_tab[1],
        "tab2_words": p_tab2[0],
        "tab2_scales": p_tab2[1],
        "wer_words": p_wer[0],
        "wer_scales": p_wer[1],
        "wei_words": p_wei[0],
        "wei_scales": p_wei[1],
        "wrr_words": p_wrr[0],
        "wrr_scales": p_wrr[1],
        "wri_words": p_wri[0],
        "wri_scales": p_wri[1],
        "nr_words": p_nr[0],
        "nr_scales": p_nr[1],
        "ni_words": p_ni[0],
        "ni_scales": p_ni[1],
        "offs": striped(np.random.permutation(T)[:J]),
        "offs2": striped(np.random.permutation(T)[:J]),
    }


def reference(tab_words, tab_scales, tab2_words, tab2_scales, wer_words, wer_scales, wei_words, wei_scales, wrr_words, wrr_scales, wri_words, wri_scales, nr_words, nr_scales, ni_words, ni_scales, offs, offs2):
    idx = unstriped(offs)
    idx2 = unstriped(offs2)
    tab_ = unpack_table4(tab_words, tab_scales)[:, idx]
    tab2_ = unpack_weight(tab2_words, tab2_scales, "e4m3")[:, idx2]
    wer_ = unpack_weight(wer_words, wer_scales, "e2m1")
    aer = wer_.T @ tab_
    wei_ = unpack_weight(wei_words, wei_scales, "e2m1")
    aei = wei_.T @ tab_
    wrr_ = unpack_weight(wrr_words, wrr_scales, "e4m3")
    arr = wrr_.T @ tab2_
    wri_ = unpack_weight(wri_words, wri_scales, "e4m3")
    ari = wri_.T @ tab2_
    hr = aer * arr - aei * ari
    hi = aer * ari + aei * arr
    hr_ = mxq(hr, 0, "e4m3")
    hi_ = mxq(hi, 0, "e4m3")
    nr_ = unpack_weight(nr_words, nr_scales, "e4m3")
    ni_ = unpack_weight(ni_words, ni_scales, "e2m1")
    y = nr_.T @ hr_ + ni_.T @ hi_
    return y

@@ -1,0 +1,201 @@
+from contextlib import ExitStack
+
+import concourse.mybir as mybir
+from concourse.masks import make_identity
+
+K, L, R, N, T, J = 1024, 512, 512, 256, 4096, 1024
+FLOPS = 2 * J * (2 * K * R + 2 * L * R + 2 * R * N)
+
+F32 = mybir.dt.float32
+BF16 = mybir.dt.bfloat16
+I32 = mybir.dt.int32
+U32 = mybir.dt.uint32
+U16 = mybir.dt.uint16
+U8 = mybir.dt.uint8
+FP8X4 = mybir.dt.float8_e4m3fn_x4
+FP4X4 = mybir.dt.float4_e2m1fn_x4
+MULT = mybir.AluOpType.mult
+SUBTRACT = mybir.AluOpType.subtract
+
+P = 128
+PACK = 4
+BLOCKS = J // P
+HALF = J // 2
+COL_TAB, COL_TAB2, COL_WER, COL_WEI = 0, J, 2 * J, 2 * J + 2 * R
+COL_WRR = COL_WEI + 2 * R
+COL_WRI = COL_WRR + R
+COL_NR = COL_WRI + R
+COL_NI = COL_NR + N
+COL_TAB1 = COL_NI + N
+COLS = COL_TAB1 + J
+
+
+def tile_list_ckg_none_kernel(
+    tc, tab_words, tab_scales, tab2_words, tab2_scales, wer_words, wer_scales, wei_words, wei_scales,
+    wrr_words, wrr_scales, wri_words, wri_scales, nr_words, nr_scales, ni_words, ni_scales, offs, offs2, out,
+):
+    nc = tc.nc
+    with ExitStack() as ctx:
+        keep = ctx.enter_context(tc.tile_pool(name="keep", bufs=1))
+        ring = ctx.enter_context(tc.tile_pool(name="ring", bufs=3))
+        psum = ctx.enter_context(tc.psum_pool(name="psum", bufs=1))
+
+        list1 = keep.tile([P, J // 16], U16, name="list1")
+        list2 = keep.tile([P, J // 16], U16, name="list2")
+        tab_sb = keep.tile([P, T], I32, name="tab_sb", align_bytes=64)
+        wer_sb = keep.tile([P, 2, 2 * R], U8, name="wer_sb", align_bytes=256)
+        wei_sb = keep.tile([P, 2, 2 * R], U8, name="wei_sb", align_bytes=256)
+        tab_rows = keep.tile([P, T], U8, name="tab_rows", tag="first", align_bytes=64)
+        tab2_rows = keep.tile([P, T], U8, name="tab2_rows", tag="second", align_bytes=256)
+        planes = keep.tile([P, COLS], U8, name="planes", align_bytes=256)
+        identity = keep.tile([P, P], F32, name="identity", align_bytes=64)
+
+        def words_view(ap):
+            return ap.rearrange("a p n i -> p (a n i)").bitcast(I32)
+
+        nc.vector.memset(tab_rows[:].bitcast(I32), 0)
+        nc.vector.memset(planes[:, COL_WER:COLS].bitcast(I32), 0)
+        nc.vector.memset(tab2_rows[:].bitcast(I32), 0)
+
+        nc.sync.dma_start(list1[:], offs)
+        nc.sync.dma_start(tab_sb[:], words_view(tab_words))
+        nc.scalar.dma_start(
+            tab_rows[0:P:4, :].bitcast(I32), tab_scales.rearrange("a q t -> q a t").bitcast(I32))
+        nc.sync.dma_start(list2[:], offs2)
+        nc.scalar.dma_start(tab2_rows[0:P:8, :].bitcast(I32), tab2_scales[0].bitcast(I32))
+        for col, scales in ((COL_WER, wer_scales), (COL_WEI, wei_scales), (COL_WRR, wrr_scales),
+                            (COL_WRI, wri_scales), (COL_NR, nr_scales), (COL_NI, ni_scales)):
+            passes, width = scales.shape[0], scales.shape[2]
+            nc.gpsimd.dma_start(
+                planes[0:P:8, col:col + passes * width].bitcast(I32).rearrange("q (a n) -> q a n", a=passes),
+                scales.rearrange("a q n -> q a n").bitcast(I32))
+        nc.sync.dma_start(wer_sb[:].bitcast(I32), wer_words.rearrange("a p n -> p a n").bitcast(I32))
+        nc.sync.dma_start(wei_sb[:].bitcast(I32), wei_words.rearrange("a p n -> p a n").bitcast(I32))
+        make_identity(nc, identity[:])
+
+        got_rows = keep.tile([P, J], U8, name="got_rows", tag="third", align_bytes=256)
+        nc.vector.tensor_copy(got_rows[:], tab_rows[:].indirect(list1[:]))
+        nc.scalar.dma_start(planes[0:P:8, COL_TAB1:COLS].bitcast(I32), got_rows[4:P:8, :].bitcast(I32))
+        tab2_sb = keep.tile([P, T], I32, name="tab2_sb", tag="first", align_bytes=64)
+        nc.scalar.dma_start(tab2_sb[:], words_view(tab2_words))
+        nc.vector.tensor_copy(planes[:, COL_TAB:COL_TAB + J].bitcast(I32), got_rows[:].bitcast(I32))
+        got2_rows = keep.tile([P, J], U8, name="got2_rows", align_bytes=64)
+        nc.vector.tensor_copy(got2_rows[:], tab2_rows[:].indirect(list2[:]))
+        nc.vector.tensor_copy(planes[:, COL_TAB2:COL_TAB2 + J].bitcast(I32), got2_rows[:].bitcast(I32))
+        wr_sb = keep.tile([P, 2, R], I32, name="wr_sb", tag="third", align_bytes=256)
+        nc.scalar.dma_start(wr_sb[:, 0, :], words_view(wrr_words))
+        nc.scalar.dma_start(wr_sb[:, 1, :], words_view(wri_words))
+        for r in range(1, 4):
+            nc.sync.dma_start(planes[r:P:32, :].bitcast(I32), planes[8 * r:P:32, :].bitcast(I32))
+
+        ent_words, rel_words = [], []
+        for h in range(2):
+            pairs = keep.tile([P, HALF], U32, name=f"pairs{h}", tag="second", align_bytes=256)
+            nc.vector.tensor_copy(pairs[:], tab_sb[:].bitcast(U32).indirect(list1[:, 32 * h:32 * h + 32]))
+            parted = keep.tile([P, 2, HALF], U16, name=f"parted{h}", align_bytes=256)
+            nc.vector.tensor_copy(parted[:], pairs[:].bitcast(U16).rearrange("p (j d) -> p d j", d=2))
+            ent_words.append(parted)
+        cand_sb = keep.tile([P, 6 * N], U8, name="cand_sb", tag="second", align_bytes=256)
+        nc.sync.dma_start(cand_sb[:, 0:4 * N].bitcast(I32), words_view(nr_words))
+        nc.sync.dma_start(cand_sb[:, 4 * N:6 * N].bitcast(I32), ni_words[0].bitcast(I32))
+        for h in range(2):
+            picked = keep.tile([P, HALF], U32, name=f"picked{h}", align_bytes=256)
+            nc.vector.tensor_copy(picked[:], tab2_sb[:].bitcast(U32).indirect(list2[:, 32 * h:32 * h + 32]))
+            rel_words.append(picked)
+
+        def dealt(bank):
+            return bank[:].rearrange("j (m t) -> j t m", t=PACK)
+
+        ent, rel, prod, diff, turned, quant = {}, {}, {}, {}, {}, {}
+
+        def project_entity(b):
+            h, j0 = divmod(b * P, HALF)
+            ent[b] = keep.tile([P, 2, PACK, P], F32, name=f"ent{b}")
+            for c, (w_sb, col) in enumerate(((wer_sb, COL_WER), (wei_sb, COL_WEI))):
+                bank = psum.tile([P, R], F32, name="ent_bank", bufs=2)
+                for a in range(2):
+                    plane = planes[:, (COL_TAB, COL_TAB1)[a] + b * P:(COL_TAB, COL_TAB1)[a] + (b + 1) * P]
+                    nc.tensor.matmul_mx(
+                        out=bank[:], lhsT=ent_words[h][:, a, j0:j0 + P].bitcast(FP4X4), lhsT_scale=plane,
+                        rhs=w_sb[:, a, :].bitcast(FP4X4), rhs_scale=planes[:, col + a * R:col + (a + 1) * R],
+                        start=(a == 0), stop=(a == 1))
+                nc.scalar.copy(ent[b][:, c], dealt(bank))
+
+        def project_relation(b):
+            h, j0 = divmod(b * P, HALF)
+            rel[b] = []
+            for c, col in enumerate((COL_WRR, COL_WRI)):
+                bank = psum.tile([P, R], F32, name="rel_bank", bufs=3)
+                nc.tensor.matmul_mx(
+                    out=bank[:], lhsT=rel_words[h][:, j0:j0 + P].bitcast(FP8X4),
+                    lhsT_scale=planes[:, COL_TAB2 + b * P:COL_TAB2 + (b + 1) * P],
+                    rhs=wr_sb[:, c, :].bitcast(FP8X4), rhs_scale=planes[:, col:col + R], start=True, stop=True)
+                rel[b].append(bank)
+
+        def multiply(b):
+            prod[b] = []
+            for c in range(2):
+                both = ring.tile([P, 2, PACK, P], F32, name=f"prod{c}")
+                nc.vector.tensor_tensor(
+                    both[:], dealt(rel[b][c]).unsqueeze(1).to_broadcast([P, 2, PACK, P]), ent[b][:], MULT)
+                prod[b].append(both)
+
+        def subtract(b):
+            diff[b] = ring.tile([P, PACK, P], F32, name="diff")
+            engine = nc.vector if b == BLOCKS - 1 else nc.gpsimd
+            engine.tensor_tensor(diff[b][:], prod[b][0][:, 0], prod[b][1][:, 1], SUBTRACT)
+
+        def turn(b):
+            turned[b] = ring.tile([P, 2, P, PACK], BF16, name="turned", align_bytes=64)
+            hi_bank = psum.tile([P, PACK, P], F32, name="turn_bank", bufs=2)
+            for t in range(PACK):
+                nc.tensor.matmul(hi_bank[:, t, :], prod[b][0][:, 1, t, :], identity[:],
+                                 start=True, stop=False, is_transpose=True)
+                nc.tensor.matmul(hi_bank[:, t, :], prod[b][1][:, 0, t, :], identity[:],
+                                 start=False, stop=True, is_transpose=True)
+            nc.scalar.copy(turned[b][:, 1], hi_bank[:].rearrange("p t j -> p j t"))
+            hr_bank = psum.tile([P, PACK, P], F32, name="turn_bank", bufs=2)
+            for t in range(PACK):
+                nc.tensor.transpose(hr_bank[:, t, :], diff[b][:, t, :], identity[:])
+            nc.scalar.copy(turned[b][:, 0], hr_bank[:].rearrange("p t j -> p j t"))
+
+        def quantise(b):
+            codes = ring.tile([P, 2 * P], U32, name="codes", align_bytes=256)
+            scales = ring.tile([P, 2 * P], U8, name="scales", align_bytes=256)
+            nc.vector.quantize_mx(out=codes[:].bitcast(FP8X4), scales=scales[:],
+                                  in_=turned[b][:].rearrange("p c j t -> p (c j t)"))
+            quant[b] = (codes, scales)
+
+        def score(b):
+            codes, scales = quant[b]
+            bank = psum.tile([P, 2, P], F32, name="score_bank", bufs=1)
+            for g in range(2):
+                nc.tensor.matmul_mx(
+                    out=bank[:, g, :], lhsT=cand_sb[:, 4 * P * g:4 * P * (g + 1)].bitcast(FP8X4),
+                    lhsT_scale=planes[:, COL_NR + g * P:COL_NR + (g + 1) * P],
+                    rhs=codes[:, 0:P].bitcast(FP8X4), rhs_scale=scales[:, 0:P], start=True, stop=False)
+                nc.tensor.matmul_mx(
+                    out=bank[:, g, :], lhsT=cand_sb[:, 4 * N + 2 * P * g:4 * N + 2 * P * (g + 1)].bitcast(FP4X4),
+                    lhsT_scale=planes[:, COL_NI + g * P:COL_NI + (g + 1) * P],
+                    rhs=codes[:, P:2 * P].bitcast(FP8X4), rhs_scale=scales[:, P:2 * P], start=False, stop=True)
+            result = ring.tile([P, 2, P], F32, name="result")
+            nc.scalar.copy(result[:], bank[:])
+            nc.sync.dma_start(out[:, b * P:(b + 1) * P].rearrange("(g n) j -> n g j", g=2), result[:])
+
+        AHEAD = 2
+        for b in range(AHEAD):
+            project_entity(b)
+        project_relation(0)
+        for step in range(BLOCKS + 2):
+            if step < BLOCKS:
+                multiply(step)
+                subtract(step)
+            if step + 1 < BLOCKS:
+                project_relation(step + 1)
+            if 0 <= step - 1 < BLOCKS:
+                turn(step - 1)
+            if 0 <= step - 2 < BLOCKS:
+                quantise(step - 2)
+                score(step - 2)
+            if step + AHEAD < BLOCKS:
+                project_entity(step + AHEAD)

@@ -16,18 +16,17 @@ FP8X4 = mybir.dt.float8_e4m3fn_x4
 FP4X4 = mybir.dt.float4_e2m1fn_x4
 MULT = mybir.AluOpType.mult
 SUBTRACT = mybir.AluOpType.subtract
+ADD = mybir.AluOpType.add
 
 P = 128
 PACK = 4
 BLOCKS = J // P
 HALF = J // 2
-COL_TAB, COL_TAB2, COL_WER, COL_WEI = 0, J, 2 * J, 2 * J + 2 * R
-COL_WRR = COL_WEI + 2 * R
-COL_WRI = COL_WRR + R
-COL_NR = COL_WRI + R
-COL_NI = COL_NR + N
-COL_TAB1 = COL_NI + N
-COLS = COL_TAB1 + J
+AHEAD = 2
+COL_WER, COL_WEI, COLS_ENT = J, J + 2 * R, J + 4 * R
+COL_WRR, COL_WRI, COL_NR, COL_NI, COLS_REL = J, J + R, J + 2 * R, J + 2 * R + N, J + 2 * R + 2 * N
+SUMMED_ON_TENSOR = (1, 3, 5)
+LAST = BLOCKS - 1
 
 
 def tile_list_ckg_none_kernel(
@@ -42,51 +41,66 @@ def tile_list_ckg_none_kernel(
 
         list1 = keep.tile([P, J // 16], U16, name="list1")
         list2 = keep.tile([P, J // 16], U16, name="list2")
-        tab_sb = keep.tile([P, T], I32, name="tab_sb", align_bytes=64)
+        zeros = keep.tile([P, 2 * N // 4], I32, name="zeros", tag="table", align_bytes=64)
         wer_sb = keep.tile([P, 2, 2 * R], U8, name="wer_sb", align_bytes=256)
         wei_sb = keep.tile([P, 2, 2 * R], U8, name="wei_sb", align_bytes=256)
-        tab_rows = keep.tile([P, T], U8, name="tab_rows", tag="first", align_bytes=64)
+        tab_rows = keep.tile([P, T], U8, name="tab_rows", align_bytes=64)
         tab2_rows = keep.tile([P, T], U8, name="tab2_rows", tag="second", align_bytes=256)
-        planes = keep.tile([P, COLS], U8, name="planes", align_bytes=256)
+        ent_planes = keep.tile([P, COLS_ENT], U8, name="ent_planes", align_bytes=256)
+        ent_plane1 = keep.tile([P, J], U8, name="ent_plane1", align_bytes=256)
+        rel_rows = keep.tile([P, COLS_REL], U8, name="rel_rows", align_bytes=256)
+        rel_planes = keep.tile([P, COLS_REL], U8, name="rel_planes", align_bytes=256)
         identity = keep.tile([P, P], F32, name="identity", align_bytes=64)
 
         def words_view(ap):
             return ap.rearrange("a p n i -> p (a n i)").bitcast(I32)
 
-        nc.vector.memset(tab_rows[:].bitcast(I32), 0)
-        nc.vector.memset(planes[:, COL_WER:COLS].bitcast(I32), 0)
+        def load_scale_rows(queue, rows, scales):
+            queue.dma_start(rows.bitcast(I32).rearrange("q (a n) -> q a n", a=scales.shape[0]),
+                            scales.rearrange("a q n -> q a n").bitcast(I32))
+
+        nc.vector.memset(tab_rows[32:64, :].bitcast(I32), 0)
+        nc.vector.memset(tab_rows[64:P, :].bitcast(I32), 0)
+        nc.vector.memset(ent_planes[:, COL_WER:COLS_ENT].bitcast(I32), 0)
         nc.vector.memset(tab2_rows[:].bitcast(I32), 0)
+        nc.vector.memset(zeros[:], 0)
+        nc.vector.tensor_copy(rel_planes[:, COL_NR:COLS_REL].bitcast(I32), zeros[:])
+        for col, scales in ((COL_WRR, wrr_scales), (COL_WRI, wri_scales), (COL_NR, nr_scales), (COL_NI, ni_scales)):
+            load_scale_rows(nc.gpsimd, rel_rows[0:P:8, col:col + scales.shape[2]], scales)
 
         nc.sync.dma_start(list1[:], offs)
-        nc.sync.dma_start(tab_sb[:], words_view(tab_words))
-        nc.scalar.dma_start(
-            tab_rows[0:P:4, :].bitcast(I32), tab_scales.rearrange("a q t -> q a t").bitcast(I32))
+        nc.sync.dma_start(tab_rows[0:32, :].bitcast(I32), tab_scales.rearrange("a q t -> (a q) t").bitcast(I32))
         nc.sync.dma_start(list2[:], offs2)
-        nc.scalar.dma_start(tab2_rows[0:P:8, :].bitcast(I32), tab2_scales[0].bitcast(I32))
-        for col, scales in ((COL_WER, wer_scales), (COL_WEI, wei_scales), (COL_WRR, wrr_scales),
-                            (COL_WRI, wri_scales), (COL_NR, nr_scales), (COL_NI, ni_scales)):
-            passes, width = scales.shape[0], scales.shape[2]
-            nc.gpsimd.dma_start(
-                planes[0:P:8, col:col + passes * width].bitcast(I32).rearrange("q (a n) -> q a n", a=passes),
-                scales.rearrange("a q n -> q a n").bitcast(I32))
         nc.sync.dma_start(wer_sb[:].bitcast(I32), wer_words.rearrange("a p n -> p a n").bitcast(I32))
         nc.sync.dma_start(wei_sb[:].bitcast(I32), wei_words.rearrange("a p n -> p a n").bitcast(I32))
-        make_identity(nc, identity[:])
+        load_scale_rows(nc.sync, ent_planes[0:16, COL_WER:COL_WEI], wer_scales)
+        load_scale_rows(nc.sync, ent_planes[0:16, COL_WEI:COLS_ENT], wei_scales)
+        nc.sync.dma_start(tab2_rows[0:P:8, :].bitcast(I32), tab2_scales[0].bitcast(I32))
+        tab_sb = keep.tile([P, T], I32, name="tab_sb", tag="table", align_bytes=64)
+        nc.sync.dma_start(tab_sb[:], words_view(tab_words))
 
-        got_rows = keep.tile([P, J], U8, name="got_rows", tag="third", align_bytes=256)
+        got_rows = keep.tile([P, J], U8, name="got_rows", align_bytes=256)
+        nc.vector.memset(ent_plane1[:].bitcast(I32), 0)
         nc.vector.tensor_copy(got_rows[:], tab_rows[:].indirect(list1[:]))
-        nc.scalar.dma_start(planes[0:P:8, COL_TAB1:COLS].bitcast(I32), got_rows[4:P:8, :].bitcast(I32))
-        tab2_sb = keep.tile([P, T], I32, name="tab2_sb", tag="first", align_bytes=64)
-        nc.scalar.dma_start(tab2_sb[:], words_view(tab2_words))
-        nc.vector.tensor_copy(planes[:, COL_TAB:COL_TAB + J].bitcast(I32), got_rows[:].bitcast(I32))
-        got2_rows = keep.tile([P, J], U8, name="got2_rows", align_bytes=64)
-        nc.vector.tensor_copy(got2_rows[:], tab2_rows[:].indirect(list2[:]))
-        nc.vector.tensor_copy(planes[:, COL_TAB2:COL_TAB2 + J].bitcast(I32), got2_rows[:].bitcast(I32))
-        wr_sb = keep.tile([P, 2, R], I32, name="wr_sb", tag="third", align_bytes=256)
-        nc.scalar.dma_start(wr_sb[:, 0, :], words_view(wrr_words))
-        nc.scalar.dma_start(wr_sb[:, 1, :], words_view(wri_words))
-        for r in range(1, 4):
-            nc.sync.dma_start(planes[r:P:32, :].bitcast(I32), planes[8 * r:P:32, :].bitcast(I32))
+        nc.vector.tensor_copy(ent_planes[:, 0:J].bitcast(I32), got_rows[:].bitcast(I32))
+        for quadrant in range(4):
+            queue = nc.gpsimd if quadrant == 0 else nc.sync
+            queue.dma_start(ent_plane1[32 * quadrant:32 * quadrant + 4, :].bitcast(I32),
+                            got_rows[16 + 4 * quadrant:20 + 4 * quadrant, :].bitcast(I32))
+        for quadrant in range(1, 4):
+            nc.sync.dma_start(ent_planes[32 * quadrant:32 * quadrant + 4, :].bitcast(I32),
+                              ent_planes[4 * quadrant:4 * quadrant + 4, :].bitcast(I32))
+        make_identity(nc, identity[:])
+        nc.vector.memset(rel_planes[:, 0:COL_NR].bitcast(I32), 0)
+        for h in range(2):
+            got2_rows = keep.tile([P, HALF], U8, name=f"got2_rows{h}", tag=f"gathered{h}", align_bytes=256)
+            nc.vector.tensor_copy(got2_rows[:], tab2_rows[:].indirect(list2[:, 32 * h:32 * h + 32]))
+            nc.vector.tensor_copy(
+                rel_rows[:, h * HALF:(h + 1) * HALF].bitcast(I32), got2_rows[:].bitcast(I32))
+        tab2_sb = keep.tile([P, T], I32, name="tab2_sb", tag="gathered0", align_bytes=256)
+        nc.sync.dma_start(tab2_sb[:], words_view(tab2_words))
+        for base in range(0, P, 32):
+            nc.sync.dma_start(rel_planes[base:base + 4, :].bitcast(I32), rel_rows[base:base + 32:8, :].bitcast(I32))
 
         ent_words, rel_words = [], []
         for h in range(2):
@@ -95,6 +109,9 @@ def tile_list_ckg_none_kernel(
             parted = keep.tile([P, 2, HALF], U16, name=f"parted{h}", align_bytes=256)
             nc.vector.tensor_copy(parted[:], pairs[:].bitcast(U16).rearrange("p (j d) -> p d j", d=2))
             ent_words.append(parted)
+        wr_sb = keep.tile([P, 2, R], I32, name="wr_sb", tag="gathered1", align_bytes=256)
+        nc.sync.dma_start(wr_sb[:, 0, :], words_view(wrr_words))
+        nc.sync.dma_start(wr_sb[:, 1, :], words_view(wri_words))
         cand_sb = keep.tile([P, 6 * N], U8, name="cand_sb", tag="second", align_bytes=256)
         nc.sync.dma_start(cand_sb[:, 0:4 * N].bitcast(I32), words_view(nr_words))
         nc.sync.dma_start(cand_sb[:, 4 * N:6 * N].bitcast(I32), ni_words[0].bitcast(I32))
@@ -103,23 +120,25 @@ def tile_list_ckg_none_kernel(
             nc.vector.tensor_copy(picked[:], tab2_sb[:].bitcast(U32).indirect(list2[:, 32 * h:32 * h + 32]))
             rel_words.append(picked)
 
-        def dealt(bank):
-            return bank[:].rearrange("j (m t) -> j t m", t=PACK)
+        def ordered(bank, b):
+            if b in SUMMED_ON_TENSOR:
+                return bank[:].rearrange("j (m t) -> j t m", t=PACK)
+            return bank[:].rearrange("j (t m) -> j t m", t=PACK)
 
         ent, rel, prod, diff, turned, quant = {}, {}, {}, {}, {}, {}
 
         def project_entity(b):
             h, j0 = divmod(b * P, HALF)
-            ent[b] = keep.tile([P, 2, PACK, P], F32, name=f"ent{b}")
+            ent[b] = ring.tile([P, 2, PACK, P], F32, name="ent", bufs=2)
             for c, (w_sb, col) in enumerate(((wer_sb, COL_WER), (wei_sb, COL_WEI))):
                 bank = psum.tile([P, R], F32, name="ent_bank", bufs=2)
                 for a in range(2):
-                    plane = planes[:, (COL_TAB, COL_TAB1)[a] + b * P:(COL_TAB, COL_TAB1)[a] + (b + 1) * P]
+                    plane = (ent_planes, ent_plane1)[a][:, b * P:(b + 1) * P]
                     nc.tensor.matmul_mx(
                         out=bank[:], lhsT=ent_words[h][:, a, j0:j0 + P].bitcast(FP4X4), lhsT_scale=plane,
-                        rhs=w_sb[:, a, :].bitcast(FP4X4), rhs_scale=planes[:, col + a * R:col + (a + 1) * R],
+                        rhs=w_sb[:, a, :].bitcast(FP4X4), rhs_scale=ent_planes[:, col + a * R:col + (a + 1) * R],
                         start=(a == 0), stop=(a == 1))
-                nc.scalar.copy(ent[b][:, c], dealt(bank))
+                nc.scalar.copy(ent[b][:, c], ordered(bank, b))
 
         def project_relation(b):
             h, j0 = divmod(b * P, HALF)
@@ -128,8 +147,8 @@ def tile_list_ckg_none_kernel(
                 bank = psum.tile([P, R], F32, name="rel_bank", bufs=3)
                 nc.tensor.matmul_mx(
                     out=bank[:], lhsT=rel_words[h][:, j0:j0 + P].bitcast(FP8X4),
-                    lhsT_scale=planes[:, COL_TAB2 + b * P:COL_TAB2 + (b + 1) * P],
-                    rhs=wr_sb[:, c, :].bitcast(FP8X4), rhs_scale=planes[:, col:col + R], start=True, stop=True)
+                    lhsT_scale=rel_planes[:, b * P:(b + 1) * P],
+                    rhs=wr_sb[:, c, :].bitcast(FP8X4), rhs_scale=rel_planes[:, col:col + R], start=True, stop=True)
                 rel[b].append(bank)
 
         def multiply(b):
@@ -137,16 +156,31 @@ def tile_list_ckg_none_kernel(
             for c in range(2):
                 both = ring.tile([P, 2, PACK, P], F32, name=f"prod{c}")
                 nc.vector.tensor_tensor(
-                    both[:], dealt(rel[b][c]).unsqueeze(1).to_broadcast([P, 2, PACK, P]), ent[b][:], MULT)
+                    both[:], ordered(rel[b][c], b).unsqueeze(1).to_broadcast([P, 2, PACK, P]), ent[b][:], MULT)
                 prod[b].append(both)
 
         def subtract(b):
-            diff[b] = ring.tile([P, PACK, P], F32, name="diff")
-            engine = nc.vector if b == BLOCKS - 1 else nc.gpsimd
-            engine.tensor_tensor(diff[b][:], prod[b][0][:, 0], prod[b][1][:, 1], SUBTRACT)
+            engine = nc.gpsimd
+            if b in SUMMED_ON_TENSOR:
+                diff[b] = ring.tile([P, PACK, P], F32, name="diff")
+                engine.tensor_tensor(diff[b][:], prod[b][0][:, 0], prod[b][1][:, 1], SUBTRACT)
+                return
+            diff[b] = ring.tile([P, 2, PACK, P], BF16, name="pair", align_bytes=64)
+            engine.tensor_tensor(diff[b][:, 0], prod[b][0][:, 0], prod[b][1][:, 1], SUBTRACT)
+            engine.tensor_tensor(diff[b][:, 1], prod[b][0][:, 1], prod[b][1][:, 0], ADD)
 
         def turn(b):
             turned[b] = ring.tile([P, 2, P, PACK], BF16, name="turned", align_bytes=64)
+            if b not in SUMMED_ON_TENSOR:
+                bank = psum.tile([P, 2, 2, P], F32, name="turn_bank", bufs=2)
+                words = diff[b][:].rearrange("j c t m -> j (c t m)").bitcast(F32).rearrange("j (c p u) -> j c u p", c=2, u=2)
+                for c in range(2):
+                    for u in range(2):
+                        nc.tensor.transpose(bank[:, c, u, :], words[:, c, u, :], identity[:])
+                nc.scalar.copy(
+                    turned[b][:].rearrange("p c j t -> p (c j t)").bitcast(F32).rearrange("p (c j u) -> p c j u", c=2, u=2),
+                    bank[:].rearrange("p c u j -> p c j u"))
+                return
             hi_bank = psum.tile([P, PACK, P], F32, name="turn_bank", bufs=2)
             for t in range(PACK):
                 nc.tensor.matmul(hi_bank[:, t, :], prod[b][0][:, 1, t, :], identity[:],
@@ -166,36 +200,61 @@ def tile_list_ckg_none_kernel(
                                   in_=turned[b][:].rearrange("p c j t -> p (c j t)"))
             quant[b] = (codes, scales)
 
+        def finish_last():
+            codes = ring.tile([P, 2 * P], U32, name="codes", align_bytes=256)
+            scales = ring.tile([P, 2 * P], U8, name="scales", align_bytes=256)
+            arr, ari = rel[LAST]
+            aer, aei = (ent[LAST][:, c].rearrange("j t m -> j (t m)") for c in range(2))
+            for c, (first, second, op) in enumerate(((aer, aei, SUBTRACT), (aei, aer, ADD))):
+                left = ring.tile([P, R], F32, name="left", bufs=2)
+                nc.vector.tensor_tensor(left[:], arr[:], first, MULT)
+                right = ring.tile([P, R], F32, name="right", bufs=2)
+                nc.vector.tensor_tensor(right[:], ari[:], second, MULT)
+                part = ring.tile([P, R], BF16, name="part", bufs=2, align_bytes=64)
+                nc.vector.tensor_tensor(part[:], left[:], right[:], op)
+                bank = psum.tile([P, 2, P], F32, name="turn_bank", bufs=2)
+                words = part[:].bitcast(F32).rearrange("j (p u) -> j u p", u=2)
+                for u in range(2):
+                    nc.tensor.transpose(bank[:, u, :], words[:, u, :], identity[:])
+                part_turned = ring.tile([P, P * PACK], BF16, name="part_turned", bufs=2, align_bytes=64)
+                nc.scalar.copy(part_turned[:].bitcast(F32).rearrange("p (j u) -> p j u", u=2),
+                               bank[:].rearrange("p u j -> p j u"))
+                nc.vector.quantize_mx(out=codes[:, c * P:(c + 1) * P].bitcast(FP8X4),
+                                      scales=scales[:, c * P:(c + 1) * P], in_=part_turned[:])
+            quant[LAST] = (codes, scales)
+
         def score(b):
             codes, scales = quant[b]
             bank = psum.tile([P, 2, P], F32, name="score_bank", bufs=1)
             for g in range(2):
                 nc.tensor.matmul_mx(
                     out=bank[:, g, :], lhsT=cand_sb[:, 4 * P * g:4 * P * (g + 1)].bitcast(FP8X4),
-                    lhsT_scale=planes[:, COL_NR + g * P:COL_NR + (g + 1) * P],
+                    lhsT_scale=rel_planes[:, COL_NR + g * P:COL_NR + (g + 1) * P],
                     rhs=codes[:, 0:P].bitcast(FP8X4), rhs_scale=scales[:, 0:P], start=True, stop=False)
                 nc.tensor.matmul_mx(
                     out=bank[:, g, :], lhsT=cand_sb[:, 4 * N + 2 * P * g:4 * N + 2 * P * (g + 1)].bitcast(FP4X4),
-                    lhsT_scale=planes[:, COL_NI + g * P:COL_NI + (g + 1) * P],
+                    lhsT_scale=rel_planes[:, COL_NI + g * P:COL_NI + (g + 1) * P],
                     rhs=codes[:, P:2 * P].bitcast(FP8X4), rhs_scale=scales[:, P:2 * P], start=False, stop=True)
             result = ring.tile([P, 2, P], F32, name="result")
             nc.scalar.copy(result[:], bank[:])
             nc.sync.dma_start(out[:, b * P:(b + 1) * P].rearrange("(g n) j -> n g j", g=2), result[:])
 
-        AHEAD = 2
         for b in range(AHEAD):
             project_entity(b)
         project_relation(0)
-        for step in range(BLOCKS + 2):
-            if step < BLOCKS:
+        for step in range(BLOCKS + 1):
+            if step < LAST:
                 multiply(step)
                 subtract(step)
             if step + 1 < BLOCKS:
                 project_relation(step + 1)
-            if 0 <= step - 1 < BLOCKS:
+            if 0 <= step - 1 < LAST:
                 turn(step - 1)
-            if 0 <= step - 2 < BLOCKS:
+            if step == LAST:
+                finish_last()
+            if 0 <= step - 2:
                 quantise(step - 2)
                 score(step - 2)
             if step + AHEAD < BLOCKS:
                 project_entity(step + AHEAD)
+        score(LAST)

@@ -24,8 +24,7 @@ BLOCKS = J // P
 HALF = J // 2
 AHEAD = 2
 COL_WER, COL_WEI, COLS_ENT = J, J + 2 * R, J + 4 * R
-COL_WRR, COL_WRI, COL_NR, COL_NI, COLS_REL = J, J + R, J + 2 * R, J + 2 * R + N, J + 2 * R + 2 * N
-SUMMED_ON_TENSOR = (1, 3, 5)
+COL_WRR, COL_WRI, COLS_REL = J, J + R, J + 2 * R
 LAST = BLOCKS - 1
 
 
@@ -41,15 +40,14 @@ def tile_list_ckg_none_kernel(
 
         list1 = keep.tile([P, J // 16], U16, name="list1")
         list2 = keep.tile([P, J // 16], U16, name="list2")
-        zeros = keep.tile([P, 2 * N // 4], I32, name="zeros", tag="table", align_bytes=64)
+        zeros = keep.tile([P, J // 4], I32, name="zeros", tag="table", align_bytes=64)
         wer_sb = keep.tile([P, 2, 2 * R], U8, name="wer_sb", align_bytes=256)
         wei_sb = keep.tile([P, 2, 2 * R], U8, name="wei_sb", align_bytes=256)
-        tab_rows = keep.tile([P, T], U8, name="tab_rows", align_bytes=64)
+        tab_rows = keep.tile([P, T], U8, name="tab_rows", tag="first", align_bytes=256)
         tab2_rows = keep.tile([P, T], U8, name="tab2_rows", tag="second", align_bytes=256)
         ent_planes = keep.tile([P, COLS_ENT], U8, name="ent_planes", align_bytes=256)
         ent_plane1 = keep.tile([P, J], U8, name="ent_plane1", align_bytes=256)
         rel_rows = keep.tile([P, COLS_REL], U8, name="rel_rows", align_bytes=256)
-        rel_planes = keep.tile([P, COLS_REL], U8, name="rel_planes", align_bytes=256)
         identity = keep.tile([P, P], F32, name="identity", align_bytes=64)
 
         def words_view(ap):
@@ -59,14 +57,14 @@ def tile_list_ckg_none_kernel(
             queue.dma_start(rows.bitcast(I32).rearrange("q (a n) -> q a n", a=scales.shape[0]),
                             scales.rearrange("a q n -> q a n").bitcast(I32))
 
-        nc.vector.memset(tab_rows[32:64, :].bitcast(I32), 0)
-        nc.vector.memset(tab_rows[64:P, :].bitcast(I32), 0)
-        nc.vector.memset(ent_planes[:, COL_WER:COLS_ENT].bitcast(I32), 0)
+        nc.gpsimd.memset(tab_rows[32:64, :].bitcast(I32), 0)
+        nc.gpsimd.memset(ent_planes[:, COL_WER:COLS_ENT].bitcast(I32), 0)
         nc.vector.memset(tab2_rows[:].bitcast(I32), 0)
         nc.vector.memset(zeros[:], 0)
-        nc.vector.tensor_copy(rel_planes[:, COL_NR:COLS_REL].bitcast(I32), zeros[:])
-        for col, scales in ((COL_WRR, wrr_scales), (COL_WRI, wri_scales), (COL_NR, nr_scales), (COL_NI, ni_scales)):
-            load_scale_rows(nc.gpsimd, rel_rows[0:P:8, col:col + scales.shape[2]], scales)
+        nc.vector.tensor_copy(ent_plane1[:].bitcast(I32), zeros[:])
+        nc.vector.memset(tab_rows[64:P, :].bitcast(I32), 0)
+        load_scale_rows(nc.gpsimd, rel_rows[0:P:8, COL_WRR:COL_WRI], wrr_scales)
+        load_scale_rows(nc.gpsimd, rel_rows[0:P:8, COL_WRI:COLS_REL], wri_scales)
 
         nc.sync.dma_start(list1[:], offs)
         nc.sync.dma_start(tab_rows[0:32, :].bitcast(I32), tab_scales.rearrange("a q t -> (a q) t").bitcast(I32))
@@ -80,7 +78,6 @@ def tile_list_ckg_none_kernel(
         nc.sync.dma_start(tab_sb[:], words_view(tab_words))
 
         got_rows = keep.tile([P, J], U8, name="got_rows", align_bytes=256)
-        nc.vector.memset(ent_plane1[:].bitcast(I32), 0)
         nc.vector.tensor_copy(got_rows[:], tab_rows[:].indirect(list1[:]))
         nc.vector.tensor_copy(ent_planes[:, 0:J].bitcast(I32), got_rows[:].bitcast(I32))
         for quadrant in range(4):
@@ -91,7 +88,6 @@ def tile_list_ckg_none_kernel(
             nc.sync.dma_start(ent_planes[32 * quadrant:32 * quadrant + 4, :].bitcast(I32),
                               ent_planes[4 * quadrant:4 * quadrant + 4, :].bitcast(I32))
         make_identity(nc, identity[:])
-        nc.vector.memset(rel_planes[:, 0:COL_NR].bitcast(I32), 0)
         for h in range(2):
             got2_rows = keep.tile([P, HALF], U8, name=f"got2_rows{h}", tag=f"gathered{h}", align_bytes=256)
             nc.vector.tensor_copy(got2_rows[:], tab2_rows[:].indirect(list2[:, 32 * h:32 * h + 32]))
@@ -99,6 +95,8 @@ def tile_list_ckg_none_kernel(
                 rel_rows[:, h * HALF:(h + 1) * HALF].bitcast(I32), got2_rows[:].bitcast(I32))
         tab2_sb = keep.tile([P, T], I32, name="tab2_sb", tag="gathered0", align_bytes=256)
         nc.sync.dma_start(tab2_sb[:], words_view(tab2_words))
+        rel_planes = keep.tile([P, COLS_REL], U8, name="rel_planes", tag="first", align_bytes=256)
+        nc.vector.memset(rel_planes[:].bitcast(I32), 0)
         for base in range(0, P, 32):
             nc.sync.dma_start(rel_planes[base:base + 4, :].bitcast(I32), rel_rows[base:base + 32:8, :].bitcast(I32))
 
@@ -115,21 +113,22 @@ def tile_list_ckg_none_kernel(
         cand_sb = keep.tile([P, 6 * N], U8, name="cand_sb", tag="second", align_bytes=256)
         nc.sync.dma_start(cand_sb[:, 0:4 * N].bitcast(I32), words_view(nr_words))
         nc.sync.dma_start(cand_sb[:, 4 * N:6 * N].bitcast(I32), ni_words[0].bitcast(I32))
+        cand_planes = keep.tile([P, 2, N], U8, name="cand_planes", tag="table", align_bytes=64)
+        nc.vector.memset(cand_planes[:].bitcast(I32), 0)
+        for c, scales in enumerate((nr_scales, ni_scales)):
+            for quadrant in range(4):
+                nc.sync.dma_start(cand_planes[32 * quadrant:32 * quadrant + 4, c, :].bitcast(I32),
+                                  scales[0, 4 * quadrant:4 * quadrant + 4, :].bitcast(I32))
         for h in range(2):
             picked = keep.tile([P, HALF], U32, name=f"picked{h}", align_bytes=256)
             nc.vector.tensor_copy(picked[:], tab2_sb[:].bitcast(U32).indirect(list2[:, 32 * h:32 * h + 32]))
             rel_words.append(picked)
 
-        def ordered(bank, b):
-            if b in SUMMED_ON_TENSOR:
-                return bank[:].rearrange("j (m t) -> j t m", t=PACK)
-            return bank[:].rearrange("j (t m) -> j t m", t=PACK)
-
-        ent, rel, prod, diff, turned, quant = {}, {}, {}, {}, {}, {}
+        ent, rel, prod, summed, turned, quant = {}, {}, {}, {}, {}, {}
 
         def project_entity(b):
             h, j0 = divmod(b * P, HALF)
-            ent[b] = ring.tile([P, 2, PACK, P], F32, name="ent", bufs=2)
+            ent[b] = ring.tile([P, 2, R], F32, name="ent", bufs=2)
             for c, (w_sb, col) in enumerate(((wer_sb, COL_WER), (wei_sb, COL_WEI))):
                 bank = psum.tile([P, R], F32, name="ent_bank", bufs=2)
                 for a in range(2):
@@ -138,7 +137,7 @@ def tile_list_ckg_none_kernel(
                         out=bank[:], lhsT=ent_words[h][:, a, j0:j0 + P].bitcast(FP4X4), lhsT_scale=plane,
                         rhs=w_sb[:, a, :].bitcast(FP4X4), rhs_scale=ent_planes[:, col + a * R:col + (a + 1) * R],
                         start=(a == 0), stop=(a == 1))
-                nc.scalar.copy(ent[b][:, c], ordered(bank, b))
+                nc.scalar.copy(ent[b][:, c, :], bank[:])
 
         def project_relation(b):
             h, j0 = divmod(b * P, HALF)
@@ -152,46 +151,28 @@ def tile_list_ckg_none_kernel(
                 rel[b].append(bank)
 
         def multiply(b):
-            prod[b] = []
-            for c in range(2):
-                both = ring.tile([P, 2, PACK, P], F32, name=f"prod{c}")
-                nc.vector.tensor_tensor(
-                    both[:], ordered(rel[b][c], b).unsqueeze(1).to_broadcast([P, 2, PACK, P]), ent[b][:], MULT)
-                prod[b].append(both)
+            arr, ari = rel[b]
+            with_arr = ring.tile([P, 2, R], F32, name="with_arr")
+            nc.vector.tensor_tensor(with_arr[:], ent[b][:], arr[:].unsqueeze(1).to_broadcast([P, 2, R]), MULT)
+            with_ari = ring.tile([P, 2, R], F32, name="with_ari")
+            nc.vector.scalar_tensor_tensor(with_ari[:, 0, :], ent[b][:, 1, :], -1.0, ari[:], MULT, MULT)
+            nc.vector.tensor_tensor(with_ari[:, 1, :], ent[b][:, 0, :], ari[:], MULT)
+            prod[b] = (with_arr, with_ari)
 
-        def subtract(b):
-            engine = nc.gpsimd
-            if b in SUMMED_ON_TENSOR:
-                diff[b] = ring.tile([P, PACK, P], F32, name="diff")
-                engine.tensor_tensor(diff[b][:], prod[b][0][:, 0], prod[b][1][:, 1], SUBTRACT)
-                return
-            diff[b] = ring.tile([P, 2, PACK, P], BF16, name="pair", align_bytes=64)
-            engine.tensor_tensor(diff[b][:, 0], prod[b][0][:, 0], prod[b][1][:, 1], SUBTRACT)
-            engine.tensor_tensor(diff[b][:, 1], prod[b][0][:, 1], prod[b][1][:, 0], ADD)
+        def combine(b):
+            summed[b] = ring.tile([P, 2, R], BF16, name="summed", align_bytes=64)
+            nc.gpsimd.tensor_tensor(summed[b][:], prod[b][0][:], prod[b][1][:], ADD)
 
         def turn(b):
             turned[b] = ring.tile([P, 2, P, PACK], BF16, name="turned", align_bytes=64)
-            if b not in SUMMED_ON_TENSOR:
-                bank = psum.tile([P, 2, 2, P], F32, name="turn_bank", bufs=2)
-                words = diff[b][:].rearrange("j c t m -> j (c t m)").bitcast(F32).rearrange("j (c p u) -> j c u p", c=2, u=2)
-                for c in range(2):
-                    for u in range(2):
-                        nc.tensor.transpose(bank[:, c, u, :], words[:, c, u, :], identity[:])
-                nc.scalar.copy(
-                    turned[b][:].rearrange("p c j t -> p (c j t)").bitcast(F32).rearrange("p (c j u) -> p c j u", c=2, u=2),
-                    bank[:].rearrange("p c u j -> p c j u"))
-                return
-            hi_bank = psum.tile([P, PACK, P], F32, name="turn_bank", bufs=2)
-            for t in range(PACK):
-                nc.tensor.matmul(hi_bank[:, t, :], prod[b][0][:, 1, t, :], identity[:],
-                                 start=True, stop=False, is_transpose=True)
-                nc.tensor.matmul(hi_bank[:, t, :], prod[b][1][:, 0, t, :], identity[:],
-                                 start=False, stop=True, is_transpose=True)
-            nc.scalar.copy(turned[b][:, 1], hi_bank[:].rearrange("p t j -> p j t"))
-            hr_bank = psum.tile([P, PACK, P], F32, name="turn_bank", bufs=2)
-            for t in range(PACK):
-                nc.tensor.transpose(hr_bank[:, t, :], diff[b][:, t, :], identity[:])
-            nc.scalar.copy(turned[b][:, 0], hr_bank[:].rearrange("p t j -> p j t"))
+            bank = psum.tile([P, 2, 2, P], F32, name="turn_bank", bufs=1)
+            words = summed[b][:].rearrange("j c r -> j (c r)").bitcast(F32).rearrange("j (c p u) -> j c u p", c=2, u=2)
+            for c in range(2):
+                for u in range(2):
+                    nc.tensor.transpose(bank[:, c, u, :], words[:, c, u, :], identity[:])
+            nc.scalar.copy(
+                turned[b][:].rearrange("p c j t -> p (c j t)").bitcast(F32).rearrange("p (c j u) -> p c j u", c=2, u=2),
+                bank[:].rearrange("p c u j -> p c j u"))
 
         def quantise(b):
             codes = ring.tile([P, 2 * P], U32, name="codes", align_bytes=256)
@@ -204,15 +185,15 @@ def tile_list_ckg_none_kernel(
             codes = ring.tile([P, 2 * P], U32, name="codes", align_bytes=256)
             scales = ring.tile([P, 2 * P], U8, name="scales", align_bytes=256)
             arr, ari = rel[LAST]
-            aer, aei = (ent[LAST][:, c].rearrange("j t m -> j (t m)") for c in range(2))
+            aer, aei = ent[LAST][:, 0, :], ent[LAST][:, 1, :]
             for c, (first, second, op) in enumerate(((aer, aei, SUBTRACT), (aei, aer, ADD))):
                 left = ring.tile([P, R], F32, name="left", bufs=2)
-                nc.vector.tensor_tensor(left[:], arr[:], first, MULT)
+                nc.vector.tensor_tensor(left[:], first, arr[:], MULT)
                 right = ring.tile([P, R], F32, name="right", bufs=2)
-                nc.vector.tensor_tensor(right[:], ari[:], second, MULT)
+                nc.vector.tensor_tensor(right[:], second, ari[:], MULT)
                 part = ring.tile([P, R], BF16, name="part", bufs=2, align_bytes=64)
                 nc.vector.tensor_tensor(part[:], left[:], right[:], op)
-                bank = psum.tile([P, 2, P], F32, name="turn_bank", bufs=2)
+                bank = psum.tile([P, 2, P], F32, name="ent_bank", bufs=2)
                 words = part[:].bitcast(F32).rearrange("j (p u) -> j u p", u=2)
                 for u in range(2):
                     nc.tensor.transpose(bank[:, u, :], words[:, u, :], identity[:])
@@ -225,15 +206,15 @@ def tile_list_ckg_none_kernel(
 
         def score(b):
             codes, scales = quant[b]
-            bank = psum.tile([P, 2, P], F32, name="score_bank", bufs=1)
+            bank = psum.tile([P, 2, P], F32, name="score_bank", bufs=2)
             for g in range(2):
                 nc.tensor.matmul_mx(
                     out=bank[:, g, :], lhsT=cand_sb[:, 4 * P * g:4 * P * (g + 1)].bitcast(FP8X4),
-                    lhsT_scale=rel_planes[:, COL_NR + g * P:COL_NR + (g + 1) * P],
+                    lhsT_scale=cand_planes[:, 0, g * P:(g + 1) * P],
                     rhs=codes[:, 0:P].bitcast(FP8X4), rhs_scale=scales[:, 0:P], start=True, stop=False)
                 nc.tensor.matmul_mx(
                     out=bank[:, g, :], lhsT=cand_sb[:, 4 * N + 2 * P * g:4 * N + 2 * P * (g + 1)].bitcast(FP4X4),
-                    lhsT_scale=rel_planes[:, COL_NI + g * P:COL_NI + (g + 1) * P],
+                    lhsT_scale=cand_planes[:, 1, g * P:(g + 1) * P],
                     rhs=codes[:, P:2 * P].bitcast(FP8X4), rhs_scale=scales[:, P:2 * P], start=False, stop=True)
             result = ring.tile([P, 2, P], F32, name="result")
             nc.scalar.copy(result[:], bank[:])
@@ -242,19 +223,19 @@ def tile_list_ckg_none_kernel(
         for b in range(AHEAD):
             project_entity(b)
         project_relation(0)
-        for step in range(BLOCKS + 1):
+        for step in range(BLOCKS):
             if step < LAST:
                 multiply(step)
-                subtract(step)
-            if step + 1 < BLOCKS:
+                combine(step)
                 project_relation(step + 1)
-            if 0 <= step - 1 < LAST:
+            if step >= 1:
                 turn(step - 1)
-            if step == LAST:
-                finish_last()
-            if 0 <= step - 2:
+            if step >= 2:
                 quantise(step - 2)
                 score(step - 2)
             if step + AHEAD < BLOCKS:
                 project_entity(step + AHEAD)
+        finish_last()
+        quantise(LAST - 1)
+        score(LAST - 1)
         score(LAST)

@@ -20,12 +20,16 @@ ADD = mybir.AluOpType.add
 
 P = 128
 PACK = 4
+QUADRANT = 32
 BLOCKS = J // P
 HALF = J // 2
+HALF_COLS = HALF // 16
 AHEAD = 2
+LAST = BLOCKS - 1
+ON_TENSOR = LAST - 1
 COL_WER, COL_WEI, COLS_ENT = J, J + 2 * R, J + 4 * R
 COL_WRR, COL_WRI, COLS_REL = J, J + R, J + 2 * R
-LAST = BLOCKS - 1
+COL_NI = PACK * N
 
 
 def tile_list_ckg_none_kernel(
@@ -50,8 +54,8 @@ def tile_list_ckg_none_kernel(
         rel_rows = keep.tile([P, COLS_REL], U8, name="rel_rows", align_bytes=256)
         identity = keep.tile([P, P], F32, name="identity", align_bytes=64)
 
-        def words_view(ap):
-            return ap.rearrange("a p n i -> p (a n i)").bitcast(I32)
+        def words_view(words):
+            return words.rearrange("a p n i -> p (a n i)").bitcast(I32)
 
         def load_scale_rows(queue, rows, scales):
             queue.dma_start(rows.bitcast(I32).rearrange("q (a n) -> q a n", a=scales.shape[0]),
@@ -63,9 +67,9 @@ def tile_list_ckg_none_kernel(
         nc.vector.memset(zeros[:], 0)
         nc.vector.tensor_copy(ent_plane1[:].bitcast(I32), zeros[:])
         nc.vector.memset(tab_rows[64:P, :].bitcast(I32), 0)
+
         load_scale_rows(nc.gpsimd, rel_rows[0:P:8, COL_WRR:COL_WRI], wrr_scales)
         load_scale_rows(nc.gpsimd, rel_rows[0:P:8, COL_WRI:COLS_REL], wri_scales)
-
         nc.sync.dma_start(list1[:], offs)
         nc.sync.dma_start(tab_rows[0:32, :].bitcast(I32), tab_scales.rearrange("a q t -> (a q) t").bitcast(I32))
         nc.sync.dma_start(list2[:], offs2)
@@ -80,64 +84,78 @@ def tile_list_ckg_none_kernel(
         got_rows = keep.tile([P, J], U8, name="got_rows", align_bytes=256)
         nc.vector.tensor_copy(got_rows[:], tab_rows[:].indirect(list1[:]))
         nc.vector.tensor_copy(ent_planes[:, 0:J].bitcast(I32), got_rows[:].bitcast(I32))
-        for quadrant in range(4):
-            queue = nc.gpsimd if quadrant == 0 else nc.sync
-            queue.dma_start(ent_plane1[32 * quadrant:32 * quadrant + 4, :].bitcast(I32),
-                            got_rows[16 + 4 * quadrant:20 + 4 * quadrant, :].bitcast(I32))
-        for quadrant in range(1, 4):
-            nc.sync.dma_start(ent_planes[32 * quadrant:32 * quadrant + 4, :].bitcast(I32),
-                              ent_planes[4 * quadrant:4 * quadrant + 4, :].bitcast(I32))
+        for quad in range(4):
+            queue = nc.gpsimd if quad == 0 else nc.sync
+            queue.dma_start(ent_plane1[QUADRANT * quad:QUADRANT * quad + 4, :].bitcast(I32),
+                            got_rows[16 + 4 * quad:20 + 4 * quad, :].bitcast(I32))
+        for quad in range(1, 4):
+            nc.sync.dma_start(ent_planes[QUADRANT * quad:QUADRANT * quad + 4, :].bitcast(I32),
+                              ent_planes[4 * quad:4 * quad + 4, :].bitcast(I32))
         make_identity(nc, identity[:])
+
         for h in range(2):
             got2_rows = keep.tile([P, HALF], U8, name=f"got2_rows{h}", tag=f"gathered{h}", align_bytes=256)
-            nc.vector.tensor_copy(got2_rows[:], tab2_rows[:].indirect(list2[:, 32 * h:32 * h + 32]))
+            nc.vector.tensor_copy(got2_rows[:], tab2_rows[:].indirect(list2[:, HALF_COLS * h:HALF_COLS * (h + 1)]))
             nc.vector.tensor_copy(
                 rel_rows[:, h * HALF:(h + 1) * HALF].bitcast(I32), got2_rows[:].bitcast(I32))
         tab2_sb = keep.tile([P, T], I32, name="tab2_sb", tag="gathered0", align_bytes=256)
         nc.sync.dma_start(tab2_sb[:], words_view(tab2_words))
         rel_planes = keep.tile([P, COLS_REL], U8, name="rel_planes", tag="first", align_bytes=256)
         nc.vector.memset(rel_planes[:].bitcast(I32), 0)
-        for base in range(0, P, 32):
-            nc.sync.dma_start(rel_planes[base:base + 4, :].bitcast(I32), rel_rows[base:base + 32:8, :].bitcast(I32))
+        for base in range(0, P, QUADRANT):
+            nc.sync.dma_start(rel_planes[base:base + 4, :].bitcast(I32),
+                              rel_rows[base:base + QUADRANT:8, :].bitcast(I32))
 
         ent_words, rel_words = [], []
         for h in range(2):
             pairs = keep.tile([P, HALF], U32, name=f"pairs{h}", tag="second", align_bytes=256)
-            nc.vector.tensor_copy(pairs[:], tab_sb[:].bitcast(U32).indirect(list1[:, 32 * h:32 * h + 32]))
+            nc.vector.tensor_copy(
+                pairs[:], tab_sb[:].bitcast(U32).indirect(list1[:, HALF_COLS * h:HALF_COLS * (h + 1)]))
             parted = keep.tile([P, 2, HALF], U16, name=f"parted{h}", align_bytes=256)
             nc.vector.tensor_copy(parted[:], pairs[:].bitcast(U16).rearrange("p (j d) -> p d j", d=2))
             ent_words.append(parted)
         wr_sb = keep.tile([P, 2, R], I32, name="wr_sb", tag="gathered1", align_bytes=256)
         nc.sync.dma_start(wr_sb[:, 0, :], words_view(wrr_words))
         nc.sync.dma_start(wr_sb[:, 1, :], words_view(wri_words))
-        cand_sb = keep.tile([P, 6 * N], U8, name="cand_sb", tag="second", align_bytes=256)
-        nc.sync.dma_start(cand_sb[:, 0:4 * N].bitcast(I32), words_view(nr_words))
-        nc.sync.dma_start(cand_sb[:, 4 * N:6 * N].bitcast(I32), ni_words[0].bitcast(I32))
+
+        cand_sb = keep.tile([P, COL_NI + 2 * N], U8, name="cand_sb", tag="second", align_bytes=256)
+        nc.sync.dma_start(cand_sb[:, 0:COL_NI].bitcast(I32), words_view(nr_words))
+        nc.sync.dma_start(cand_sb[:, COL_NI:COL_NI + 2 * N].bitcast(I32), ni_words[0].bitcast(I32))
         cand_planes = keep.tile([P, 2, N], U8, name="cand_planes", tag="table", align_bytes=64)
         nc.vector.memset(cand_planes[:].bitcast(I32), 0)
-        for c, scales in enumerate((nr_scales, ni_scales)):
-            for quadrant in range(4):
-                nc.sync.dma_start(cand_planes[32 * quadrant:32 * quadrant + 4, c, :].bitcast(I32),
-                                  scales[0, 4 * quadrant:4 * quadrant + 4, :].bitcast(I32))
+        for c, cand_scales in enumerate((nr_scales, ni_scales)):
+            for quad in range(4):
+                nc.sync.dma_start(cand_planes[QUADRANT * quad:QUADRANT * quad + 4, c, :].bitcast(I32),
+                                  cand_scales[0, 4 * quad:4 * quad + 4, :].bitcast(I32))
         for h in range(2):
             picked = keep.tile([P, HALF], U32, name=f"picked{h}", align_bytes=256)
-            nc.vector.tensor_copy(picked[:], tab2_sb[:].bitcast(U32).indirect(list2[:, 32 * h:32 * h + 32]))
+            nc.vector.tensor_copy(
+                picked[:], tab2_sb[:].bitcast(U32).indirect(list2[:, HALF_COLS * h:HALF_COLS * (h + 1)]))
             rel_words.append(picked)
+
+        def ent_bank(shape):
+            return psum.tile(shape, F32, name="ent_bank", bufs=2)
+
+        def turn_bank(shape):
+            return psum.tile(shape, F32, name="turn_bank", bufs=1)
+
+        def by_place(bank, b):
+            return bank[:].rearrange("j (m t) -> j t m" if b == ON_TENSOR else "j (t m) -> j t m", t=PACK)
 
         ent, rel, prod, summed, turned, quant = {}, {}, {}, {}, {}, {}
 
         def project_entity(b):
             h, j0 = divmod(b * P, HALF)
-            ent[b] = ring.tile([P, 2, R], F32, name="ent", bufs=2)
+            ent[b] = ring.tile([P, 2, PACK, P], F32, name="ent", bufs=AHEAD)
             for c, (w_sb, col) in enumerate(((wer_sb, COL_WER), (wei_sb, COL_WEI))):
-                bank = psum.tile([P, R], F32, name="ent_bank", bufs=2)
+                bank = ent_bank([P, R])
                 for a in range(2):
                     plane = (ent_planes, ent_plane1)[a][:, b * P:(b + 1) * P]
                     nc.tensor.matmul_mx(
                         out=bank[:], lhsT=ent_words[h][:, a, j0:j0 + P].bitcast(FP4X4), lhsT_scale=plane,
                         rhs=w_sb[:, a, :].bitcast(FP4X4), rhs_scale=ent_planes[:, col + a * R:col + (a + 1) * R],
                         start=(a == 0), stop=(a == 1))
-                nc.scalar.copy(ent[b][:, c, :], bank[:])
+                nc.scalar.copy(ent[b][:, c], by_place(bank, b))
 
         def project_relation(b):
             h, j0 = divmod(b * P, HALF)
@@ -148,25 +166,34 @@ def tile_list_ckg_none_kernel(
                     out=bank[:], lhsT=rel_words[h][:, j0:j0 + P].bitcast(FP8X4),
                     lhsT_scale=rel_planes[:, b * P:(b + 1) * P],
                     rhs=wr_sb[:, c, :].bitcast(FP8X4), rhs_scale=rel_planes[:, col:col + R], start=True, stop=True)
-                rel[b].append(bank)
+                rel[b].append(by_place(bank, b))
 
         def multiply(b):
             arr, ari = rel[b]
-            with_arr = ring.tile([P, 2, R], F32, name="with_arr")
-            nc.vector.tensor_tensor(with_arr[:], ent[b][:], arr[:].unsqueeze(1).to_broadcast([P, 2, R]), MULT)
-            with_ari = ring.tile([P, 2, R], F32, name="with_ari")
-            nc.vector.scalar_tensor_tensor(with_ari[:, 0, :], ent[b][:, 1, :], -1.0, ari[:], MULT, MULT)
-            nc.vector.tensor_tensor(with_ari[:, 1, :], ent[b][:, 0, :], ari[:], MULT)
+            with_arr = ring.tile([P, 2, PACK, P], F32, name="with_arr")
+            nc.vector.tensor_tensor(with_arr[:], ent[b][:], arr.unsqueeze(1).to_broadcast([P, 2, PACK, P]), MULT)
+            with_ari = ring.tile([P, 2, PACK, P], F32, name="with_ari")
+            nc.vector.scalar_tensor_tensor(with_ari[:, 0], ent[b][:, 1], -1.0, ari, MULT, MULT)
+            nc.vector.tensor_tensor(with_ari[:, 1], ent[b][:, 0], ari, MULT)
             prod[b] = (with_arr, with_ari)
 
         def combine(b):
-            summed[b] = ring.tile([P, 2, R], BF16, name="summed", align_bytes=64)
+            summed[b] = ring.tile([P, 2, PACK, P], BF16, name="summed", align_bytes=64)
             nc.gpsimd.tensor_tensor(summed[b][:], prod[b][0][:], prod[b][1][:], ADD)
 
         def turn(b):
             turned[b] = ring.tile([P, 2, P, PACK], BF16, name="turned", align_bytes=64)
-            bank = psum.tile([P, 2, 2, P], F32, name="turn_bank", bufs=1)
-            words = summed[b][:].rearrange("j c r -> j (c r)").bitcast(F32).rearrange("j (c p u) -> j c u p", c=2, u=2)
+            if b == ON_TENSOR:
+                for c, bank in enumerate((turn_bank([P, PACK, P]), ent_bank([P, PACK, P]))):
+                    for t in range(PACK):
+                        for term in range(2):
+                            nc.tensor.matmul(bank[:, t, :], prod[b][term][:, c, t, :], identity[:],
+                                             start=(term == 0), stop=(term == 1), is_transpose=True)
+                    nc.scalar.copy(turned[b][:, c], bank[:].rearrange("p t j -> p j t"))
+                return
+            bank = turn_bank([P, 2, 2, P])
+            words = summed[b][:].rearrange("j c t m -> j (c t m)").bitcast(F32).rearrange(
+                "j (c p u) -> j c u p", c=2, u=2)
             for c in range(2):
                 for u in range(2):
                     nc.tensor.transpose(bank[:, c, u, :], words[:, c, u, :], identity[:])
@@ -174,48 +201,51 @@ def tile_list_ckg_none_kernel(
                 turned[b][:].rearrange("p c j t -> p (c j t)").bitcast(F32).rearrange("p (c j u) -> p c j u", c=2, u=2),
                 bank[:].rearrange("p c u j -> p c j u"))
 
-        def quantise(b):
+        def quantised_tiles(b):
             codes = ring.tile([P, 2 * P], U32, name="codes", align_bytes=256)
-            scales = ring.tile([P, 2 * P], U8, name="scales", align_bytes=256)
-            nc.vector.quantize_mx(out=codes[:].bitcast(FP8X4), scales=scales[:],
+            plane = ring.tile([P, 2 * P], U8, name="plane", align_bytes=256)
+            quant[b] = (codes, plane)
+            return codes, plane
+
+        def quantise(b):
+            codes, plane = quantised_tiles(b)
+            nc.vector.quantize_mx(out=codes[:].bitcast(FP8X4), scales=plane[:],
                                   in_=turned[b][:].rearrange("p c j t -> p (c j t)"))
-            quant[b] = (codes, scales)
 
         def finish_last():
-            codes = ring.tile([P, 2 * P], U32, name="codes", align_bytes=256)
-            scales = ring.tile([P, 2 * P], U8, name="scales", align_bytes=256)
+            codes, plane = quantised_tiles(LAST)
             arr, ari = rel[LAST]
-            aer, aei = ent[LAST][:, 0, :], ent[LAST][:, 1, :]
-            for c, (first, second, op) in enumerate(((aer, aei, SUBTRACT), (aei, aer, ADD))):
-                left = ring.tile([P, R], F32, name="left", bufs=2)
-                nc.vector.tensor_tensor(left[:], first, arr[:], MULT)
-                right = ring.tile([P, R], F32, name="right", bufs=2)
-                nc.vector.tensor_tensor(right[:], second, ari[:], MULT)
-                part = ring.tile([P, R], BF16, name="part", bufs=2, align_bytes=64)
+            aer, aei = ent[LAST][:, 0], ent[LAST][:, 1]
+            for c, (first, second, op, new_bank) in enumerate(
+                    ((aer, aei, SUBTRACT, ent_bank), (aei, aer, ADD, turn_bank))):
+                left = ring.tile([P, PACK, P], F32, name="left", bufs=2)
+                nc.vector.tensor_tensor(left[:], first, arr, MULT)
+                right = ring.tile([P, PACK, P], F32, name="right", bufs=2)
+                nc.vector.tensor_tensor(right[:], second, ari, MULT)
+                part = ring.tile([P, PACK, P], BF16, name="part", bufs=2, align_bytes=64)
                 nc.vector.tensor_tensor(part[:], left[:], right[:], op)
-                bank = psum.tile([P, 2, P], F32, name="ent_bank", bufs=2)
-                words = part[:].bitcast(F32).rearrange("j (p u) -> j u p", u=2)
+                bank = new_bank([P, 2, P])
+                words = part[:].rearrange("j t m -> j (t m)").bitcast(F32).rearrange("j (p u) -> j u p", u=2)
                 for u in range(2):
                     nc.tensor.transpose(bank[:, u, :], words[:, u, :], identity[:])
                 part_turned = ring.tile([P, P * PACK], BF16, name="part_turned", bufs=2, align_bytes=64)
                 nc.scalar.copy(part_turned[:].bitcast(F32).rearrange("p (j u) -> p j u", u=2),
                                bank[:].rearrange("p u j -> p j u"))
                 nc.vector.quantize_mx(out=codes[:, c * P:(c + 1) * P].bitcast(FP8X4),
-                                      scales=scales[:, c * P:(c + 1) * P], in_=part_turned[:])
-            quant[LAST] = (codes, scales)
+                                      scales=plane[:, c * P:(c + 1) * P], in_=part_turned[:])
 
         def score(b):
-            codes, scales = quant[b]
+            codes, plane = quant[b]
             bank = psum.tile([P, 2, P], F32, name="score_bank", bufs=2)
             for g in range(2):
                 nc.tensor.matmul_mx(
-                    out=bank[:, g, :], lhsT=cand_sb[:, 4 * P * g:4 * P * (g + 1)].bitcast(FP8X4),
+                    out=bank[:, g, :], lhsT=cand_sb[:, PACK * P * g:PACK * P * (g + 1)].bitcast(FP8X4),
                     lhsT_scale=cand_planes[:, 0, g * P:(g + 1) * P],
-                    rhs=codes[:, 0:P].bitcast(FP8X4), rhs_scale=scales[:, 0:P], start=True, stop=False)
+                    rhs=codes[:, 0:P].bitcast(FP8X4), rhs_scale=plane[:, 0:P], start=True, stop=False)
                 nc.tensor.matmul_mx(
-                    out=bank[:, g, :], lhsT=cand_sb[:, 4 * N + 2 * P * g:4 * N + 2 * P * (g + 1)].bitcast(FP4X4),
+                    out=bank[:, g, :], lhsT=cand_sb[:, COL_NI + 2 * P * g:COL_NI + 2 * P * (g + 1)].bitcast(FP4X4),
                     lhsT_scale=cand_planes[:, 1, g * P:(g + 1) * P],
-                    rhs=codes[:, P:2 * P].bitcast(FP8X4), rhs_scale=scales[:, P:2 * P], start=False, stop=True)
+                    rhs=codes[:, P:2 * P].bitcast(FP8X4), rhs_scale=plane[:, P:2 * P], start=False, stop=True)
             result = ring.tile([P, 2, P], F32, name="result")
             nc.scalar.copy(result[:], bank[:])
             nc.sync.dma_start(out[:, b * P:(b + 1) * P].rearrange("(g n) j -> n g j", g=2), result[:])
@@ -226,7 +256,8 @@ def tile_list_ckg_none_kernel(
         for step in range(BLOCKS):
             if step < LAST:
                 multiply(step)
-                combine(step)
+                if step != ON_TENSOR:
+                    combine(step)
                 project_relation(step + 1)
             if step >= 1:
                 turn(step - 1)

@@ -15,7 +15,6 @@ U8 = mybir.dt.uint8
 FP8X4 = mybir.dt.float8_e4m3fn_x4
 FP4X4 = mybir.dt.float4_e2m1fn_x4
 MULT = mybir.AluOpType.mult
-SUBTRACT = mybir.AluOpType.subtract
 ADD = mybir.AluOpType.add
 
 P = 128
@@ -25,6 +24,7 @@ BLOCKS = J // P
 HALF = J // 2
 HALF_COLS = HALF // 16
 AHEAD = 2
+LAG = 2
 LAST = BLOCKS - 1
 ON_TENSOR = LAST - 1
 COL_WER, COL_WEI, COLS_ENT = J, J + 2 * R, J + 4 * R
@@ -139,14 +139,24 @@ def tile_list_ckg_none_kernel(
         def turn_bank(shape):
             return psum.tile(shape, F32, name="turn_bank", bufs=1)
 
-        def by_place(bank, b):
-            return bank[:].rearrange("j (m t) -> j t m" if b == ON_TENSOR else "j (t m) -> j t m", t=PACK)
+        def rel_bank(shape):
+            return psum.tile(shape, F32, name="rel_bank", bufs=4)
+
+        def by_place(view, b):
+            if b >= ON_TENSOR:
+                return view.rearrange("j (m t) -> j t m", t=PACK)
+            return view.rearrange("j (m u e) -> j u m e", u=2, e=2)
+
+        def as_placed(view, b):
+            if b >= ON_TENSOR:
+                return view.rearrange("j (t m) -> j t m", t=PACK)
+            return view.rearrange("j (u m e) -> j u m e", u=2, e=2)
 
         ent, rel, prod, summed, turned, quant = {}, {}, {}, {}, {}, {}
 
         def project_entity(b):
             h, j0 = divmod(b * P, HALF)
-            ent[b] = ring.tile([P, 2, PACK, P], F32, name="ent", bufs=AHEAD)
+            ent[b] = ring.tile([P, 2, R], F32, name="ent", bufs=AHEAD)
             for c, (w_sb, col) in enumerate(((wer_sb, COL_WER), (wei_sb, COL_WEI))):
                 bank = ent_bank([P, R])
                 for a in range(2):
@@ -155,45 +165,52 @@ def tile_list_ckg_none_kernel(
                         out=bank[:], lhsT=ent_words[h][:, a, j0:j0 + P].bitcast(FP4X4), lhsT_scale=plane,
                         rhs=w_sb[:, a, :].bitcast(FP4X4), rhs_scale=ent_planes[:, col + a * R:col + (a + 1) * R],
                         start=(a == 0), stop=(a == 1))
-                nc.scalar.copy(ent[b][:, c], by_place(bank, b))
+                nc.scalar.copy(as_placed(ent[b][:, c], b), by_place(bank[:], b))
 
         def project_relation(b):
             h, j0 = divmod(b * P, HALF)
             rel[b] = []
             for c, col in enumerate((COL_WRR, COL_WRI)):
-                bank = psum.tile([P, R], F32, name="rel_bank", bufs=3)
+                bank = rel_bank([P, R])
                 nc.tensor.matmul_mx(
                     out=bank[:], lhsT=rel_words[h][:, j0:j0 + P].bitcast(FP8X4),
                     lhsT_scale=rel_planes[:, b * P:(b + 1) * P],
                     rhs=wr_sb[:, c, :].bitcast(FP8X4), rhs_scale=rel_planes[:, col:col + R], start=True, stop=True)
-                rel[b].append(by_place(bank, b))
+                rel[b].append(by_place(bank[:], b))
 
         def multiply(b):
             arr, ari = rel[b]
-            with_arr = ring.tile([P, 2, PACK, P], F32, name="with_arr")
-            nc.vector.tensor_tensor(with_arr[:], ent[b][:], arr.unsqueeze(1).to_broadcast([P, 2, PACK, P]), MULT)
-            with_ari = ring.tile([P, 2, PACK, P], F32, name="with_ari")
-            nc.vector.scalar_tensor_tensor(with_ari[:, 0], ent[b][:, 1], -1.0, ari, MULT, MULT)
-            nc.vector.tensor_tensor(with_ari[:, 1], ent[b][:, 0], ari, MULT)
+            aer, aei = as_placed(ent[b][:, 0], b), as_placed(ent[b][:, 1], b)
+            with_arr = ring.tile([P, 2, R], F32, name="with_arr")
+            with_ari = ring.tile([P, 2, R], F32, name="with_ari")
+            nc.vector.tensor_tensor(as_placed(with_arr[:, 0], b), aer, arr, MULT)
+            nc.vector.tensor_tensor(as_placed(with_arr[:, 1], b), aei, arr, MULT)
+            negated = as_placed(with_ari[:, 0], b)
+            if b >= ON_TENSOR:
+                nc.vector.scalar_tensor_tensor(negated, aei, -1.0, ari, MULT, MULT)
+            else:
+                for u in range(2):
+                    nc.vector.scalar_tensor_tensor(negated[:, u], aei[:, u], -1.0, ari[:, u], MULT, MULT)
+            nc.vector.tensor_tensor(as_placed(with_ari[:, 1], b), aer, ari, MULT)
             prod[b] = (with_arr, with_ari)
 
         def combine(b):
-            summed[b] = ring.tile([P, 2, PACK, P], BF16, name="summed", align_bytes=64)
+            summed[b] = ring.tile([P, 2, R], BF16, name="summed", align_bytes=64)
             nc.gpsimd.tensor_tensor(summed[b][:], prod[b][0][:], prod[b][1][:], ADD)
 
         def turn(b):
             turned[b] = ring.tile([P, 2, P, PACK], BF16, name="turned", align_bytes=64)
             if b == ON_TENSOR:
-                for c, bank in enumerate((turn_bank([P, PACK, P]), ent_bank([P, PACK, P]))):
+                for c, bank in enumerate((ent_bank([P, PACK, P]), ent_bank([P, PACK, P]))):
                     for t in range(PACK):
                         for term in range(2):
-                            nc.tensor.matmul(bank[:, t, :], prod[b][term][:, c, t, :], identity[:],
+                            nc.tensor.matmul(bank[:, t, :], prod[b][term][:, c, t * P:(t + 1) * P], identity[:],
                                              start=(term == 0), stop=(term == 1), is_transpose=True)
                     nc.scalar.copy(turned[b][:, c], bank[:].rearrange("p t j -> p j t"))
                 return
             bank = turn_bank([P, 2, 2, P])
-            words = summed[b][:].rearrange("j c t m -> j (c t m)").bitcast(F32).rearrange(
-                "j (c p u) -> j c u p", c=2, u=2)
+            words = summed[b][:].rearrange("j c r -> j (c r)").bitcast(F32).rearrange(
+                "j (c u p) -> j c u p", c=2, u=2)
             for c in range(2):
                 for u in range(2):
                     nc.tensor.transpose(bank[:, c, u, :], words[:, c, u, :], identity[:])
@@ -215,28 +232,29 @@ def tile_list_ckg_none_kernel(
         def finish_last():
             codes, plane = quantised_tiles(LAST)
             arr, ari = rel[LAST]
-            aer, aei = ent[LAST][:, 0], ent[LAST][:, 1]
-            for c, (first, second, op, new_bank) in enumerate(
-                    ((aer, aei, SUBTRACT, ent_bank), (aei, aer, ADD, turn_bank))):
+            aer, aei = as_placed(ent[LAST][:, 0], LAST), as_placed(ent[LAST][:, 1], LAST)
+            for c, bank in enumerate((turn_bank([P, PACK, P]), rel_bank([P, PACK, P]))):
                 left = ring.tile([P, PACK, P], F32, name="left", bufs=2)
-                nc.vector.tensor_tensor(left[:], first, arr, MULT)
                 right = ring.tile([P, PACK, P], F32, name="right", bufs=2)
-                nc.vector.tensor_tensor(right[:], second, ari, MULT)
-                part = ring.tile([P, PACK, P], BF16, name="part", bufs=2, align_bytes=64)
-                nc.vector.tensor_tensor(part[:], left[:], right[:], op)
-                bank = new_bank([P, 2, P])
-                words = part[:].rearrange("j t m -> j (t m)").bitcast(F32).rearrange("j (p u) -> j u p", u=2)
-                for u in range(2):
-                    nc.tensor.transpose(bank[:, u, :], words[:, u, :], identity[:])
-                part_turned = ring.tile([P, P * PACK], BF16, name="part_turned", bufs=2, align_bytes=64)
-                nc.scalar.copy(part_turned[:].bitcast(F32).rearrange("p (j u) -> p j u", u=2),
-                               bank[:].rearrange("p u j -> p j u"))
+                if c == 0:
+                    nc.vector.tensor_tensor(left[:], aer, arr, MULT)
+                    nc.vector.scalar_tensor_tensor(right[:], aei, -1.0, ari, MULT, MULT)
+                else:
+                    nc.vector.tensor_tensor(left[:], aei, arr, MULT)
+                    nc.vector.tensor_tensor(right[:], aer, ari, MULT)
+                for term, tile in enumerate((left, right)):
+                    for t in range(PACK):
+                        nc.tensor.matmul(bank[:, t, :], tile[:, t, :], identity[:], start=(term == 0 and t == 0),
+                                         stop=(term == 1 and t == PACK - 1), is_transpose=True)
+                part_turned = ring.tile([P, P, PACK], BF16, name="part_turned", bufs=2, align_bytes=64)
+                nc.scalar.copy(part_turned[:], bank[:].rearrange("p t j -> p j t"))
                 nc.vector.quantize_mx(out=codes[:, c * P:(c + 1) * P].bitcast(FP8X4),
-                                      scales=plane[:, c * P:(c + 1) * P], in_=part_turned[:])
+                                      scales=plane[:, c * P:(c + 1) * P],
+                                      in_=part_turned[:].rearrange("p j t -> p (j t)"))
 
         def score(b):
             codes, plane = quant[b]
-            bank = psum.tile([P, 2, P], F32, name="score_bank", bufs=2)
+            bank = rel_bank([P, 2, P]) if b >= ON_TENSOR else psum.tile([P, 2, P], F32, name="score_bank", bufs=1)
             for g in range(2):
                 nc.tensor.matmul_mx(
                     out=bank[:, g, :], lhsT=cand_sb[:, PACK * P * g:PACK * P * (g + 1)].bitcast(FP8X4),
@@ -253,20 +271,25 @@ def tile_list_ckg_none_kernel(
         for b in range(AHEAD):
             project_entity(b)
         project_relation(0)
-        for step in range(BLOCKS):
-            if step < LAST:
-                multiply(step)
-                if step != ON_TENSOR:
-                    combine(step)
-                project_relation(step + 1)
-            if step >= 1:
-                turn(step - 1)
-            if step >= 2:
-                quantise(step - 2)
-                score(step - 2)
+        project_relation(1)
+        for step in range(LAST):
+            multiply(step)
+            if step >= LAG:
+                quantise(step - LAG)
+            if step != ON_TENSOR:
+                combine(step)
             if step + AHEAD < BLOCKS:
                 project_entity(step + AHEAD)
+                project_relation(step + AHEAD)
+            if step >= 1:
+                turn(step - 1)
+            if step >= LAG:
+                score(step - LAG)
+        quantise(LAST - LAG)
+        turn(LAST - 1)
+        score(LAST - LAG)
         finish_last()
-        quantise(LAST - 1)
-        score(LAST - 1)
+        for b in range(BLOCKS - LAG, LAST):
+            quantise(b)
+            score(b)
         score(LAST)

@@ -24,7 +24,7 @@ BLOCKS = J // P
 HALF = J // 2
 HALF_COLS = HALF // 16
 AHEAD = 2
-LAG = 2
+LAG = 3
 LAST = BLOCKS - 1
 ON_TENSOR = LAST - 1
 COL_WER, COL_WEI, COLS_ENT = J, J + 2 * R, J + 4 * R

@@ -24,9 +24,9 @@ BLOCKS = J // P
 HALF = J // 2
 HALF_COLS = HALF // 16
 AHEAD = 2
-LAG = 3
 LAST = BLOCKS - 1
-ON_TENSOR = LAST - 1
+MIDDLE = BLOCKS // 2 - 1
+ON_TENSOR = (MIDDLE, LAST)
 COL_WER, COL_WEI, COLS_ENT = J, J + 2 * R, J + 4 * R
 COL_WRR, COL_WRI, COLS_REL = J, J + R, J + 2 * R
 COL_NI = PACK * N
@@ -139,16 +139,19 @@ def tile_list_ckg_none_kernel(
         def turn_bank(shape):
             return psum.tile(shape, F32, name="turn_bank", bufs=1)
 
+        def score_bank(shape):
+            return psum.tile(shape, F32, name="score_bank", bufs=1)
+
         def rel_bank(shape):
             return psum.tile(shape, F32, name="rel_bank", bufs=4)
 
         def by_place(view, b):
-            if b >= ON_TENSOR:
+            if b in ON_TENSOR:
                 return view.rearrange("j (m t) -> j t m", t=PACK)
             return view.rearrange("j (m u e) -> j u m e", u=2, e=2)
 
         def as_placed(view, b):
-            if b >= ON_TENSOR:
+            if b in ON_TENSOR:
                 return view.rearrange("j (t m) -> j t m", t=PACK)
             return view.rearrange("j (u m e) -> j u m e", u=2, e=2)
 
@@ -182,11 +185,14 @@ def tile_list_ckg_none_kernel(
             arr, ari = rel[b]
             aer, aei = as_placed(ent[b][:, 0], b), as_placed(ent[b][:, 1], b)
             with_arr = ring.tile([P, 2, R], F32, name="with_arr")
-            with_ari = ring.tile([P, 2, R], F32, name="with_ari")
+            if b + 1 in ON_TENSOR:
+                with_ari = keep.tile([P, 2, R], F32, name="with_ari", tag=f"pause{b + 1}", align_bytes=256)
+            else:
+                with_ari = ring.tile([P, 2, R], F32, name="with_ari")
             nc.vector.tensor_tensor(as_placed(with_arr[:, 0], b), aer, arr, MULT)
             nc.vector.tensor_tensor(as_placed(with_arr[:, 1], b), aei, arr, MULT)
             negated = as_placed(with_ari[:, 0], b)
-            if b >= ON_TENSOR:
+            if b in ON_TENSOR:
                 nc.vector.scalar_tensor_tensor(negated, aei, -1.0, ari, MULT, MULT)
             else:
                 for u in range(2):
@@ -195,13 +201,16 @@ def tile_list_ckg_none_kernel(
             prod[b] = (with_arr, with_ari)
 
         def combine(b):
-            summed[b] = ring.tile([P, 2, R], BF16, name="summed", align_bytes=64)
+            if b == MIDDLE + 1:
+                summed[b] = keep.tile([P, 2, R], BF16, name="summed", tag=f"turned{MIDDLE - 1}", align_bytes=64)
+            else:
+                summed[b] = ring.tile([P, 2, R], BF16, name="summed", align_bytes=64)
             nc.gpsimd.tensor_tensor(summed[b][:], prod[b][0][:], prod[b][1][:], ADD)
 
         def turn(b):
-            turned[b] = ring.tile([P, 2, P, PACK], BF16, name="turned", align_bytes=64)
-            if b == ON_TENSOR:
-                for c, bank in enumerate((ent_bank([P, PACK, P]), ent_bank([P, PACK, P]))):
+            turned[b] = keep.tile([P, 2, P, PACK], BF16, name="turned", tag=f"turned{b}", align_bytes=64)
+            if b == MIDDLE:
+                for c, bank in enumerate((turn_bank([P, PACK, P]), score_bank([P, PACK, P]))):
                     for t in range(PACK):
                         for term in range(2):
                             nc.tensor.matmul(bank[:, t, :], prod[b][term][:, c, t * P:(t + 1) * P], identity[:],
@@ -218,22 +227,23 @@ def tile_list_ckg_none_kernel(
                 turned[b][:].rearrange("p c j t -> p (c j t)").bitcast(F32).rearrange("p (c j u) -> p c j u", c=2, u=2),
                 bank[:].rearrange("p c u j -> p c j u"))
 
-        def quantised_tiles(b):
-            codes = ring.tile([P, 2 * P], U32, name="codes", align_bytes=256)
-            plane = ring.tile([P, 2 * P], U8, name="plane", align_bytes=256)
-            quant[b] = (codes, plane)
-            return codes, plane
-
-        def quantise(b):
-            codes, plane = quantised_tiles(b)
-            nc.vector.quantize_mx(out=codes[:].bitcast(FP8X4), scales=plane[:],
-                                  in_=turned[b][:].rearrange("p c j t -> p (c j t)"))
+        def quantise(blocks, pause):
+            codes = keep.tile([P, len(blocks), 2 * P], U32, name="codes", tag=f"pause{pause}", align_bytes=256)
+            planes = keep.tile([P, len(blocks), 2 * P], U8, name=f"planes{pause}", align_bytes=256)
+            for i, b in enumerate(blocks):
+                if b not in turned:
+                    turn(b)
+                quant[b] = (codes[:, i, :], planes[:, i, :])
+                nc.vector.quantize_mx(out=codes[:, i, :].bitcast(FP8X4), scales=planes[:, i, :],
+                                      in_=turned[b][:].rearrange("p c j t -> p (c j t)"))
 
         def finish_last():
-            codes, plane = quantised_tiles(LAST)
+            codes = keep.tile([P, 2 * P], U32, name="last_codes", align_bytes=256)
+            plane = keep.tile([P, 2 * P], U8, name="last_plane", align_bytes=256)
+            quant[LAST] = (codes, plane)
             arr, ari = rel[LAST]
             aer, aei = as_placed(ent[LAST][:, 0], LAST), as_placed(ent[LAST][:, 1], LAST)
-            for c, bank in enumerate((turn_bank([P, PACK, P]), rel_bank([P, PACK, P]))):
+            for c, bank in enumerate((ent_bank([P, PACK, P]), ent_bank([P, PACK, P]))):
                 left = ring.tile([P, PACK, P], F32, name="left", bufs=2)
                 right = ring.tile([P, PACK, P], F32, name="right", bufs=2)
                 if c == 0:
@@ -254,7 +264,7 @@ def tile_list_ckg_none_kernel(
 
         def score(b):
             codes, plane = quant[b]
-            bank = rel_bank([P, 2, P]) if b >= ON_TENSOR else psum.tile([P, 2, P], F32, name="score_bank", bufs=1)
+            bank = (rel_bank if b > MIDDLE else score_bank)([P, 2, P])
             for g in range(2):
                 nc.tensor.matmul_mx(
                     out=bank[:, g, :], lhsT=cand_sb[:, PACK * P * g:PACK * P * (g + 1)].bitcast(FP8X4),
@@ -264,32 +274,30 @@ def tile_list_ckg_none_kernel(
                     out=bank[:, g, :], lhsT=cand_sb[:, COL_NI + 2 * P * g:COL_NI + 2 * P * (g + 1)].bitcast(FP4X4),
                     lhsT_scale=cand_planes[:, 1, g * P:(g + 1) * P],
                     rhs=codes[:, P:2 * P].bitcast(FP8X4), rhs_scale=plane[:, P:2 * P], start=False, stop=True)
-            result = ring.tile([P, 2, P], F32, name="result")
-            nc.scalar.copy(result[:], bank[:])
+            result = ring.tile([P, 2, P], F32, name="result", bufs=5)
+            if MIDDLE <= b < LAST - 1:
+                nc.vector.tensor_copy(result[:], bank[:])
+            else:
+                nc.scalar.copy(result[:], bank[:])
             nc.sync.dma_start(out[:, b * P:(b + 1) * P].rearrange("(g n) j -> n g j", g=2), result[:])
 
         for b in range(AHEAD):
             project_entity(b)
-        project_relation(0)
-        project_relation(1)
+            project_relation(b)
         for step in range(LAST):
             multiply(step)
-            if step >= LAG:
-                quantise(step - LAG)
-            if step != ON_TENSOR:
+            if step == MIDDLE + 1:
+                quantise(range(MIDDLE), MIDDLE)
+            if step != MIDDLE:
                 combine(step)
             if step + AHEAD < BLOCKS:
                 project_entity(step + AHEAD)
                 project_relation(step + AHEAD)
             if step >= 1:
                 turn(step - 1)
-            if step >= LAG:
-                score(step - LAG)
-        quantise(LAST - LAG)
-        turn(LAST - 1)
-        score(LAST - LAG)
+            if step > MIDDLE:
+                score(step - MIDDLE - 1)
         finish_last()
-        for b in range(BLOCKS - LAG, LAST):
-            quantise(b)
+        quantise(range(MIDDLE, LAST), LAST)
+        for b in range(MIDDLE, BLOCKS):
             score(b)
-        score(LAST)

@@ -26,7 +26,8 @@ HALF_COLS = HALF // 16
 AHEAD = 2
 LAST = BLOCKS - 1
 MIDDLE = BLOCKS // 2 - 1
-ON_TENSOR = (MIDDLE, LAST)
+ON_TENSOR = (MIDDLE, LAST - 1, LAST)
+LATE_RESULTS = BLOCKS - MIDDLE
 COL_WER, COL_WEI, COLS_ENT = J, J + 2 * R, J + 4 * R
 COL_WRR, COL_WRI, COLS_REL = J, J + R, J + 2 * R
 COL_NI = PACK * N
@@ -185,7 +186,7 @@ def tile_list_ckg_none_kernel(
             arr, ari = rel[b]
             aer, aei = as_placed(ent[b][:, 0], b), as_placed(ent[b][:, 1], b)
             with_arr = ring.tile([P, 2, R], F32, name="with_arr")
-            if b + 1 in ON_TENSOR:
+            if b + 1 in ON_TENSOR and b not in ON_TENSOR:
                 with_ari = keep.tile([P, 2, R], F32, name="with_ari", tag=f"pause{b + 1}", align_bytes=256)
             else:
                 with_ari = ring.tile([P, 2, R], F32, name="with_ari")
@@ -209,8 +210,9 @@ def tile_list_ckg_none_kernel(
 
         def turn(b):
             turned[b] = keep.tile([P, 2, P, PACK], BF16, name="turned", tag=f"turned{b}", align_bytes=64)
-            if b == MIDDLE:
-                for c, bank in enumerate((turn_bank([P, PACK, P]), score_bank([P, PACK, P]))):
+            if b in ON_TENSOR:
+                for c, new_bank in enumerate((turn_bank, score_bank) if b == MIDDLE else (ent_bank, ent_bank)):
+                    bank = new_bank([P, PACK, P])
                     for t in range(PACK):
                         for term in range(2):
                             nc.tensor.matmul(bank[:, t, :], prod[b][term][:, c, t * P:(t + 1) * P], identity[:],
@@ -231,8 +233,6 @@ def tile_list_ckg_none_kernel(
             codes = keep.tile([P, len(blocks), 2 * P], U32, name="codes", tag=f"pause{pause}", align_bytes=256)
             planes = keep.tile([P, len(blocks), 2 * P], U8, name=f"planes{pause}", align_bytes=256)
             for i, b in enumerate(blocks):
-                if b not in turned:
-                    turn(b)
                 quant[b] = (codes[:, i, :], planes[:, i, :])
                 nc.vector.quantize_mx(out=codes[:, i, :].bitcast(FP8X4), scales=planes[:, i, :],
                                       in_=turned[b][:].rearrange("p c j t -> p (c j t)"))
@@ -243,7 +243,7 @@ def tile_list_ckg_none_kernel(
             quant[LAST] = (codes, plane)
             arr, ari = rel[LAST]
             aer, aei = as_placed(ent[LAST][:, 0], LAST), as_placed(ent[LAST][:, 1], LAST)
-            for c, bank in enumerate((ent_bank([P, PACK, P]), ent_bank([P, PACK, P]))):
+            for c, bank in enumerate((turn_bank([P, PACK, P]), rel_bank([P, PACK, P]))):
                 left = ring.tile([P, PACK, P], F32, name="left", bufs=2)
                 right = ring.tile([P, PACK, P], F32, name="right", bufs=2)
                 if c == 0:
@@ -264,7 +264,7 @@ def tile_list_ckg_none_kernel(
 
         def score(b):
             codes, plane = quant[b]
-            bank = (rel_bank if b > MIDDLE else score_bank)([P, 2, P])
+            bank = (score_bank if b <= MIDDLE else ent_bank if b < LAST - 1 else rel_bank)([P, 2, P])
             for g in range(2):
                 nc.tensor.matmul_mx(
                     out=bank[:, g, :], lhsT=cand_sb[:, PACK * P * g:PACK * P * (g + 1)].bitcast(FP8X4),
@@ -274,7 +274,7 @@ def tile_list_ckg_none_kernel(
                     out=bank[:, g, :], lhsT=cand_sb[:, COL_NI + 2 * P * g:COL_NI + 2 * P * (g + 1)].bitcast(FP4X4),
                     lhsT_scale=cand_planes[:, 1, g * P:(g + 1) * P],
                     rhs=codes[:, P:2 * P].bitcast(FP8X4), rhs_scale=plane[:, P:2 * P], start=False, stop=True)
-            result = ring.tile([P, 2, P], F32, name="result", bufs=5)
+            result = ring.tile([P, 2, P], F32, name="result", bufs=LATE_RESULTS)
             if MIDDLE <= b < LAST - 1:
                 nc.vector.tensor_copy(result[:], bank[:])
             else:
@@ -288,7 +288,7 @@ def tile_list_ckg_none_kernel(
             multiply(step)
             if step == MIDDLE + 1:
                 quantise(range(MIDDLE), MIDDLE)
-            if step != MIDDLE:
+            if step not in ON_TENSOR:
                 combine(step)
             if step + AHEAD < BLOCKS:
                 project_entity(step + AHEAD)
@@ -297,7 +297,8 @@ def tile_list_ckg_none_kernel(
                 turn(step - 1)
             if step > MIDDLE:
                 score(step - MIDDLE - 1)
+        turn(LAST - 1)
         finish_last()
-        quantise(range(MIDDLE, LAST), LAST)
+        quantise(range(MIDDLE, LAST), LAST - 1)
         for b in range(MIDDLE, BLOCKS):
             score(b)

@@ -26,7 +26,7 @@ HALF_COLS = HALF // 16
 AHEAD = 2
 LAST = BLOCKS - 1
 MIDDLE = BLOCKS // 2 - 1
-ON_TENSOR = (MIDDLE, LAST - 1, LAST)
+ON_TENSOR = (2, 5, 7)
 LATE_RESULTS = BLOCKS - MIDDLE
 COL_WER, COL_WEI, COLS_ENT = J, J + 2 * R, J + 4 * R
 COL_WRR, COL_WRI, COLS_REL = J, J + R, J + 2 * R
@@ -134,17 +134,8 @@ def tile_list_ckg_none_kernel(
                 picked[:], tab2_sb[:].bitcast(U32).indirect(list2[:, HALF_COLS * h:HALF_COLS * (h + 1)]))
             rel_words.append(picked)
 
-        def ent_bank(shape):
-            return psum.tile(shape, F32, name="ent_bank", bufs=2)
-
-        def turn_bank(shape):
-            return psum.tile(shape, F32, name="turn_bank", bufs=1)
-
-        def score_bank(shape):
-            return psum.tile(shape, F32, name="score_bank", bufs=1)
-
-        def rel_bank(shape):
-            return psum.tile(shape, F32, name="rel_bank", bufs=4)
+        def bank(number, shape):
+            return psum.tile(shape, F32, name=f"bank{number}", bufs=1)
 
         def by_place(view, b):
             if b in ON_TENSOR:
@@ -156,149 +147,189 @@ def tile_list_ckg_none_kernel(
                 return view.rearrange("j (t m) -> j t m", t=PACK)
             return view.rearrange("j (u m e) -> j u m e", u=2, e=2)
 
-        ent, rel, prod, summed, turned, quant = {}, {}, {}, {}, {}, {}
+        ent, rel, terms, summed, turned, quant = {}, {}, {}, {}, {}, {}
 
         def project_entity(b):
             h, j0 = divmod(b * P, HALF)
-            ent[b] = ring.tile([P, 2, R], F32, name="ent", bufs=AHEAD)
+            ent[b] = keep.tile([P, 2, R], F32, name=f"ent{b}")
             for c, (w_sb, col) in enumerate(((wer_sb, COL_WER), (wei_sb, COL_WEI))):
-                bank = ent_bank([P, R])
+                acc = bank(2 * min(b, 3) + c, [P, R])
                 for a in range(2):
                     plane = (ent_planes, ent_plane1)[a][:, b * P:(b + 1) * P]
                     nc.tensor.matmul_mx(
-                        out=bank[:], lhsT=ent_words[h][:, a, j0:j0 + P].bitcast(FP4X4), lhsT_scale=plane,
+                        out=acc[:], lhsT=ent_words[h][:, a, j0:j0 + P].bitcast(FP4X4), lhsT_scale=plane,
                         rhs=w_sb[:, a, :].bitcast(FP4X4), rhs_scale=ent_planes[:, col + a * R:col + (a + 1) * R],
                         start=(a == 0), stop=(a == 1))
-                nc.scalar.copy(as_placed(ent[b][:, c], b), by_place(bank[:], b))
+                nc.scalar.copy(as_placed(ent[b][:, c], b), by_place(acc[:], b))
 
         def project_relation(b):
             h, j0 = divmod(b * P, HALF)
             rel[b] = []
             for c, col in enumerate((COL_WRR, COL_WRI)):
-                bank = rel_bank([P, R])
+                acc = bank((6, 0)[b] + c if b < 2 else 2 + 2 * (b % 2) + c, [P, R])
                 nc.tensor.matmul_mx(
-                    out=bank[:], lhsT=rel_words[h][:, j0:j0 + P].bitcast(FP8X4),
+                    out=acc[:], lhsT=rel_words[h][:, j0:j0 + P].bitcast(FP8X4),
                     lhsT_scale=rel_planes[:, b * P:(b + 1) * P],
                     rhs=wr_sb[:, c, :].bitcast(FP8X4), rhs_scale=rel_planes[:, col:col + R], start=True, stop=True)
-                rel[b].append(by_place(bank[:], b))
+                rel[b].append(by_place(acc[:], b))
 
-        def multiply(b):
+        def multiply(b, c, hold=None):
             arr, ari = rel[b]
             aer, aei = as_placed(ent[b][:, 0], b), as_placed(ent[b][:, 1], b)
-            with_arr = ring.tile([P, 2, R], F32, name="with_arr")
-            if b + 1 in ON_TENSOR and b not in ON_TENSOR:
-                with_ari = keep.tile([P, 2, R], F32, name="with_ari", tag=f"pause{b + 1}", align_bytes=256)
+            if c == 0:
+                with_arr = ring.tile([P, 2, R], F32, name="with_arr")
+                if hold is None:
+                    with_ari = ring.tile([P, 2, R], F32, name="with_ari")
+                else:
+                    with_ari = keep.tile([P, 2, R], F32, name="with_ari", tag=hold, align_bytes=256)
+                terms[b] = (with_arr, with_ari)
+                nc.vector.tensor_tensor(as_placed(with_arr[:, 0], b), aer, arr, MULT)
+                negated = as_placed(with_ari[:, 0], b)
+                if b in ON_TENSOR:
+                    nc.vector.scalar_tensor_tensor(negated, aei, -1.0, ari, MULT, MULT)
+                else:
+                    for u in range(2):
+                        nc.vector.scalar_tensor_tensor(negated[:, u], aei[:, u], -1.0, ari[:, u], MULT, MULT)
             else:
-                with_ari = ring.tile([P, 2, R], F32, name="with_ari")
-            nc.vector.tensor_tensor(as_placed(with_arr[:, 0], b), aer, arr, MULT)
-            nc.vector.tensor_tensor(as_placed(with_arr[:, 1], b), aei, arr, MULT)
-            negated = as_placed(with_ari[:, 0], b)
-            if b in ON_TENSOR:
-                nc.vector.scalar_tensor_tensor(negated, aei, -1.0, ari, MULT, MULT)
-            else:
-                for u in range(2):
-                    nc.vector.scalar_tensor_tensor(negated[:, u], aei[:, u], -1.0, ari[:, u], MULT, MULT)
-            nc.vector.tensor_tensor(as_placed(with_ari[:, 1], b), aer, ari, MULT)
-            prod[b] = (with_arr, with_ari)
+                with_arr, with_ari = terms[b]
+                nc.vector.tensor_tensor(as_placed(with_arr[:, 1], b), aei, arr, MULT)
+                nc.vector.tensor_tensor(as_placed(with_ari[:, 1], b), aer, ari, MULT)
 
-        def combine(b):
-            if b == MIDDLE + 1:
-                summed[b] = keep.tile([P, 2, R], BF16, name="summed", tag=f"turned{MIDDLE - 1}", align_bytes=64)
+        def combine(b, parts, hold=None):
+            n = parts.stop - parts.start
+            if hold is None:
+                total = ring.tile([P, n, R], BF16, name="summed", align_bytes=64)
             else:
-                summed[b] = ring.tile([P, 2, R], BF16, name="summed", align_bytes=64)
-            nc.gpsimd.tensor_tensor(summed[b][:], prod[b][0][:], prod[b][1][:], ADD)
+                total = keep.tile([P, n, R], BF16, name="summed", tag=hold, align_bytes=64)
+            nc.gpsimd.tensor_tensor(total[:], terms[b][0][:, parts], terms[b][1][:, parts], ADD)
+            summed[b, parts.start] = total
 
-        def turn(b):
-            turned[b] = keep.tile([P, 2, P, PACK], BF16, name="turned", tag=f"turned{b}", align_bytes=64)
-            if b in ON_TENSOR:
-                for c, new_bank in enumerate((turn_bank, score_bank) if b == MIDDLE else (ent_bank, ent_bank)):
-                    bank = new_bank([P, PACK, P])
-                    for t in range(PACK):
-                        for term in range(2):
-                            nc.tensor.matmul(bank[:, t, :], prod[b][term][:, c, t * P:(t + 1) * P], identity[:],
-                                             start=(term == 0), stop=(term == 1), is_transpose=True)
-                    nc.scalar.copy(turned[b][:, c], bank[:].rearrange("p t j -> p j t"))
-                return
-            bank = turn_bank([P, 2, 2, P])
-            words = summed[b][:].rearrange("j c r -> j (c r)").bitcast(F32).rearrange(
-                "j (c u p) -> j c u p", c=2, u=2)
-            for c in range(2):
+        def new_turned(b, c, n):
+            tile = keep.tile([P, n, P, PACK], BF16, name="turned", tag=f"turned{b}_{c}", align_bytes=64)
+            for i in range(n):
+                turned[b, c + i] = tile[:, i]
+            turned[b, "all"] = tile
+            return tile
+
+        def turn_pairs(b, c, n, number):
+            tile = new_turned(b, c, n)
+            acc = bank(number, [P, n, 2, P])
+            words = summed[b, c][:].rearrange("j c r -> j (c r)").bitcast(F32).rearrange(
+                "j (c u p) -> j c u p", c=n, u=2)
+            for i in range(n):
                 for u in range(2):
-                    nc.tensor.transpose(bank[:, c, u, :], words[:, c, u, :], identity[:])
+                    nc.tensor.transpose(acc[:, i, u, :], words[:, i, u, :], identity[:])
             nc.scalar.copy(
-                turned[b][:].rearrange("p c j t -> p (c j t)").bitcast(F32).rearrange("p (c j u) -> p c j u", c=2, u=2),
-                bank[:].rearrange("p c u j -> p c j u"))
+                tile[:].rearrange("p c j t -> p (c j t)").bitcast(F32).rearrange("p (c j u) -> p c j u", c=n, u=2),
+                acc[:].rearrange("p c u j -> p c j u"))
 
-        def quantise(blocks, pause):
-            codes = keep.tile([P, len(blocks), 2 * P], U32, name="codes", tag=f"pause{pause}", align_bytes=256)
-            planes = keep.tile([P, len(blocks), 2 * P], U8, name=f"planes{pause}", align_bytes=256)
+        def turn_terms(b, c, number, tile):
+            acc = bank(number, [P, PACK, P])
+            for term in range(2):
+                for t in range(PACK):
+                    nc.tensor.matmul(acc[:, t, :], terms[b][term][:, c, t * P:(t + 1) * P], identity[:],
+                                     start=(term == 0 and t == 0), stop=(term == 1 and t == PACK - 1),
+                                     is_transpose=True)
+            nc.scalar.copy(tile, acc[:].rearrange("p t j -> p j t"))
+
+        def new_codes(blocks, hold):
+            codes = keep.tile([P, len(blocks), 2 * P], U32, name="codes", tag=hold, align_bytes=256)
+            planes = keep.tile([P, len(blocks), 2 * P], U8, name=f"planes_{hold}", align_bytes=256)
             for i, b in enumerate(blocks):
                 quant[b] = (codes[:, i, :], planes[:, i, :])
-                nc.vector.quantize_mx(out=codes[:, i, :].bitcast(FP8X4), scales=planes[:, i, :],
-                                      in_=turned[b][:].rearrange("p c j t -> p (c j t)"))
 
-        def finish_last():
-            codes = keep.tile([P, 2 * P], U32, name="last_codes", align_bytes=256)
-            plane = keep.tile([P, 2 * P], U8, name="last_plane", align_bytes=256)
-            quant[LAST] = (codes, plane)
-            arr, ari = rel[LAST]
-            aer, aei = as_placed(ent[LAST][:, 0], LAST), as_placed(ent[LAST][:, 1], LAST)
-            for c, bank in enumerate((turn_bank([P, PACK, P]), rel_bank([P, PACK, P]))):
-                left = ring.tile([P, PACK, P], F32, name="left", bufs=2)
-                right = ring.tile([P, PACK, P], F32, name="right", bufs=2)
-                if c == 0:
-                    nc.vector.tensor_tensor(left[:], aer, arr, MULT)
-                    nc.vector.scalar_tensor_tensor(right[:], aei, -1.0, ari, MULT, MULT)
-                else:
-                    nc.vector.tensor_tensor(left[:], aei, arr, MULT)
-                    nc.vector.tensor_tensor(right[:], aer, ari, MULT)
-                for term, tile in enumerate((left, right)):
-                    for t in range(PACK):
-                        nc.tensor.matmul(bank[:, t, :], tile[:, t, :], identity[:], start=(term == 0 and t == 0),
-                                         stop=(term == 1 and t == PACK - 1), is_transpose=True)
-                part_turned = ring.tile([P, P, PACK], BF16, name="part_turned", bufs=2, align_bytes=64)
-                nc.scalar.copy(part_turned[:], bank[:].rearrange("p t j -> p j t"))
+        def quantise(b, c=None):
+            codes, plane = quant[b]
+            if c is None:
+                nc.vector.quantize_mx(out=codes.bitcast(FP8X4), scales=plane,
+                                      in_=turned[b, "all"][:].rearrange("p c j t -> p (c j t)"))
+            else:
                 nc.vector.quantize_mx(out=codes[:, c * P:(c + 1) * P].bitcast(FP8X4),
                                       scales=plane[:, c * P:(c + 1) * P],
-                                      in_=part_turned[:].rearrange("p j t -> p (j t)"))
+                                      in_=turned[b, c].rearrange("p j t -> p (j t)"))
 
-        def score(b):
+        def score_pass(acc, b, g, c):
             codes, plane = quant[b]
-            bank = (score_bank if b <= MIDDLE else ent_bank if b < LAST - 1 else rel_bank)([P, 2, P])
-            for g in range(2):
-                nc.tensor.matmul_mx(
-                    out=bank[:, g, :], lhsT=cand_sb[:, PACK * P * g:PACK * P * (g + 1)].bitcast(FP8X4),
-                    lhsT_scale=cand_planes[:, 0, g * P:(g + 1) * P],
-                    rhs=codes[:, 0:P].bitcast(FP8X4), rhs_scale=plane[:, 0:P], start=True, stop=False)
-                nc.tensor.matmul_mx(
-                    out=bank[:, g, :], lhsT=cand_sb[:, COL_NI + 2 * P * g:COL_NI + 2 * P * (g + 1)].bitcast(FP4X4),
-                    lhsT_scale=cand_planes[:, 1, g * P:(g + 1) * P],
-                    rhs=codes[:, P:2 * P].bitcast(FP8X4), rhs_scale=plane[:, P:2 * P], start=False, stop=True)
-            result = ring.tile([P, 2, P], F32, name="result", bufs=LATE_RESULTS)
-            if MIDDLE <= b < LAST - 1:
-                nc.vector.tensor_copy(result[:], bank[:])
+            if c == 0:
+                words = cand_sb[:, PACK * P * g:PACK * P * (g + 1)].bitcast(FP8X4)
             else:
-                nc.scalar.copy(result[:], bank[:])
-            nc.sync.dma_start(out[:, b * P:(b + 1) * P].rearrange("(g n) j -> n g j", g=2), result[:])
+                words = cand_sb[:, COL_NI + 2 * P * g:COL_NI + 2 * P * (g + 1)].bitcast(FP4X4)
+            nc.tensor.matmul_mx(
+                out=acc, lhsT=words, lhsT_scale=cand_planes[:, c, g * P:(g + 1) * P],
+                rhs=codes[:, c * P:(c + 1) * P].bitcast(FP8X4), rhs_scale=plane[:, c * P:(c + 1) * P],
+                start=(c == 0), stop=(c == 1))
 
-        for b in range(AHEAD):
+        def score(first, n, number, copy=nc.scalar.copy):
+            acc = bank(number, [P, 2, n, P])
+            for i in range(n):
+                for g in range(2):
+                    for c in range(2):
+                        score_pass(acc[:, g, i, :], first + i, g, c)
+            result = keep.tile([P, 2, n * P], F32, name=f"result{first}")
+            copy(result[:], acc[:].rearrange("n g i j -> n g (i j)"))
+            nc.sync.dma_start(out[:, first * P:(first + n) * P].rearrange("(g n) j -> n g j", g=2), result[:])
+
+        both = slice(0, 2)
+        for b in range(3):
             project_entity(b)
+        for b in range(4):
             project_relation(b)
-        for step in range(LAST):
-            multiply(step)
-            if step == MIDDLE + 1:
-                quantise(range(MIDDLE), MIDDLE)
-            if step not in ON_TENSOR:
-                combine(step)
-            if step + AHEAD < BLOCKS:
-                project_entity(step + AHEAD)
-                project_relation(step + AHEAD)
-            if step >= 1:
-                turn(step - 1)
-            if step > MIDDLE:
-                score(step - MIDDLE - 1)
-        turn(LAST - 1)
-        finish_last()
-        quantise(range(MIDDLE, LAST), LAST - 1)
-        for b in range(MIDDLE, BLOCKS):
-            score(b)
+        for first in (0, 3):
+            for b in (first, first + 1):
+                multiply(b, 0, hold=f"pause{first}" if b > first else None)
+                multiply(b, 1)
+                if b == 3:
+                    new_codes((0, 1), "pause0")
+                    quantise(0)
+                    quantise(1)
+                combine(b, both, hold="turned1_0" if b == 3 else None)
+                if b >= 2:
+                    project_relation(b + 2)
+                if b > first:
+                    turn_pairs(first, 0, 2, 0)
+                if b == 4:
+                    score(0, 2, 1)
+                project_entity(b + 3)
+            b = first + 2
+            multiply(b, 0)
+            multiply(b, 1)
+            project_relation(b + 2)
+            turn_pairs(b - 1, 0, 2, 0)
+            tile = new_turned(b, 0, 2)
+            turn_terms(b, 0, 1, tile[:, 0])
+            turn_terms(b, 1, 0, tile[:, 1])
+            if b + 3 < BLOCKS:
+                project_entity(b + 3)
+
+        multiply(6, 0, hold="pause6")
+        new_codes((2, 3), "pause3")
+        for b in (2, 3):
+            quantise(b)
+        combine(6, slice(0, 1), hold="turned3_0")
+        multiply(6, 1)
+        combine(6, slice(1, 2))
+        score(2, 2, 6)
+        turn_pairs(6, 0, 1, 7)
+        multiply(7, 0)
+        turn_pairs(6, 1, 1, 2)
+        turn_terms(7, 0, 3, new_turned(7, 0, 1)[:, 0])
+        multiply(7, 1)
+        turn_terms(7, 1, 6, new_turned(7, 1, 1)[:, 0])
+        new_codes((4, 5, 6, 7), "pause6")
+        quantise(4)
+        quantise(5)
+        score(4, 2, 1)
+        quantise(6, 0)
+        quantise(6, 1)
+        quantise(7, 0)
+        score(6, 1, 0, nc.vector.tensor_copy)
+        last = [bank(number, [P, P]) for number in (7, 2)]
+        for g in range(2):
+            score_pass(last[g][:], 7, g, 0)
+        quantise(7, 1)
+        result = keep.tile([P, 2, P], F32, name="result7")
+        for g in range(2):
+            score_pass(last[g][:], 7, g, 1)
+        nc.scalar.copy(result[:, 0], last[0][:])
+        nc.vector.tensor_copy(result[:, 1], last[1][:])
+        nc.sync.dma_start(out[:, 7 * P:8 * P].rearrange("(g n) j -> n g j", g=2), result[:])

@@ -103,9 +103,8 @@ def tile_list_ckg_none_kernel(
         nc.sync.dma_start(tab2_sb[:], words_view(tab2_words))
         rel_planes = keep.tile([P, COLS_REL], U8, name="rel_planes", tag="first", align_bytes=256)
         nc.vector.memset(rel_planes[:].bitcast(I32), 0)
-        for base in range(0, P, QUADRANT):
-            nc.sync.dma_start(rel_planes[base:base + 4, :].bitcast(I32),
-                              rel_rows[base:base + QUADRANT:8, :].bitcast(I32))
+        for r in range(4):
+            nc.sync.dma_start(rel_planes[r:P:QUADRANT, :].bitcast(I32), rel_rows[8 * r:P:QUADRANT, :].bitcast(I32))
 
         ent_words, rel_words = [], []
         for h in range(2):
@@ -151,9 +150,9 @@ def tile_list_ckg_none_kernel(
 
         def project_entity(b):
             h, j0 = divmod(b * P, HALF)
-            ent[b] = keep.tile([P, 2, R], F32, name=f"ent{b}")
+            ent[b] = ring.tile([P, 2, R], F32, name="ent", bufs=AHEAD)
             for c, (w_sb, col) in enumerate(((wer_sb, COL_WER), (wei_sb, COL_WEI))):
-                acc = bank(2 * min(b, 3) + c, [P, R])
+                acc = bank(c, [P, R])
                 for a in range(2):
                     plane = (ent_planes, ent_plane1)[a][:, b * P:(b + 1) * P]
                     nc.tensor.matmul_mx(
@@ -166,7 +165,7 @@ def tile_list_ckg_none_kernel(
             h, j0 = divmod(b * P, HALF)
             rel[b] = []
             for c, col in enumerate((COL_WRR, COL_WRI)):
-                acc = bank((6, 0)[b] + c if b < 2 else 2 + 2 * (b % 2) + c, [P, R])
+                acc = bank(2 + 2 * (b % 2) + c, [P, R])
                 nc.tensor.matmul_mx(
                     out=acc[:], lhsT=rel_words[h][:, j0:j0 + P].bitcast(FP8X4),
                     lhsT_scale=rel_planes[:, b * P:(b + 1) * P],
@@ -270,9 +269,8 @@ def tile_list_ckg_none_kernel(
             nc.sync.dma_start(out[:, first * P:(first + n) * P].rearrange("(g n) j -> n g j", g=2), result[:])
 
         both = slice(0, 2)
-        for b in range(3):
+        for b in range(AHEAD):
             project_entity(b)
-        for b in range(4):
             project_relation(b)
         for first in (0, 3):
             for b in (first, first + 1):
@@ -283,24 +281,21 @@ def tile_list_ckg_none_kernel(
                     quantise(0)
                     quantise(1)
                 combine(b, both, hold="turned1_0" if b == 3 else None)
-                if b >= 2:
-                    project_relation(b + 2)
+                project_entity(b + AHEAD)
+                project_relation(b + AHEAD)
                 if b > first:
-                    turn_pairs(first, 0, 2, 0)
-                if b == 4:
-                    score(0, 2, 1)
-                project_entity(b + 3)
+                    turn_pairs(first, 0, 2, 6)
             b = first + 2
             multiply(b, 0)
             multiply(b, 1)
-            project_relation(b + 2)
-            turn_pairs(b - 1, 0, 2, 0)
+            project_entity(b + AHEAD)
+            project_relation(b + AHEAD)
+            turn_pairs(b - 1, 0, 2, 6)
             tile = new_turned(b, 0, 2)
-            turn_terms(b, 0, 1, tile[:, 0])
-            turn_terms(b, 1, 0, tile[:, 1])
-            if b + 3 < BLOCKS:
-                project_entity(b + 3)
+            turn_terms(b, 0, 7, tile[:, 0])
+            turn_terms(b, 1, 6 if first == 0 else 0, tile[:, 1])
 
+        score(0, 2, 1)
         multiply(6, 0, hold="pause6")
         new_codes((2, 3), "pause3")
         for b in (2, 3):
@@ -308,13 +303,13 @@ def tile_list_ckg_none_kernel(
         combine(6, slice(0, 1), hold="turned3_0")
         multiply(6, 1)
         combine(6, slice(1, 2))
-        score(2, 2, 6)
-        turn_pairs(6, 0, 1, 7)
+        turn_pairs(6, 0, 1, 6)
+        score(2, 2, 2)
         multiply(7, 0)
-        turn_pairs(6, 1, 1, 2)
-        turn_terms(7, 0, 3, new_turned(7, 0, 1)[:, 0])
+        turn_pairs(6, 1, 1, 3)
+        turn_terms(7, 0, 7, new_turned(7, 0, 1)[:, 0])
         multiply(7, 1)
-        turn_terms(7, 1, 6, new_turned(7, 1, 1)[:, 0])
+        turn_terms(7, 1, 0, new_turned(7, 1, 1)[:, 0])
         new_codes((4, 5, 6, 7), "pause6")
         quantise(4)
         quantise(5)
@@ -322,8 +317,8 @@ def tile_list_ckg_none_kernel(
         quantise(6, 0)
         quantise(6, 1)
         quantise(7, 0)
-        score(6, 1, 0, nc.vector.tensor_copy)
-        last = [bank(number, [P, P]) for number in (7, 2)]
+        score(6, 1, 6, nc.vector.tensor_copy)
+        last = [bank(number, [P, P]) for number in (3, 2)]
         for g in range(2):
             score_pass(last[g][:], 7, g, 0)
         quantise(7, 1)

@@ -26,7 +26,7 @@ HALF_COLS = HALF // 16
 AHEAD = 2
 LAST = BLOCKS - 1
 MIDDLE = BLOCKS // 2 - 1
-ON_TENSOR = (2, 5, 7)
+ON_TENSOR = (1, 5, 7)
 LATE_RESULTS = BLOCKS - MIDDLE
 COL_WER, COL_WEI, COLS_ENT = J, J + 2 * R, J + 4 * R
 COL_WRR, COL_WRI, COLS_REL = J, J + R, J + 2 * R
@@ -51,6 +51,7 @@ def tile_list_ckg_none_kernel(
         tab_rows = keep.tile([P, T], U8, name="tab_rows", tag="first", align_bytes=256)
         tab2_rows = keep.tile([P, T], U8, name="tab2_rows", tag="second", align_bytes=256)
         ent_planes = keep.tile([P, COLS_ENT], U8, name="ent_planes", align_bytes=256)
+        ent_rows = keep.tile([P, COLS_ENT], U8, name="ent_rows", align_bytes=256)
         ent_plane1 = keep.tile([P, J], U8, name="ent_plane1", align_bytes=256)
         rel_rows = keep.tile([P, COLS_REL], U8, name="rel_rows", align_bytes=256)
         identity = keep.tile([P, P], F32, name="identity", align_bytes=64)
@@ -63,7 +64,7 @@ def tile_list_ckg_none_kernel(
                             scales.rearrange("a q n -> q a n").bitcast(I32))
 
         nc.gpsimd.memset(tab_rows[32:64, :].bitcast(I32), 0)
-        nc.gpsimd.memset(ent_planes[:, COL_WER:COLS_ENT].bitcast(I32), 0)
+        nc.gpsimd.memset(ent_planes[:].bitcast(I32), 0)
         nc.vector.memset(tab2_rows[:].bitcast(I32), 0)
         nc.vector.memset(zeros[:], 0)
         nc.vector.tensor_copy(ent_plane1[:].bitcast(I32), zeros[:])
@@ -76,30 +77,26 @@ def tile_list_ckg_none_kernel(
         nc.sync.dma_start(list2[:], offs2)
         nc.sync.dma_start(wer_sb[:].bitcast(I32), wer_words.rearrange("a p n -> p a n").bitcast(I32))
         nc.sync.dma_start(wei_sb[:].bitcast(I32), wei_words.rearrange("a p n -> p a n").bitcast(I32))
-        load_scale_rows(nc.sync, ent_planes[0:16, COL_WER:COL_WEI], wer_scales)
-        load_scale_rows(nc.sync, ent_planes[0:16, COL_WEI:COLS_ENT], wei_scales)
+        load_scale_rows(nc.sync, ent_rows[0:16, COL_WER:COL_WEI], wer_scales)
+        load_scale_rows(nc.sync, ent_rows[0:16, COL_WEI:COLS_ENT], wei_scales)
         nc.sync.dma_start(tab2_rows[0:P:8, :].bitcast(I32), tab2_scales[0].bitcast(I32))
         tab_sb = keep.tile([P, T], I32, name="tab_sb", tag="table", align_bytes=64)
         nc.sync.dma_start(tab_sb[:], words_view(tab_words))
 
         got_rows = keep.tile([P, J], U8, name="got_rows", align_bytes=256)
         nc.vector.tensor_copy(got_rows[:], tab_rows[:].indirect(list1[:]))
-        nc.vector.tensor_copy(ent_planes[:, 0:J].bitcast(I32), got_rows[:].bitcast(I32))
-        for quad in range(4):
-            queue = nc.gpsimd if quad == 0 else nc.sync
-            queue.dma_start(ent_plane1[QUADRANT * quad:QUADRANT * quad + 4, :].bitcast(I32),
-                            got_rows[16 + 4 * quad:20 + 4 * quad, :].bitcast(I32))
-        for quad in range(1, 4):
-            nc.sync.dma_start(ent_planes[QUADRANT * quad:QUADRANT * quad + 4, :].bitcast(I32),
-                              ent_planes[4 * quad:4 * quad + 4, :].bitcast(I32))
+        nc.vector.tensor_copy(ent_rows[:, 0:J].bitcast(I32), got_rows[:].bitcast(I32))
+        for r in range(4):
+            queue = nc.gpsimd if r < 2 else nc.sync
+            queue.dma_start(ent_plane1[r:P:QUADRANT, :].bitcast(I32), got_rows[16 + r:32:4, :].bitcast(I32))
+        for r in range(4):
+            nc.sync.dma_start(ent_planes[r:P:QUADRANT, :].bitcast(I32), ent_rows[r:16:4, :].bitcast(I32))
         make_identity(nc, identity[:])
 
-        for h in range(2):
-            got2_rows = keep.tile([P, HALF], U8, name=f"got2_rows{h}", tag=f"gathered{h}", align_bytes=256)
-            nc.vector.tensor_copy(got2_rows[:], tab2_rows[:].indirect(list2[:, HALF_COLS * h:HALF_COLS * (h + 1)]))
-            nc.vector.tensor_copy(
-                rel_rows[:, h * HALF:(h + 1) * HALF].bitcast(I32), got2_rows[:].bitcast(I32))
-        tab2_sb = keep.tile([P, T], I32, name="tab2_sb", tag="gathered0", align_bytes=256)
+        got2_rows = keep.tile([P, J], U8, name="got2_rows", tag="gathered1", align_bytes=256)
+        nc.vector.tensor_copy(got2_rows[:], tab2_rows[:].indirect(list2[:]))
+        nc.vector.tensor_copy(rel_rows[:, 0:J].bitcast(I32), got2_rows[:].bitcast(I32))
+        tab2_sb = keep.tile([P, T], I32, name="tab2_sb", tag="second", align_bytes=256)
         nc.sync.dma_start(tab2_sb[:], words_view(tab2_words))
         rel_planes = keep.tile([P, COLS_REL], U8, name="rel_planes", tag="first", align_bytes=256)
         nc.vector.memset(rel_planes[:].bitcast(I32), 0)
@@ -108,7 +105,7 @@ def tile_list_ckg_none_kernel(
 
         ent_words, rel_words = [], []
         for h in range(2):
-            pairs = keep.tile([P, HALF], U32, name=f"pairs{h}", tag="second", align_bytes=256)
+            pairs = keep.tile([P, HALF], U32, name=f"pairs{h}", tag="pairs", align_bytes=256)
             nc.vector.tensor_copy(
                 pairs[:], tab_sb[:].bitcast(U32).indirect(list1[:, HALF_COLS * h:HALF_COLS * (h + 1)]))
             parted = keep.tile([P, 2, HALF], U16, name=f"parted{h}", align_bytes=256)
@@ -118,15 +115,14 @@ def tile_list_ckg_none_kernel(
         nc.sync.dma_start(wr_sb[:, 0, :], words_view(wrr_words))
         nc.sync.dma_start(wr_sb[:, 1, :], words_view(wri_words))
 
-        cand_sb = keep.tile([P, COL_NI + 2 * N], U8, name="cand_sb", tag="second", align_bytes=256)
+        cand_sb = keep.tile([P, COL_NI + 2 * N], U8, name="cand_sb", tag="pairs", align_bytes=256)
         nc.sync.dma_start(cand_sb[:, 0:COL_NI].bitcast(I32), words_view(nr_words))
         nc.sync.dma_start(cand_sb[:, COL_NI:COL_NI + 2 * N].bitcast(I32), ni_words[0].bitcast(I32))
         cand_planes = keep.tile([P, 2, N], U8, name="cand_planes", tag="table", align_bytes=64)
         nc.vector.memset(cand_planes[:].bitcast(I32), 0)
         for c, cand_scales in enumerate((nr_scales, ni_scales)):
-            for quad in range(4):
-                nc.sync.dma_start(cand_planes[QUADRANT * quad:QUADRANT * quad + 4, c, :].bitcast(I32),
-                                  cand_scales[0, 4 * quad:4 * quad + 4, :].bitcast(I32))
+            for r in range(4):
+                nc.sync.dma_start(cand_planes[r:P:QUADRANT, c, :].bitcast(I32), cand_scales[0, r:16:4, :].bitcast(I32))
         for h in range(2):
             picked = keep.tile([P, HALF], U32, name=f"picked{h}", align_bytes=256)
             nc.vector.tensor_copy(
@@ -150,9 +146,9 @@ def tile_list_ckg_none_kernel(
 
         def project_entity(b):
             h, j0 = divmod(b * P, HALF)
-            ent[b] = ring.tile([P, 2, R], F32, name="ent", bufs=AHEAD)
+            ent[b] = ring.tile([P, 2, R], F32, name="ent", bufs=3)
             for c, (w_sb, col) in enumerate(((wer_sb, COL_WER), (wei_sb, COL_WEI))):
-                acc = bank(c, [P, R])
+                acc = bank(2 * min(b, 3) + c, [P, R])
                 for a in range(2):
                     plane = (ent_planes, ent_plane1)[a][:, b * P:(b + 1) * P]
                     nc.tensor.matmul_mx(
@@ -165,7 +161,7 @@ def tile_list_ckg_none_kernel(
             h, j0 = divmod(b * P, HALF)
             rel[b] = []
             for c, col in enumerate((COL_WRR, COL_WRI)):
-                acc = bank(2 + 2 * (b % 2) + c, [P, R])
+                acc = bank((6, 0)[b] + c if b < 2 else 2 + 2 * (b % 2) + c, [P, R])
                 nc.tensor.matmul_mx(
                     out=acc[:], lhsT=rel_words[h][:, j0:j0 + P].bitcast(FP8X4),
                     lhsT_scale=rel_planes[:, b * P:(b + 1) * P],
@@ -268,57 +264,87 @@ def tile_list_ckg_none_kernel(
             copy(result[:], acc[:].rearrange("n g i j -> n g (i j)"))
             nc.sync.dma_start(out[:, first * P:(first + n) * P].rearrange("(g n) j -> n g j", g=2), result[:])
 
-        both = slice(0, 2)
-        for b in range(AHEAD):
-            project_entity(b)
-            project_relation(b)
-        for first in (0, 3):
-            for b in (first, first + 1):
-                multiply(b, 0, hold=f"pause{first}" if b > first else None)
-                multiply(b, 1)
-                if b == 3:
-                    new_codes((0, 1), "pause0")
-                    quantise(0)
-                    quantise(1)
-                combine(b, both, hold="turned1_0" if b == 3 else None)
-                project_entity(b + AHEAD)
-                project_relation(b + AHEAD)
-                if b > first:
-                    turn_pairs(first, 0, 2, 6)
-            b = first + 2
-            multiply(b, 0)
-            multiply(b, 1)
-            project_entity(b + AHEAD)
-            project_relation(b + AHEAD)
-            turn_pairs(b - 1, 0, 2, 6)
+        def turn_both(b, numbers):
             tile = new_turned(b, 0, 2)
-            turn_terms(b, 0, 7, tile[:, 0])
-            turn_terms(b, 1, 6 if first == 0 else 0, tile[:, 1])
+            for c in range(2):
+                turn_terms(b, c, numbers[c], tile[:, c])
 
-        score(0, 2, 1)
+        both = slice(0, 2)
+        for b in range(3):
+            project_entity(b)
+        for b in range(4):
+            project_relation(b)
+
+        arr_sb = keep.tile([P, R], F32, name="arr_sb")
+        nc.scalar.copy(as_placed(arr_sb[:], 1), rel[1][0])
+        with_arr = ring.tile([P, 2, R], F32, name="with_arr")
+        nc.gpsimd.tensor_tensor(with_arr[:], ent[1][:], arr_sb[:].unsqueeze(1).to_broadcast([P, 2, R]), MULT)
+
+        multiply(0, 0)
+        multiply(0, 1)
+        combine(0, both)
+        project_entity(3)
+        with_ari = ring.tile([P, 2, R], F32, name="with_ari")
+        nc.vector.scalar_tensor_tensor(as_placed(with_ari[:, 0], 1), as_placed(ent[1][:, 1], 1), -1.0, rel[1][1],
+                                       MULT, MULT)
+        nc.vector.tensor_tensor(as_placed(with_ari[:, 1], 1), as_placed(ent[1][:, 0], 1), rel[1][1], MULT)
+        terms[1] = (with_arr, with_ari)
+        turn_both(1, (0, 1))
+        project_entity(4)
+
+        multiply(2, 0)
+        multiply(2, 1)
+        combine(2, both)
+        project_relation(4)
+        turn_pairs(0, 0, 2, 0)
+        project_entity(5)
+
+        multiply(3, 0)
+        multiply(3, 1)
+        combine(3, both)
+        project_relation(5)
+        turn_pairs(2, 0, 2, 1)
+        project_entity(6)
+
+        multiply(4, 0, hold="pause4")
+        multiply(4, 1)
+        combine(4, both)
+        project_relation(6)
+        turn_pairs(3, 0, 2, 0)
+        project_entity(7)
+
+        multiply(5, 0)
+        multiply(5, 1)
+        project_relation(7)
+        tile = new_turned(5, 0, 2)
+        turn_terms(5, 0, 0, tile[:, 0])
+        turn_pairs(4, 0, 2, 1)
+        turn_terms(5, 1, 6, tile[:, 1])
+
         multiply(6, 0, hold="pause6")
-        new_codes((2, 3), "pause3")
-        for b in (2, 3):
+        new_codes((0, 1, 2, 3), "pause4")
+        for b in range(4):
             quantise(b)
         combine(6, slice(0, 1), hold="turned3_0")
         multiply(6, 1)
         combine(6, slice(1, 2))
-        turn_pairs(6, 0, 1, 6)
-        score(2, 2, 2)
+        score(0, 2, 7)
+        turn_pairs(6, 0, 1, 1)
+        score(2, 2, 0)
         multiply(7, 0)
-        turn_pairs(6, 1, 1, 3)
-        turn_terms(7, 0, 7, new_turned(7, 0, 1)[:, 0])
+        turn_pairs(6, 1, 1, 2)
+        turn_terms(7, 0, 3, new_turned(7, 0, 1)[:, 0])
         multiply(7, 1)
-        turn_terms(7, 1, 0, new_turned(7, 1, 1)[:, 0])
+        turn_terms(7, 1, 6, new_turned(7, 1, 1)[:, 0])
         new_codes((4, 5, 6, 7), "pause6")
         quantise(4)
         quantise(5)
-        score(4, 2, 1)
+        score(4, 2, 7)
         quantise(6, 0)
         quantise(6, 1)
         quantise(7, 0)
-        score(6, 1, 6, nc.vector.tensor_copy)
-        last = [bank(number, [P, P]) for number in (3, 2)]
+        score(6, 1, 1, nc.vector.tensor_copy)
+        last = [bank(number, [P, P]) for number in (0, 2)]
         for g in range(2):
             score_pass(last[g][:], 7, g, 0)
         quantise(7, 1)

@@ -109,7 +109,12 @@ def tile_list_ckg_none_kernel(
             nc.vector.tensor_copy(
                 pairs[:], tab_sb[:].bitcast(U32).indirect(list1[:, HALF_COLS * h:HALF_COLS * (h + 1)]))
             parted = keep.tile([P, 2, HALF], U16, name=f"parted{h}", align_bytes=256)
-            nc.vector.tensor_copy(parted[:], pairs[:].bitcast(U16).rearrange("p (j d) -> p d j", d=2))
+            by_pass = pairs[:].bitcast(U16).rearrange("p (j d) -> p d j", d=2)
+            if h == 0:
+                nc.vector.tensor_copy(parted[:, :, 0:P], by_pass[:, :, 0:P])
+                nc.vector.tensor_copy(parted[:, :, P:HALF], by_pass[:, :, P:HALF])
+            else:
+                nc.vector.tensor_copy(parted[:], by_pass)
             ent_words.append(parted)
         wr_sb = keep.tile([P, 2, R], I32, name="wr_sb", tag="gathered1", align_bytes=256)
         nc.sync.dma_start(wr_sb[:, 0, :], words_view(wrr_words))
@@ -146,9 +151,9 @@ def tile_list_ckg_none_kernel(
 
         def project_entity(b):
             h, j0 = divmod(b * P, HALF)
-            ent[b] = ring.tile([P, 2, R], F32, name="ent", bufs=3)
+            ent[b] = ring.tile([P, 2, R], F32, name="ent", bufs=4)
             for c, (w_sb, col) in enumerate(((wer_sb, COL_WER), (wei_sb, COL_WEI))):
-                acc = bank(2 * min(b, 3) + c, [P, R])
+                acc = bank((2 * b + 6) % 8 + c if b < 4 else 6 + c, [P, R])
                 for a in range(2):
                     plane = (ent_planes, ent_plane1)[a][:, b * P:(b + 1) * P]
                     nc.tensor.matmul_mx(
@@ -270,7 +275,7 @@ def tile_list_ckg_none_kernel(
                 turn_terms(b, c, numbers[c], tile[:, c])
 
         both = slice(0, 2)
-        for b in range(3):
+        for b in range(4):
             project_entity(b)
         for b in range(4):
             project_relation(b)
@@ -283,35 +288,34 @@ def tile_list_ckg_none_kernel(
         multiply(0, 0)
         multiply(0, 1)
         combine(0, both)
-        project_entity(3)
+        project_entity(4)
         with_ari = ring.tile([P, 2, R], F32, name="with_ari")
         nc.vector.scalar_tensor_tensor(as_placed(with_ari[:, 0], 1), as_placed(ent[1][:, 1], 1), -1.0, rel[1][1],
                                        MULT, MULT)
         nc.vector.tensor_tensor(as_placed(with_ari[:, 1], 1), as_placed(ent[1][:, 0], 1), rel[1][1], MULT)
         terms[1] = (with_arr, with_ari)
         turn_both(1, (0, 1))
-        project_entity(4)
+        project_entity(5)
 
         multiply(2, 0)
         multiply(2, 1)
         combine(2, both)
         project_relation(4)
         turn_pairs(0, 0, 2, 0)
-        project_entity(5)
+        project_entity(6)
 
         multiply(3, 0)
         multiply(3, 1)
         combine(3, both)
         project_relation(5)
         turn_pairs(2, 0, 2, 1)
-        project_entity(6)
+        project_entity(7)
 
         multiply(4, 0, hold="pause4")
         multiply(4, 1)
         combine(4, both)
         project_relation(6)
         turn_pairs(3, 0, 2, 0)
-        project_entity(7)
 
         multiply(5, 0)
         multiply(5, 1)

@@ -26,7 +26,7 @@ HALF_COLS = HALF // 16
 AHEAD = 2
 LAST = BLOCKS - 1
 MIDDLE = BLOCKS // 2 - 1
-ON_TENSOR = (1, 5, 7)
+ON_TENSOR = (1, 4, 7)
 LATE_RESULTS = BLOCKS - MIDDLE
 COL_WER, COL_WEI, COLS_ENT = J, J + 2 * R, J + 4 * R
 COL_WRR, COL_WRI, COLS_REL = J, J + R, J + 2 * R
@@ -51,10 +51,9 @@ def tile_list_ckg_none_kernel(
         tab_rows = keep.tile([P, T], U8, name="tab_rows", tag="first", align_bytes=256)
         tab2_rows = keep.tile([P, T], U8, name="tab2_rows", tag="second", align_bytes=256)
         ent_planes = keep.tile([P, COLS_ENT], U8, name="ent_planes", align_bytes=256)
-        ent_rows = keep.tile([P, COLS_ENT], U8, name="ent_rows", align_bytes=256)
+        ent_rows = keep.tile([P, COLS_ENT], U8, name="ent_rows", tag="staged", align_bytes=256)
         ent_plane1 = keep.tile([P, J], U8, name="ent_plane1", align_bytes=256)
         rel_rows = keep.tile([P, COLS_REL], U8, name="rel_rows", align_bytes=256)
-        identity = keep.tile([P, P], F32, name="identity", align_bytes=64)
 
         def words_view(words):
             return words.rearrange("a p n i -> p (a n i)").bitcast(I32)
@@ -63,12 +62,12 @@ def tile_list_ckg_none_kernel(
             queue.dma_start(rows.bitcast(I32).rearrange("q (a n) -> q a n", a=scales.shape[0]),
                             scales.rearrange("a q n -> q a n").bitcast(I32))
 
-        nc.gpsimd.memset(tab_rows[32:64, :].bitcast(I32), 0)
-        nc.gpsimd.memset(ent_planes[:].bitcast(I32), 0)
         nc.vector.memset(tab2_rows[:].bitcast(I32), 0)
         nc.vector.memset(zeros[:], 0)
         nc.vector.tensor_copy(ent_plane1[:].bitcast(I32), zeros[:])
+        nc.vector.memset(tab_rows[32:64, :].bitcast(I32), 0)
         nc.vector.memset(tab_rows[64:P, :].bitcast(I32), 0)
+        nc.vector.memset(ent_planes[:].bitcast(I32), 0)
 
         load_scale_rows(nc.gpsimd, rel_rows[0:P:8, COL_WRR:COL_WRI], wrr_scales)
         load_scale_rows(nc.gpsimd, rel_rows[0:P:8, COL_WRI:COLS_REL], wri_scales)
@@ -91,7 +90,6 @@ def tile_list_ckg_none_kernel(
             queue.dma_start(ent_plane1[r:P:QUADRANT, :].bitcast(I32), got_rows[16 + r:32:4, :].bitcast(I32))
         for r in range(4):
             nc.sync.dma_start(ent_planes[r:P:QUADRANT, :].bitcast(I32), ent_rows[r:16:4, :].bitcast(I32))
-        make_identity(nc, identity[:])
 
         got2_rows = keep.tile([P, J], U8, name="got2_rows", tag="gathered1", align_bytes=256)
         nc.vector.tensor_copy(got2_rows[:], tab2_rows[:].indirect(list2[:]))
@@ -116,11 +114,13 @@ def tile_list_ckg_none_kernel(
             else:
                 nc.vector.tensor_copy(parted[:], by_pass)
             ent_words.append(parted)
+        identity = keep.tile([P, P], F32, name="identity", tag="pairs", align_bytes=256)
+        make_identity(nc, identity[:])
         wr_sb = keep.tile([P, 2, R], I32, name="wr_sb", tag="gathered1", align_bytes=256)
         nc.sync.dma_start(wr_sb[:, 0, :], words_view(wrr_words))
         nc.sync.dma_start(wr_sb[:, 1, :], words_view(wri_words))
 
-        cand_sb = keep.tile([P, COL_NI + 2 * N], U8, name="cand_sb", tag="pairs", align_bytes=256)
+        cand_sb = keep.tile([P, COL_NI + 2 * N], U8, name="cand_sb", tag="staged", align_bytes=256)
         nc.sync.dma_start(cand_sb[:, 0:COL_NI].bitcast(I32), words_view(nr_words))
         nc.sync.dma_start(cand_sb[:, COL_NI:COL_NI + 2 * N].bitcast(I32), ni_words[0].bitcast(I32))
         cand_planes = keep.tile([P, 2, N], U8, name="cand_planes", tag="table", align_bytes=64)
@@ -151,9 +151,9 @@ def tile_list_ckg_none_kernel(
 
         def project_entity(b):
             h, j0 = divmod(b * P, HALF)
-            ent[b] = ring.tile([P, 2, R], F32, name="ent", bufs=4)
+            ent[b] = ring.tile([P, 2, R], F32, name="ent", bufs=5)
             for c, (w_sb, col) in enumerate(((wer_sb, COL_WER), (wei_sb, COL_WEI))):
-                acc = bank((2 * b + 6) % 8 + c if b < 4 else 6 + c, [P, R])
+                acc = bank((2 * b + 6) % 8 + c if b < 4 else 6 * c, [P, R])
                 for a in range(2):
                     plane = (ent_planes, ent_plane1)[a][:, b * P:(b + 1) * P]
                     nc.tensor.matmul_mx(
@@ -173,27 +173,30 @@ def tile_list_ckg_none_kernel(
                     rhs=wr_sb[:, c, :].bitcast(FP8X4), rhs_scale=rel_planes[:, col:col + R], start=True, stop=True)
                 rel[b].append(by_place(acc[:], b))
 
-        def multiply(b, c, hold=None):
-            arr, ari = rel[b]
-            aer, aei = as_placed(ent[b][:, 0], b), as_placed(ent[b][:, 1], b)
-            if c == 0:
-                with_arr = ring.tile([P, 2, R], F32, name="with_arr")
-                if hold is None:
-                    with_ari = ring.tile([P, 2, R], F32, name="with_ari")
-                else:
-                    with_ari = keep.tile([P, 2, R], F32, name="with_ari", tag=hold, align_bytes=256)
-                terms[b] = (with_arr, with_ari)
-                nc.vector.tensor_tensor(as_placed(with_arr[:, 0], b), aer, arr, MULT)
-                negated = as_placed(with_ari[:, 0], b)
-                if b in ON_TENSOR:
-                    nc.vector.scalar_tensor_tensor(negated, aei, -1.0, ari, MULT, MULT)
-                else:
-                    for u in range(2):
-                        nc.vector.scalar_tensor_tensor(negated[:, u], aei[:, u], -1.0, ari[:, u], MULT, MULT)
+        def new_terms(b, hold=None):
+            with_arr = ring.tile([P, 2, R], F32, name="with_arr")
+            if hold is None:
+                with_ari = ring.tile([P, 2, R], F32, name="with_ari")
             else:
-                with_arr, with_ari = terms[b]
-                nc.vector.tensor_tensor(as_placed(with_arr[:, 1], b), aei, arr, MULT)
-                nc.vector.tensor_tensor(as_placed(with_ari[:, 1], b), aer, ari, MULT)
+                with_ari = keep.tile([P, 2, R], F32, name="with_ari", tag=hold, align_bytes=256)
+            terms[b] = (with_arr, with_ari)
+
+        def product(b, c, term):
+            target = as_placed(terms[b][term][:, c], b)
+            factor = as_placed(ent[b][:, (c + term) % 2], b)
+            if (c, term) != (0, 1):
+                nc.vector.tensor_tensor(target, factor, rel[b][term], MULT)
+            elif b in ON_TENSOR:
+                nc.vector.scalar_tensor_tensor(target, factor, -1.0, rel[b][term], MULT, MULT)
+            else:
+                for u in range(2):
+                    nc.vector.scalar_tensor_tensor(target[:, u], factor[:, u], -1.0, rel[b][term][:, u], MULT, MULT)
+
+        def multiply(b, c, hold=None):
+            if c == 0:
+                new_terms(b, hold)
+            product(b, c, 0)
+            product(b, c, 1)
 
         def combine(b, parts, hold=None):
             n = parts.stop - parts.start
@@ -211,7 +214,7 @@ def tile_list_ckg_none_kernel(
             turned[b, "all"] = tile
             return tile
 
-        def turn_pairs(b, c, n, number):
+        def turn_pairs(b, c, n, number, copy=nc.scalar.copy):
             tile = new_turned(b, c, n)
             acc = bank(number, [P, n, 2, P])
             words = summed[b, c][:].rearrange("j c r -> j (c r)").bitcast(F32).rearrange(
@@ -219,7 +222,7 @@ def tile_list_ckg_none_kernel(
             for i in range(n):
                 for u in range(2):
                     nc.tensor.transpose(acc[:, i, u, :], words[:, i, u, :], identity[:])
-            nc.scalar.copy(
+            copy(
                 tile[:].rearrange("p c j t -> p (c j t)").bitcast(F32).rearrange("p (c j u) -> p c j u", c=n, u=2),
                 acc[:].rearrange("p c u j -> p c j u"))
 
@@ -275,6 +278,12 @@ def tile_list_ckg_none_kernel(
                 turn_terms(b, c, numbers[c], tile[:, c])
 
         both = slice(0, 2)
+        warm = bank(6, [P, R])
+        for i in range(4):
+            nc.tensor.matmul_mx(
+                out=warm[:], lhsT=wer_sb[:, 0, 0:2 * P].bitcast(FP4X4), lhsT_scale=ent_planes[:, COL_WER:COL_WER + P],
+                rhs=wer_sb[:, 0, :].bitcast(FP4X4), rhs_scale=ent_planes[:, COL_WER:COL_WER + R],
+                start=True, stop=True)
         for b in range(4):
             project_entity(b)
         for b in range(4):
@@ -282,79 +291,79 @@ def tile_list_ckg_none_kernel(
 
         arr_sb = keep.tile([P, R], F32, name="arr_sb")
         nc.scalar.copy(as_placed(arr_sb[:], 1), rel[1][0])
-        with_arr = ring.tile([P, 2, R], F32, name="with_arr")
-        nc.gpsimd.tensor_tensor(with_arr[:], ent[1][:], arr_sb[:].unsqueeze(1).to_broadcast([P, 2, R]), MULT)
-
-        multiply(0, 0)
-        multiply(0, 1)
-        combine(0, both)
+        new_terms(1)
+        nc.gpsimd.tensor_tensor(terms[1][0][:], ent[1][:], arr_sb[:].unsqueeze(1).to_broadcast([P, 2, R]), MULT)
         project_entity(4)
-        with_ari = ring.tile([P, 2, R], F32, name="with_ari")
-        nc.vector.scalar_tensor_tensor(as_placed(with_ari[:, 0], 1), as_placed(ent[1][:, 1], 1), -1.0, rel[1][1],
-                                       MULT, MULT)
-        nc.vector.tensor_tensor(as_placed(with_ari[:, 1], 1), as_placed(ent[1][:, 0], 1), rel[1][1], MULT)
-        terms[1] = (with_arr, with_ari)
-        turn_both(1, (0, 1))
+
+        new_terms(0)
+        for term in range(2):
+            for c in range(2):
+                product(0, c, term)
+        combine(0, both)
+        for c in range(2):
+            product(1, c, 1)
+        turn_both(1, (7, 1))
         project_entity(5)
 
         multiply(2, 0)
         multiply(2, 1)
         combine(2, both)
         project_relation(4)
-        turn_pairs(0, 0, 2, 0)
+        turn_pairs(0, 0, 2, 7)
         project_entity(6)
 
-        multiply(3, 0)
+        multiply(3, 0, hold="pause3")
         multiply(3, 1)
         combine(3, both)
         project_relation(5)
         turn_pairs(2, 0, 2, 1)
         project_entity(7)
 
-        multiply(4, 0, hold="pause4")
+        multiply(4, 0)
         multiply(4, 1)
-        combine(4, both)
+        turn_pairs(3, 0, 2, 7)
         project_relation(6)
-        turn_pairs(3, 0, 2, 0)
+        turn_both(4, (1, 6))
 
         multiply(5, 0)
-        multiply(5, 1)
-        project_relation(7)
-        tile = new_turned(5, 0, 2)
-        turn_terms(5, 0, 0, tile[:, 0])
-        turn_pairs(4, 0, 2, 1)
-        turn_terms(5, 1, 6, tile[:, 1])
-
-        multiply(6, 0, hold="pause6")
-        new_codes((0, 1, 2, 3), "pause4")
+        new_codes((0, 1, 2, 3), "pause3")
         for b in range(4):
             quantise(b)
-        combine(6, slice(0, 1), hold="turned3_0")
+        combine(5, slice(0, 1), hold="turned3_0")
+        multiply(5, 1)
+        combine(5, slice(1, 2))
+        project_relation(7)
+        score(0, 2, 0)
+        score(2, 2, 7)
+        turn_pairs(5, 0, 1, 1)
+
+        multiply(6, 0, hold="pause6")
+        combine(6, slice(0, 1))
         multiply(6, 1)
         combine(6, slice(1, 2))
-        score(0, 2, 7)
-        turn_pairs(6, 0, 1, 1)
-        score(2, 2, 0)
+        turn_pairs(5, 1, 1, 6)
         multiply(7, 0)
-        turn_pairs(6, 1, 1, 2)
+        turn_pairs(6, 0, 1, 1)
         turn_terms(7, 0, 3, new_turned(7, 0, 1)[:, 0])
         multiply(7, 1)
-        turn_terms(7, 1, 6, new_turned(7, 1, 1)[:, 0])
+        turn_terms(7, 1, 0, new_turned(7, 1, 1)[:, 0])
         new_codes((4, 5, 6, 7), "pause6")
         quantise(4)
-        quantise(5)
-        score(4, 2, 7)
+        quantise(5, 0)
+        quantise(5, 1)
         quantise(6, 0)
-        quantise(6, 1)
         quantise(7, 0)
-        score(6, 1, 1, nc.vector.tensor_copy)
-        last = [bank(number, [P, P]) for number in (0, 2)]
+        turn_pairs(6, 1, 1, 5, nc.vector.tensor_copy)
+        score(4, 2, 7)
+        last = [bank(number, [P, P]) for number in (2, 1)]
         for g in range(2):
             score_pass(last[g][:], 7, g, 0)
         quantise(7, 1)
+        quantise(6, 1)
         result = keep.tile([P, 2, P], F32, name="result7")
         for g in range(2):
             score_pass(last[g][:], 7, g, 1)
         nc.scalar.copy(result[:, 0], last[0][:])
-        nc.vector.tensor_copy(result[:, 1], last[1][:])
+        nc.scalar.copy(result[:, 1], last[1][:])
         nc.sync.dma_start(out[:, 7 * P:8 * P].rearrange("(g n) j -> n g j", g=2), result[:])
+        score(6, 1, 6, nc.vector.tensor_copy)

@@ -20,14 +20,12 @@ ADD = mybir.AluOpType.add
 P = 128
 PACK = 4
 QUADRANT = 32
-BLOCKS = J // P
+ROWS = 16
 HALF = J // 2
 HALF_COLS = HALF // 16
-AHEAD = 2
-LAST = BLOCKS - 1
-MIDDLE = BLOCKS // 2 - 1
+EARLY = 4
 ON_TENSOR = (1, 4, 7)
-LATE_RESULTS = BLOCKS - MIDDLE
+HR, HI, BOTH = slice(0, 1), slice(1, 2), slice(0, 2)
 COL_WER, COL_WEI, COLS_ENT = J, J + 2 * R, J + 4 * R
 COL_WRR, COL_WRI, COLS_REL = J, J + R, J + 2 * R
 COL_NI = PACK * N
@@ -72,12 +70,12 @@ def tile_list_ckg_none_kernel(
         load_scale_rows(nc.gpsimd, rel_rows[0:P:8, COL_WRR:COL_WRI], wrr_scales)
         load_scale_rows(nc.gpsimd, rel_rows[0:P:8, COL_WRI:COLS_REL], wri_scales)
         nc.sync.dma_start(list1[:], offs)
-        nc.sync.dma_start(tab_rows[0:32, :].bitcast(I32), tab_scales.rearrange("a q t -> (a q) t").bitcast(I32))
+        nc.sync.dma_start(tab_rows[0:2 * ROWS, :].bitcast(I32), tab_scales.rearrange("a q t -> (a q) t").bitcast(I32))
         nc.sync.dma_start(list2[:], offs2)
         nc.sync.dma_start(wer_sb[:].bitcast(I32), wer_words.rearrange("a p n -> p a n").bitcast(I32))
         nc.sync.dma_start(wei_sb[:].bitcast(I32), wei_words.rearrange("a p n -> p a n").bitcast(I32))
-        load_scale_rows(nc.sync, ent_rows[0:16, COL_WER:COL_WEI], wer_scales)
-        load_scale_rows(nc.sync, ent_rows[0:16, COL_WEI:COLS_ENT], wei_scales)
+        load_scale_rows(nc.sync, ent_rows[0:ROWS, COL_WER:COL_WEI], wer_scales)
+        load_scale_rows(nc.sync, ent_rows[0:ROWS, COL_WEI:COLS_ENT], wei_scales)
         nc.sync.dma_start(tab2_rows[0:P:8, :].bitcast(I32), tab2_scales[0].bitcast(I32))
         tab_sb = keep.tile([P, T], I32, name="tab_sb", tag="table", align_bytes=64)
         nc.sync.dma_start(tab_sb[:], words_view(tab_words))
@@ -87,9 +85,9 @@ def tile_list_ckg_none_kernel(
         nc.vector.tensor_copy(ent_rows[:, 0:J].bitcast(I32), got_rows[:].bitcast(I32))
         for r in range(4):
             queue = nc.gpsimd if r < 2 else nc.sync
-            queue.dma_start(ent_plane1[r:P:QUADRANT, :].bitcast(I32), got_rows[16 + r:32:4, :].bitcast(I32))
+            queue.dma_start(ent_plane1[r:P:QUADRANT, :].bitcast(I32), got_rows[ROWS + r:2 * ROWS:4, :].bitcast(I32))
         for r in range(4):
-            nc.sync.dma_start(ent_planes[r:P:QUADRANT, :].bitcast(I32), ent_rows[r:16:4, :].bitcast(I32))
+            nc.sync.dma_start(ent_planes[r:P:QUADRANT, :].bitcast(I32), ent_rows[r:ROWS:4, :].bitcast(I32))
 
         got2_rows = keep.tile([P, J], U8, name="got2_rows", tag="gathered1", align_bytes=256)
         nc.vector.tensor_copy(got2_rows[:], tab2_rows[:].indirect(list2[:]))
@@ -102,17 +100,14 @@ def tile_list_ckg_none_kernel(
             nc.sync.dma_start(rel_planes[r:P:QUADRANT, :].bitcast(I32), rel_rows[8 * r:P:QUADRANT, :].bitcast(I32))
 
         ent_words, rel_words = [], []
-        for h in range(2):
+        for h, pieces in enumerate(((slice(0, P), slice(P, HALF)), (slice(0, HALF),))):
             pairs = keep.tile([P, HALF], U32, name=f"pairs{h}", tag="pairs", align_bytes=256)
             nc.vector.tensor_copy(
                 pairs[:], tab_sb[:].bitcast(U32).indirect(list1[:, HALF_COLS * h:HALF_COLS * (h + 1)]))
             parted = keep.tile([P, 2, HALF], U16, name=f"parted{h}", align_bytes=256)
             by_pass = pairs[:].bitcast(U16).rearrange("p (j d) -> p d j", d=2)
-            if h == 0:
-                nc.vector.tensor_copy(parted[:, :, 0:P], by_pass[:, :, 0:P])
-                nc.vector.tensor_copy(parted[:, :, P:HALF], by_pass[:, :, P:HALF])
-            else:
-                nc.vector.tensor_copy(parted[:], by_pass)
+            for piece in pieces:
+                nc.vector.tensor_copy(parted[:, :, piece], by_pass[:, :, piece])
             ent_words.append(parted)
         identity = keep.tile([P, P], F32, name="identity", tag="pairs", align_bytes=256)
         make_identity(nc, identity[:])
@@ -127,7 +122,8 @@ def tile_list_ckg_none_kernel(
         nc.vector.memset(cand_planes[:].bitcast(I32), 0)
         for c, cand_scales in enumerate((nr_scales, ni_scales)):
             for r in range(4):
-                nc.sync.dma_start(cand_planes[r:P:QUADRANT, c, :].bitcast(I32), cand_scales[0, r:16:4, :].bitcast(I32))
+                nc.sync.dma_start(cand_planes[r:P:QUADRANT, c, :].bitcast(I32),
+                                  cand_scales[0, r:ROWS:4, :].bitcast(I32))
         for h in range(2):
             picked = keep.tile([P, HALF], U32, name=f"picked{h}", align_bytes=256)
             nc.vector.tensor_copy(
@@ -136,6 +132,9 @@ def tile_list_ckg_none_kernel(
 
         def bank(number, shape):
             return psum.tile(shape, F32, name=f"bank{number}", bufs=1)
+
+        def early_bank(b, c):
+            return (2 * b + 6) % 8 + c
 
         def by_place(view, b):
             if b in ON_TENSOR:
@@ -151,9 +150,9 @@ def tile_list_ckg_none_kernel(
 
         def project_entity(b):
             h, j0 = divmod(b * P, HALF)
-            ent[b] = ring.tile([P, 2, R], F32, name="ent", bufs=5)
+            ent[b] = ring.tile([P, 2, R], F32, name="ent", bufs=EARLY + 1)
             for c, (w_sb, col) in enumerate(((wer_sb, COL_WER), (wei_sb, COL_WEI))):
-                acc = bank((2 * b + 6) % 8 + c if b < 4 else 6 * c, [P, R])
+                acc = bank(early_bank(b, c) if b < EARLY else (0, 6)[c], [P, R])
                 for a in range(2):
                     plane = (ent_planes, ent_plane1)[a][:, b * P:(b + 1) * P]
                     nc.tensor.matmul_mx(
@@ -166,19 +165,19 @@ def tile_list_ckg_none_kernel(
             h, j0 = divmod(b * P, HALF)
             rel[b] = []
             for c, col in enumerate((COL_WRR, COL_WRI)):
-                acc = bank((6, 0)[b] + c if b < 2 else 2 + 2 * (b % 2) + c, [P, R])
+                acc = bank(early_bank(b if b < EARLY else 2 + b % 2, c), [P, R])
                 nc.tensor.matmul_mx(
                     out=acc[:], lhsT=rel_words[h][:, j0:j0 + P].bitcast(FP8X4),
                     lhsT_scale=rel_planes[:, b * P:(b + 1) * P],
                     rhs=wr_sb[:, c, :].bitcast(FP8X4), rhs_scale=rel_planes[:, col:col + R], start=True, stop=True)
                 rel[b].append(by_place(acc[:], b))
 
-        def new_terms(b, hold=None):
+        def new_terms(b, tag=None):
             with_arr = ring.tile([P, 2, R], F32, name="with_arr")
-            if hold is None:
+            if tag is None:
                 with_ari = ring.tile([P, 2, R], F32, name="with_ari")
             else:
-                with_ari = keep.tile([P, 2, R], F32, name="with_ari", tag=hold, align_bytes=256)
+                with_ari = keep.tile([P, 2, R], F32, name="with_ari", tag=tag, align_bytes=256)
             terms[b] = (with_arr, with_ari)
 
         def product(b, c, term):
@@ -192,64 +191,60 @@ def tile_list_ckg_none_kernel(
                 for u in range(2):
                     nc.vector.scalar_tensor_tensor(target[:, u], factor[:, u], -1.0, rel[b][term][:, u], MULT, MULT)
 
-        def multiply(b, c, hold=None):
-            if c == 0:
-                new_terms(b, hold)
-            product(b, c, 0)
-            product(b, c, 1)
+        def multiply(b, parts):
+            for c in range(parts.start, parts.stop):
+                for term in range(2):
+                    product(b, c, term)
 
-        def combine(b, parts, hold=None):
-            n = parts.stop - parts.start
-            if hold is None:
-                total = ring.tile([P, n, R], BF16, name="summed", align_bytes=64)
+        def combine(b, parts, tag=None):
+            shape = [P, parts.stop - parts.start, R]
+            if tag is None:
+                total = ring.tile(shape, BF16, name="summed", align_bytes=64)
             else:
-                total = keep.tile([P, n, R], BF16, name="summed", tag=hold, align_bytes=64)
+                total = keep.tile(shape, BF16, name="summed", tag=tag, align_bytes=64)
             nc.gpsimd.tensor_tensor(total[:], terms[b][0][:, parts], terms[b][1][:, parts], ADD)
             summed[b, parts.start] = total
 
-        def new_turned(b, c, n):
-            tile = keep.tile([P, n, P, PACK], BF16, name="turned", tag=f"turned{b}_{c}", align_bytes=64)
-            for i in range(n):
-                turned[b, c + i] = tile[:, i]
-            turned[b, "all"] = tile
-            return tile
+        def new_turned(b, parts):
+            turned[b, parts.start] = keep.tile([P, parts.stop - parts.start, P, PACK], BF16, name="turned",
+                                               tag=f"turned{b}_{parts.start}", align_bytes=64)
+            return turned[b, parts.start]
 
-        def turn_pairs(b, c, n, number, copy=nc.scalar.copy):
-            tile = new_turned(b, c, n)
+        def turn_pairs(b, parts, number, copy=nc.scalar.copy):
+            n = parts.stop - parts.start
+            target = new_turned(b, parts)
             acc = bank(number, [P, n, 2, P])
-            words = summed[b, c][:].rearrange("j c r -> j (c r)").bitcast(F32).rearrange(
+            words = summed[b, parts.start][:].rearrange("j c r -> j (c r)").bitcast(F32).rearrange(
                 "j (c u p) -> j c u p", c=n, u=2)
             for i in range(n):
                 for u in range(2):
                     nc.tensor.transpose(acc[:, i, u, :], words[:, i, u, :], identity[:])
             copy(
-                tile[:].rearrange("p c j t -> p (c j t)").bitcast(F32).rearrange("p (c j u) -> p c j u", c=n, u=2),
+                target[:].rearrange("p c j t -> p (c j t)").bitcast(F32).rearrange("p (c j u) -> p c j u", c=n, u=2),
                 acc[:].rearrange("p c u j -> p c j u"))
 
-        def turn_terms(b, c, number, tile):
-            acc = bank(number, [P, PACK, P])
-            for term in range(2):
-                for t in range(PACK):
-                    nc.tensor.matmul(acc[:, t, :], terms[b][term][:, c, t * P:(t + 1) * P], identity[:],
-                                     start=(term == 0 and t == 0), stop=(term == 1 and t == PACK - 1),
-                                     is_transpose=True)
-            nc.scalar.copy(tile, acc[:].rearrange("p t j -> p j t"))
+        def turn_terms(b, parts, numbers):
+            target = new_turned(b, parts)
+            for i, number in enumerate(numbers):
+                acc = bank(number, [P, PACK, P])
+                for term in range(2):
+                    for t in range(PACK):
+                        nc.tensor.matmul(acc[:, t, :], terms[b][term][:, parts.start + i, t * P:(t + 1) * P],
+                                         identity[:], start=(term == 0 and t == 0),
+                                         stop=(term == 1 and t == PACK - 1), is_transpose=True)
+                nc.scalar.copy(target[:, i], acc[:].rearrange("p t j -> p j t"))
 
-        def new_codes(blocks, hold):
-            codes = keep.tile([P, len(blocks), 2 * P], U32, name="codes", tag=hold, align_bytes=256)
-            planes = keep.tile([P, len(blocks), 2 * P], U8, name=f"planes_{hold}", align_bytes=256)
+        def new_codes(blocks, tag):
+            codes = keep.tile([P, len(blocks), 2 * P], U32, name="codes", tag=tag, align_bytes=256)
+            planes = keep.tile([P, len(blocks), 2 * P], U8, name=f"planes_{tag}", align_bytes=256)
             for i, b in enumerate(blocks):
                 quant[b] = (codes[:, i, :], planes[:, i, :])
 
-        def quantise(b, c=None):
+        def quantise(b, parts):
             codes, plane = quant[b]
-            if c is None:
-                nc.vector.quantize_mx(out=codes.bitcast(FP8X4), scales=plane,
-                                      in_=turned[b, "all"][:].rearrange("p c j t -> p (c j t)"))
-            else:
-                nc.vector.quantize_mx(out=codes[:, c * P:(c + 1) * P].bitcast(FP8X4),
-                                      scales=plane[:, c * P:(c + 1) * P],
-                                      in_=turned[b, c].rearrange("p j t -> p (j t)"))
+            cols = slice(parts.start * P, parts.stop * P)
+            nc.vector.quantize_mx(out=codes[:, cols].bitcast(FP8X4), scales=plane[:, cols],
+                                  in_=turned[b, parts.start][:].rearrange("p c j t -> p (c j t)"))
 
         def score_pass(acc, b, g, c):
             codes, plane = quant[b]
@@ -272,21 +267,9 @@ def tile_list_ckg_none_kernel(
             copy(result[:], acc[:].rearrange("n g i j -> n g (i j)"))
             nc.sync.dma_start(out[:, first * P:(first + n) * P].rearrange("(g n) j -> n g j", g=2), result[:])
 
-        def turn_both(b, numbers):
-            tile = new_turned(b, 0, 2)
-            for c in range(2):
-                turn_terms(b, c, numbers[c], tile[:, c])
-
-        both = slice(0, 2)
-        warm = bank(6, [P, R])
-        for i in range(4):
-            nc.tensor.matmul_mx(
-                out=warm[:], lhsT=wer_sb[:, 0, 0:2 * P].bitcast(FP4X4), lhsT_scale=ent_planes[:, COL_WER:COL_WER + P],
-                rhs=wer_sb[:, 0, :].bitcast(FP4X4), rhs_scale=ent_planes[:, COL_WER:COL_WER + R],
-                start=True, stop=True)
-        for b in range(4):
+        for b in range(EARLY):
             project_entity(b)
-        for b in range(4):
+        for b in range(EARLY):
             project_relation(b)
 
         arr_sb = keep.tile([P, R], F32, name="arr_sb")
@@ -294,76 +277,69 @@ def tile_list_ckg_none_kernel(
         new_terms(1)
         nc.gpsimd.tensor_tensor(terms[1][0][:], ent[1][:], arr_sb[:].unsqueeze(1).to_broadcast([P, 2, R]), MULT)
         project_entity(4)
-
         new_terms(0)
         for term in range(2):
             for c in range(2):
                 product(0, c, term)
-        combine(0, both)
+        combine(0, BOTH)
         for c in range(2):
             product(1, c, 1)
-        turn_both(1, (7, 1))
+        turn_terms(1, BOTH, (7, 1))
         project_entity(5)
 
-        multiply(2, 0)
-        multiply(2, 1)
-        combine(2, both)
-        project_relation(4)
-        turn_pairs(0, 0, 2, 7)
-        project_entity(6)
+        for b, added, number, tag in ((2, 0, 7, None), (3, 2, 1, "pause3")):
+            new_terms(b, tag)
+            multiply(b, BOTH)
+            combine(b, BOTH)
+            project_relation(b + 2)
+            turn_pairs(added, BOTH, number)
+            project_entity(b + EARLY)
 
-        multiply(3, 0, hold="pause3")
-        multiply(3, 1)
-        combine(3, both)
-        project_relation(5)
-        turn_pairs(2, 0, 2, 1)
-        project_entity(7)
-
-        multiply(4, 0)
-        multiply(4, 1)
-        turn_pairs(3, 0, 2, 7)
+        new_terms(4)
+        multiply(4, BOTH)
+        turn_pairs(3, BOTH, 7)
         project_relation(6)
-        turn_both(4, (1, 6))
+        turn_terms(4, BOTH, (1, 6))
 
-        multiply(5, 0)
+        new_terms(5)
+        multiply(5, HR)
         new_codes((0, 1, 2, 3), "pause3")
         for b in range(4):
-            quantise(b)
-        combine(5, slice(0, 1), hold="turned3_0")
-        multiply(5, 1)
-        combine(5, slice(1, 2))
+            quantise(b, BOTH)
+        combine(5, HR, tag="turned3_0")
+        multiply(5, HI)
+        combine(5, HI)
         project_relation(7)
         score(0, 2, 0)
         score(2, 2, 7)
-        turn_pairs(5, 0, 1, 1)
+        turn_pairs(5, HR, 1)
 
-        multiply(6, 0, hold="pause6")
-        combine(6, slice(0, 1))
-        multiply(6, 1)
-        combine(6, slice(1, 2))
-        turn_pairs(5, 1, 1, 6)
-        multiply(7, 0)
-        turn_pairs(6, 0, 1, 1)
-        turn_terms(7, 0, 3, new_turned(7, 0, 1)[:, 0])
-        multiply(7, 1)
-        turn_terms(7, 1, 0, new_turned(7, 1, 1)[:, 0])
+        new_terms(6, "pause6")
+        for parts in (HR, HI):
+            multiply(6, parts)
+            combine(6, parts)
+        turn_pairs(5, HI, 6)
+        new_terms(7)
+        multiply(7, HR)
+        turn_pairs(6, HR, 1)
+        turn_terms(7, HR, (3,))
+        multiply(7, HI)
+        turn_terms(7, HI, (0,))
+
         new_codes((4, 5, 6, 7), "pause6")
-        quantise(4)
-        quantise(5, 0)
-        quantise(5, 1)
-        quantise(6, 0)
-        quantise(7, 0)
-        turn_pairs(6, 1, 1, 5, nc.vector.tensor_copy)
+        for b, parts in ((4, BOTH), (5, HR), (5, HI), (6, HR), (7, HR)):
+            quantise(b, parts)
+        turn_pairs(6, HI, 5, nc.vector.tensor_copy)
         score(4, 2, 7)
-        last = [bank(number, [P, P]) for number in (2, 1)]
+        last_sums = [bank(number, [P, P]) for number in (2, 1)]
         for g in range(2):
-            score_pass(last[g][:], 7, g, 0)
-        quantise(7, 1)
-        quantise(6, 1)
-        result = keep.tile([P, 2, P], F32, name="result7")
+            score_pass(last_sums[g][:], 7, g, 0)
+        quantise(7, HI)
+        quantise(6, HI)
+        last_result = keep.tile([P, 2, P], F32, name="result7")
         for g in range(2):
-            score_pass(last[g][:], 7, g, 1)
-        nc.scalar.copy(result[:, 0], last[0][:])
-        nc.scalar.copy(result[:, 1], last[1][:])
-        nc.sync.dma_start(out[:, 7 * P:8 * P].rearrange("(g n) j -> n g j", g=2), result[:])
+            score_pass(last_sums[g][:], 7, g, 1)
+        for g in range(2):
+            nc.scalar.copy(last_result[:, g], last_sums[g][:])
+        nc.sync.dma_start(out[:, 7 * P:8 * P].rearrange("(g n) j -> n g j", g=2), last_result[:])
         score(6, 1, 6, nc.vector.tensor_copy)

@@ -28,6 +28,8 @@ ON_TENSOR = (1, 4, 7)
 HR, HI, BOTH = slice(0, 1), slice(1, 2), slice(0, 2)
 COL_WER, COL_WEI, COLS_ENT = J, J + 2 * R, J + 4 * R
 COL_WRR, COL_WRI, COLS_REL = J, J + R, J + 2 * R
+PLACE_WR, PLACE_GOT2, PLACE_GOT, PLACE_TAB2, PLACE_TAB = 0, 3 * J, 3 * J + J // 2, 4 * J, 4 * J + 4 * T
+REL_PIECES = (slice(0, 2 * P), slice(2 * P, J))
 COL_NI = PACK * N
 
 
@@ -39,65 +41,65 @@ def tile_list_ckg_none_kernel(
     with ExitStack() as ctx:
         keep = ctx.enter_context(tc.tile_pool(name="keep", bufs=1))
         ring = ctx.enter_context(tc.tile_pool(name="ring", bufs=3))
+        placed = ctx.enter_context(tc.tile_pool(name="placed", bufs=1))
         psum = ctx.enter_context(tc.psum_pool(name="psum", bufs=1))
 
         list1 = keep.tile([P, J // 16], U16, name="list1")
         list2 = keep.tile([P, J // 16], U16, name="list2")
-        zeros = keep.tile([P, J // 4], I32, name="zeros", tag="table", align_bytes=64)
+        zeros = placed.tile([P, J // 4], I32, name="zeros", offset=PLACE_TAB, align_bytes=256)
         wer_sb = keep.tile([P, 2, 2 * R], U8, name="wer_sb", align_bytes=256)
         wei_sb = keep.tile([P, 2, 2 * R], U8, name="wei_sb", align_bytes=256)
-        tab_rows = keep.tile([P, T], U8, name="tab_rows", tag="first", align_bytes=256)
-        tab2_rows = keep.tile([P, T], U8, name="tab2_rows", tag="second", align_bytes=256)
+        tab_rows = keep.tile([P, T], U8, name="tab_rows", align_bytes=256)
+        tab2_rows = keep.tile([P, T], U8, name="tab2_rows", align_bytes=256)
         ent_planes = keep.tile([P, COLS_ENT], U8, name="ent_planes", align_bytes=256)
-        ent_rows = keep.tile([P, COLS_ENT], U8, name="ent_rows", tag="staged", align_bytes=256)
+        ent_rows = keep.tile([P, COLS_ENT], U8, name="ent_rows", align_bytes=256)
         ent_plane1 = keep.tile([P, J], U8, name="ent_plane1", align_bytes=256)
-        rel_rows = keep.tile([P, COLS_REL], U8, name="rel_rows", align_bytes=256)
+        rel_planes = keep.tile([P, COLS_REL], U8, name="rel_planes", align_bytes=256)
 
         def words_view(words):
             return words.rearrange("a p n i -> p (a n i)").bitcast(I32)
 
-        def load_scale_rows(queue, rows, scales):
-            queue.dma_start(rows.bitcast(I32).rearrange("q (a n) -> q a n", a=scales.shape[0]),
-                            scales.rearrange("a q n -> q a n").bitcast(I32))
+        def load_scale_rows(rows, scales):
+            nc.sync.dma_start(rows.bitcast(I32).rearrange("q (a n) -> q a n", a=scales.shape[0]),
+                              scales.rearrange("a q n -> q a n").bitcast(I32))
 
         nc.vector.memset(tab2_rows[:].bitcast(I32), 0)
+        nc.vector.memset(rel_planes[:, J:COLS_REL].bitcast(I32), 0)
         nc.vector.memset(zeros[:], 0)
         nc.vector.tensor_copy(ent_plane1[:].bitcast(I32), zeros[:])
         nc.vector.memset(tab_rows[32:64, :].bitcast(I32), 0)
         nc.vector.memset(tab_rows[64:P, :].bitcast(I32), 0)
         nc.vector.memset(ent_planes[:].bitcast(I32), 0)
 
-        load_scale_rows(nc.gpsimd, rel_rows[0:P:8, COL_WRR:COL_WRI], wrr_scales)
-        load_scale_rows(nc.gpsimd, rel_rows[0:P:8, COL_WRI:COLS_REL], wri_scales)
         nc.sync.dma_start(list1[:], offs)
         nc.sync.dma_start(tab_rows[0:2 * ROWS, :].bitcast(I32), tab_scales.rearrange("a q t -> (a q) t").bitcast(I32))
         nc.sync.dma_start(list2[:], offs2)
         nc.sync.dma_start(wer_sb[:].bitcast(I32), wer_words.rearrange("a p n -> p a n").bitcast(I32))
         nc.sync.dma_start(wei_sb[:].bitcast(I32), wei_words.rearrange("a p n -> p a n").bitcast(I32))
-        load_scale_rows(nc.sync, ent_rows[0:ROWS, COL_WER:COL_WEI], wer_scales)
-        load_scale_rows(nc.sync, ent_rows[0:ROWS, COL_WEI:COLS_ENT], wei_scales)
+        load_scale_rows(ent_rows[0:ROWS, COL_WER:COL_WEI], wer_scales)
+        load_scale_rows(ent_rows[0:ROWS, COL_WEI:COLS_ENT], wei_scales)
         nc.sync.dma_start(tab2_rows[0:P:8, :].bitcast(I32), tab2_scales[0].bitcast(I32))
-        tab_sb = keep.tile([P, T], I32, name="tab_sb", tag="table", align_bytes=64)
+        load_scale_rows(rel_planes[0:P:8, COL_WRR:COL_WRI], wrr_scales)
+        load_scale_rows(rel_planes[0:P:8, COL_WRI:COLS_REL], wri_scales)
+        tab_sb = placed.tile([P, T], I32, name="tab_sb", offset=PLACE_TAB, align_bytes=256)
         nc.sync.dma_start(tab_sb[:], words_view(tab_words))
 
-        got_rows = keep.tile([P, J], U8, name="got_rows", align_bytes=256)
+        got_rows = placed.tile([P, J], U8, name="got_rows", offset=PLACE_GOT, align_bytes=256)
         nc.vector.tensor_copy(got_rows[:], tab_rows[:].indirect(list1[:]))
         nc.vector.tensor_copy(ent_rows[:, 0:J].bitcast(I32), got_rows[:].bitcast(I32))
         for r in range(4):
-            queue = nc.gpsimd if r < 2 else nc.sync
-            queue.dma_start(ent_plane1[r:P:QUADRANT, :].bitcast(I32), got_rows[ROWS + r:2 * ROWS:4, :].bitcast(I32))
-        for r in range(4):
             nc.sync.dma_start(ent_planes[r:P:QUADRANT, :].bitcast(I32), ent_rows[r:ROWS:4, :].bitcast(I32))
-
-        got2_rows = keep.tile([P, J], U8, name="got2_rows", tag="gathered1", align_bytes=256)
-        nc.vector.tensor_copy(got2_rows[:], tab2_rows[:].indirect(list2[:]))
-        nc.vector.tensor_copy(rel_rows[:, 0:J].bitcast(I32), got2_rows[:].bitcast(I32))
-        tab2_sb = keep.tile([P, T], I32, name="tab2_sb", tag="second", align_bytes=256)
-        nc.sync.dma_start(tab2_sb[:], words_view(tab2_words))
-        rel_planes = keep.tile([P, COLS_REL], U8, name="rel_planes", tag="first", align_bytes=256)
-        nc.vector.memset(rel_planes[:].bitcast(I32), 0)
         for r in range(4):
-            nc.sync.dma_start(rel_planes[r:P:QUADRANT, :].bitcast(I32), rel_rows[8 * r:P:QUADRANT, :].bitcast(I32))
+            nc.sync.dma_start(ent_plane1[r:P:QUADRANT, :].bitcast(I32),
+                              ent_rows[ROWS + r:2 * ROWS:4, 0:J].bitcast(I32))
+
+        tab2_sb = placed.tile([P, T], I32, name="tab2_sb", offset=PLACE_TAB2, align_bytes=256)
+        nc.sync.dma_start(tab2_sb[:], words_view(tab2_words))
+        got2_rows = placed.tile([P, J], U8, name="got2_rows", offset=PLACE_GOT2, align_bytes=256)
+        nc.vector.tensor_copy(got2_rows[:], tab2_rows[:].indirect(list2[:]))
+        nc.vector.tensor_copy(rel_planes[:, 0:J].bitcast(I32), got2_rows[:].bitcast(I32))
+        for r in range(1, 4):
+            nc.sync.dma_start(rel_planes[r:P:QUADRANT, :].bitcast(I32), rel_planes[8 * r:P:QUADRANT, :].bitcast(I32))
 
         ent_words, rel_words = [], []
         for h, pieces in enumerate(((slice(0, P), slice(P, HALF)), (slice(0, HALF),))):
@@ -111,24 +113,24 @@ def tile_list_ckg_none_kernel(
             ent_words.append(parted)
         identity = keep.tile([P, P], F32, name="identity", tag="pairs", align_bytes=256)
         make_identity(nc, identity[:])
-        wr_sb = keep.tile([P, 2, R], I32, name="wr_sb", tag="gathered1", align_bytes=256)
+        wr_sb = placed.tile([P, 2, R], I32, name="wr_sb", offset=PLACE_WR, align_bytes=256)
         nc.sync.dma_start(wr_sb[:, 0, :], words_view(wrr_words))
         nc.sync.dma_start(wr_sb[:, 1, :], words_view(wri_words))
 
-        cand_sb = keep.tile([P, COL_NI + 2 * N], U8, name="cand_sb", tag="staged", align_bytes=256)
+        cand_sb = placed.tile([P, COL_NI + 2 * N], U8, name="cand_sb", offset=PLACE_TAB, align_bytes=256)
         nc.sync.dma_start(cand_sb[:, 0:COL_NI].bitcast(I32), words_view(nr_words))
         nc.sync.dma_start(cand_sb[:, COL_NI:COL_NI + 2 * N].bitcast(I32), ni_words[0].bitcast(I32))
-        cand_planes = keep.tile([P, 2, N], U8, name="cand_planes", tag="table", align_bytes=64)
+        cand_planes = placed.tile([P, 2, N], U8, name="cand_planes", offset=PLACE_TAB + 2 * J, align_bytes=256)
         nc.vector.memset(cand_planes[:].bitcast(I32), 0)
         for c, cand_scales in enumerate((nr_scales, ni_scales)):
             for r in range(4):
                 nc.sync.dma_start(cand_planes[r:P:QUADRANT, c, :].bitcast(I32),
                                   cand_scales[0, r:ROWS:4, :].bitcast(I32))
-        for h in range(2):
-            picked = keep.tile([P, HALF], U32, name=f"picked{h}", align_bytes=256)
+        for h, piece in enumerate(REL_PIECES):
+            picked = keep.tile([P, piece.stop - piece.start], U32, name=f"picked{h}", align_bytes=256)
             nc.vector.tensor_copy(
-                picked[:], tab2_sb[:].bitcast(U32).indirect(list2[:, HALF_COLS * h:HALF_COLS * (h + 1)]))
-            rel_words.append(picked)
+                picked[:], tab2_sb[:].bitcast(U32).indirect(list2[:, piece.start // 16:piece.stop // 16]))
+            rel_words.extend(picked[:, j0:j0 + P] for j0 in range(0, piece.stop - piece.start, P))
 
         def bank(number, shape):
             return psum.tile(shape, F32, name=f"bank{number}", bufs=1)
@@ -162,12 +164,11 @@ def tile_list_ckg_none_kernel(
                 nc.scalar.copy(as_placed(ent[b][:, c], b), by_place(acc[:], b))
 
         def project_relation(b):
-            h, j0 = divmod(b * P, HALF)
             rel[b] = []
             for c, col in enumerate((COL_WRR, COL_WRI)):
                 acc = bank(early_bank(b if b < EARLY else 2 + b % 2, c), [P, R])
                 nc.tensor.matmul_mx(
-                    out=acc[:], lhsT=rel_words[h][:, j0:j0 + P].bitcast(FP8X4),
+                    out=acc[:], lhsT=rel_words[b].bitcast(FP8X4),
                     lhsT_scale=rel_planes[:, b * P:(b + 1) * P],
                     rhs=wr_sb[:, c, :].bitcast(FP8X4), rhs_scale=rel_planes[:, col:col + R], start=True, stop=True)
                 rel[b].append(by_place(acc[:], b))

@@ -24,11 +24,13 @@ ROWS = 16
 HALF = J // 2
 HALF_COLS = HALF // 16
 EARLY = 4
-ON_TENSOR = (1, 4, 7)
+ON_TENSOR = (1, 2, 6, 7)
+HOLDING = (7,)
 HR, HI, BOTH = slice(0, 1), slice(1, 2), slice(0, 2)
 COL_WER, COL_WEI, COLS_ENT = J, J + 2 * R, J + 4 * R
 COL_WRR, COL_WRI, COLS_REL = J, J + R, J + 2 * R
 PLACE_WR, PLACE_GOT2, PLACE_GOT, PLACE_TAB2, PLACE_TAB = 0, 3 * J, 3 * J + J // 2, 4 * J, 4 * J + 4 * T
+ENT_PIECES = (slice(0, 2 * P), slice(2 * P, 4 * P), slice(4 * P, J))
 REL_PIECES = (slice(0, 2 * P), slice(2 * P, J))
 COL_NI = PACK * N
 
@@ -88,11 +90,10 @@ def tile_list_ckg_none_kernel(
         nc.vector.tensor_copy(got_rows[:], tab_rows[:].indirect(list1[:]))
         nc.vector.tensor_copy(ent_rows[:, 0:J].bitcast(I32), got_rows[:].bitcast(I32))
         for r in range(4):
-            nc.sync.dma_start(ent_planes[r:P:QUADRANT, :].bitcast(I32), ent_rows[r:ROWS:4, :].bitcast(I32))
-        for r in range(4):
             nc.sync.dma_start(ent_plane1[r:P:QUADRANT, :].bitcast(I32),
                               ent_rows[ROWS + r:2 * ROWS:4, 0:J].bitcast(I32))
-
+        for r in range(4):
+            nc.sync.dma_start(ent_planes[r:P:QUADRANT, :].bitcast(I32), ent_rows[r:ROWS:4, :].bitcast(I32))
         tab2_sb = placed.tile([P, T], I32, name="tab2_sb", offset=PLACE_TAB2, align_bytes=256)
         nc.sync.dma_start(tab2_sb[:], words_view(tab2_words))
         got2_rows = placed.tile([P, J], U8, name="got2_rows", offset=PLACE_GOT2, align_bytes=256)
@@ -102,15 +103,14 @@ def tile_list_ckg_none_kernel(
             nc.sync.dma_start(rel_planes[r:P:QUADRANT, :].bitcast(I32), rel_planes[8 * r:P:QUADRANT, :].bitcast(I32))
 
         ent_words, rel_words = [], []
-        for h, pieces in enumerate(((slice(0, P), slice(P, HALF)), (slice(0, HALF),))):
-            pairs = keep.tile([P, HALF], U32, name=f"pairs{h}", tag="pairs", align_bytes=256)
+        for h, piece in enumerate(ENT_PIECES):
+            n = piece.stop - piece.start
+            pairs = keep.tile([P, n], U32, name=f"pairs{h}", tag="pairs", align_bytes=256)
             nc.vector.tensor_copy(
-                pairs[:], tab_sb[:].bitcast(U32).indirect(list1[:, HALF_COLS * h:HALF_COLS * (h + 1)]))
-            parted = keep.tile([P, 2, HALF], U16, name=f"parted{h}", align_bytes=256)
-            by_pass = pairs[:].bitcast(U16).rearrange("p (j d) -> p d j", d=2)
-            for piece in pieces:
-                nc.vector.tensor_copy(parted[:, :, piece], by_pass[:, :, piece])
-            ent_words.append(parted)
+                pairs[:], tab_sb[:].bitcast(U32).indirect(list1[:, piece.start // 16:piece.stop // 16]))
+            parted = keep.tile([P, 2, n], U16, name=f"parted{h}", align_bytes=256)
+            nc.vector.tensor_copy(parted[:], pairs[:].bitcast(U16).rearrange("p (j d) -> p d j", d=2))
+            ent_words.extend(parted[:, :, j0:j0 + P] for j0 in range(0, n, P))
         identity = keep.tile([P, P], F32, name="identity", tag="pairs", align_bytes=256)
         make_identity(nc, identity[:])
         wr_sb = placed.tile([P, 2, R], I32, name="wr_sb", offset=PLACE_WR, align_bytes=256)
@@ -135,9 +135,6 @@ def tile_list_ckg_none_kernel(
         def bank(number, shape):
             return psum.tile(shape, F32, name=f"bank{number}", bufs=1)
 
-        def early_bank(b, c):
-            return (2 * b + 6) % 8 + c
-
         def by_place(view, b):
             if b in ON_TENSOR:
                 return view.rearrange("j (m t) -> j t m", t=PACK)
@@ -148,42 +145,60 @@ def tile_list_ckg_none_kernel(
                 return view.rearrange("j (t m) -> j t m", t=PACK)
             return view.rearrange("j (u m e) -> j u m e", u=2, e=2)
 
+        ent_parts, term_parts = {}, {}
         ent, rel, terms, summed, turned, quant = {}, {}, {}, {}, {}, {}
 
-        def project_entity(b):
-            h, j0 = divmod(b * P, HALF)
-            ent[b] = ring.tile([P, 2, R], F32, name="ent", bufs=EARLY + 1)
-            for c, (w_sb, col) in enumerate(((wer_sb, COL_WER), (wei_sb, COL_WEI))):
-                acc = bank(early_bank(b, c) if b < EARLY else (0, 6)[c], [P, R])
+        def project_entity(b, numbers, parts=BOTH):
+            if b not in ent:
+                ent[b] = keep.tile([P, 2, R], F32, name=f"ent{b}")
+                ent_parts[b] = [ent[b][:, c] for c in range(2)]
+                if b in HOLDING:
+                    aei = keep.tile([P, R], F32, name="aei", tag=f"aei{b}", align_bytes=256)
+                    ent_parts[b][1] = aei[:]
+            for c, number in zip(range(parts.start, parts.stop), numbers):
+                w_sb, col = ((wer_sb, COL_WER), (wei_sb, COL_WEI))[c]
+                acc = bank(number, [P, R])
                 for a in range(2):
                     plane = (ent_planes, ent_plane1)[a][:, b * P:(b + 1) * P]
                     nc.tensor.matmul_mx(
-                        out=acc[:], lhsT=ent_words[h][:, a, j0:j0 + P].bitcast(FP4X4), lhsT_scale=plane,
+                        out=acc[:], lhsT=ent_words[b][:, a].bitcast(FP4X4), lhsT_scale=plane,
                         rhs=w_sb[:, a, :].bitcast(FP4X4), rhs_scale=ent_planes[:, col + a * R:col + (a + 1) * R],
                         start=(a == 0), stop=(a == 1))
-                nc.scalar.copy(as_placed(ent[b][:, c], b), by_place(acc[:], b))
+                nc.scalar.copy(as_placed(ent_parts[b][c], b), by_place(acc[:], b))
 
-        def project_relation(b):
+        def project_relation(b, numbers):
             rel[b] = []
             for c, col in enumerate((COL_WRR, COL_WRI)):
-                acc = bank(early_bank(b if b < EARLY else 2 + b % 2, c), [P, R])
+                acc = bank(numbers[c], [P, R])
                 nc.tensor.matmul_mx(
                     out=acc[:], lhsT=rel_words[b].bitcast(FP8X4),
                     lhsT_scale=rel_planes[:, b * P:(b + 1) * P],
                     rhs=wr_sb[:, c, :].bitcast(FP8X4), rhs_scale=rel_planes[:, col:col + R], start=True, stop=True)
                 rel[b].append(by_place(acc[:], b))
 
-        def new_terms(b, tag=None):
-            with_arr = ring.tile([P, 2, R], F32, name="with_arr")
-            if tag is None:
-                with_ari = ring.tile([P, 2, R], F32, name="with_ari")
-            else:
-                with_ari = keep.tile([P, 2, R], F32, name="with_ari", tag=tag, align_bytes=256)
+        def products_on_gpsimd(b):
+            arr_sb = keep.tile([P, R], F32, name=f"arr_sb{b}")
+            nc.scalar.copy(as_placed(arr_sb[:], b), rel[b][0])
+            new_terms(b)
+            nc.gpsimd.tensor_tensor(terms[b][0][:], ent[b][:], arr_sb[:].unsqueeze(1).to_broadcast([P, 2, R]), MULT)
+
+        def arr_first(b):
+            for term in range(2):
+                for c in range(2):
+                    product(b, c, term)
+
+        def new_terms(b, tag=None, last_tag=None):
+            with_arr = keep.tile([P, 2, R], F32, name=f"with_arr{b}")
+            with_ari = keep.tile([P, 2, R], F32, name="with_ari", tag=tag or f"with_ari{b}", align_bytes=256)
             terms[b] = (with_arr, with_ari)
+            term_parts[b] = [[tile[:, c] for c in range(2)] for tile in terms[b]]
+            if last_tag is not None:
+                last_term = keep.tile([P, R], F32, name="last_term", tag=last_tag, align_bytes=256)
+                term_parts[b][1][1] = last_term[:]
 
         def product(b, c, term):
-            target = as_placed(terms[b][term][:, c], b)
-            factor = as_placed(ent[b][:, (c + term) % 2], b)
+            target = as_placed(term_parts[b][term][c], b)
+            factor = as_placed(ent_parts[b][(c + term) % 2], b)
             if (c, term) != (0, 1):
                 nc.vector.tensor_tensor(target, factor, rel[b][term], MULT)
             elif b in ON_TENSOR:
@@ -202,13 +217,13 @@ def tile_list_ckg_none_kernel(
             if tag is None:
                 total = ring.tile(shape, BF16, name="summed", align_bytes=64)
             else:
-                total = keep.tile(shape, BF16, name="summed", tag=tag, align_bytes=64)
+                total = keep.tile(shape, BF16, name="summed", tag=tag, align_bytes=256)
             nc.gpsimd.tensor_tensor(total[:], terms[b][0][:, parts], terms[b][1][:, parts], ADD)
             summed[b, parts.start] = total
 
         def new_turned(b, parts):
             turned[b, parts.start] = keep.tile([P, parts.stop - parts.start, P, PACK], BF16, name="turned",
-                                               tag=f"turned{b}_{parts.start}", align_bytes=64)
+                                               tag=f"turned{b}_{parts.start}", align_bytes=256)
             return turned[b, parts.start]
 
         def turn_pairs(b, parts, number, copy=nc.scalar.copy):
@@ -224,20 +239,22 @@ def tile_list_ckg_none_kernel(
                 target[:].rearrange("p c j t -> p (c j t)").bitcast(F32).rearrange("p (c j u) -> p c j u", c=n, u=2),
                 acc[:].rearrange("p c u j -> p c j u"))
 
-        def turn_terms(b, parts, numbers):
+        def turn_term(acc, b, c, term, first):
+            for t in range(PACK):
+                nc.tensor.matmul(acc[:, t, :], term_parts[b][term][c][:, t * P:(t + 1) * P], identity[:],
+                                 start=(first and t == 0), stop=(not first and t == PACK - 1), is_transpose=True)
+
+        def turn_terms(b, parts, numbers, order=(1, 0)):
             target = new_turned(b, parts)
             for i, number in enumerate(numbers):
                 acc = bank(number, [P, PACK, P])
-                for term in range(2):
-                    for t in range(PACK):
-                        nc.tensor.matmul(acc[:, t, :], terms[b][term][:, parts.start + i, t * P:(t + 1) * P],
-                                         identity[:], start=(term == 0 and t == 0),
-                                         stop=(term == 1 and t == PACK - 1), is_transpose=True)
+                for term in order:
+                    turn_term(acc, b, parts.start + i, term, term == order[0])
                 nc.scalar.copy(target[:, i], acc[:].rearrange("p t j -> p j t"))
 
-        def new_codes(blocks, tag):
+        def new_codes(blocks, tag, planes_tag):
             codes = keep.tile([P, len(blocks), 2 * P], U32, name="codes", tag=tag, align_bytes=256)
-            planes = keep.tile([P, len(blocks), 2 * P], U8, name=f"planes_{tag}", align_bytes=256)
+            planes = keep.tile([P, len(blocks), 2 * P], U8, name="planes", tag=planes_tag, align_bytes=256)
             for i, b in enumerate(blocks):
                 quant[b] = (codes[:, i, :], planes[:, i, :])
 
@@ -268,79 +285,72 @@ def tile_list_ckg_none_kernel(
             copy(result[:], acc[:].rearrange("n g i j -> n g (i j)"))
             nc.sync.dma_start(out[:, first * P:(first + n) * P].rearrange("(g n) j -> n g j", g=2), result[:])
 
+        EARLY_BANKS = ((6, 7), (0, 1), (2, 3), (4, 5))
         for b in range(EARLY):
-            project_entity(b)
+            project_entity(b, EARLY_BANKS[b])
         for b in range(EARLY):
-            project_relation(b)
-
-        arr_sb = keep.tile([P, R], F32, name="arr_sb")
-        nc.scalar.copy(as_placed(arr_sb[:], 1), rel[1][0])
-        new_terms(1)
-        nc.gpsimd.tensor_tensor(terms[1][0][:], ent[1][:], arr_sb[:].unsqueeze(1).to_broadcast([P, 2, R]), MULT)
-        project_entity(4)
+            project_relation(b, EARLY_BANKS[b])
+        products_on_gpsimd(1)
+        products_on_gpsimd(2)
+        project_entity(4, (0, 2))
         new_terms(0)
-        for term in range(2):
-            for c in range(2):
-                product(0, c, term)
+        arr_first(0)
         combine(0, BOTH)
-        for c in range(2):
-            product(1, c, 1)
-        turn_terms(1, BOTH, (7, 1))
-        project_entity(5)
-
-        for b, added, number, tag in ((2, 0, 7, None), (3, 2, 1, "pause3")):
-            new_terms(b, tag)
-            multiply(b, BOTH)
-            combine(b, BOTH)
-            project_relation(b + 2)
-            turn_pairs(added, BOTH, number)
-            project_entity(b + EARLY)
-
+        for b in (1, 2):
+            for c in range(2):
+                product(b, c, 1)
+        turn_terms(1, BOTH, (6, 7), (0, 1))
+        project_relation(4, (1, 3))
+        project_entity(5, (0, 2))
+        new_terms(3)
+        arr_first(3)
+        combine(3, BOTH)
+        turn_terms(2, BOTH, (6, 7), (0, 1))
+        project_relation(5, (4, 5))
+        project_entity(6, (0, 2))
         new_terms(4)
-        multiply(4, BOTH)
+        arr_first(4)
+        combine(4, BOTH)
+        turn_pairs(0, BOTH, 6)
+        project_relation(6, (1, 3))
+        new_terms(5, "last_add")
+        arr_first(5)
+        combine(5, BOTH)
+        project_entity(7, (0, 2))
+        project_relation(7, (4, 5))
         turn_pairs(3, BOTH, 7)
-        project_relation(6)
-        turn_terms(4, BOTH, (1, 6))
-
-        new_terms(5)
-        multiply(5, HR)
-        new_codes((0, 1, 2, 3), "pause3")
-        for b in range(4):
+        new_terms(6)
+        multiply(6, BOTH)
+        turn_terms(6, BOTH, (6, 0))
+        turn_pairs(4, BOTH, 2)
+        new_terms(7, None, "turned1_0")
+        for c, term in ((0, 1), (1, 0), (0, 0)):
+            product(7, c, term)
+        turn_terms(7, HR, (7,), (1, 0))
+        last_turn = bank(6, [P, PACK, P])
+        turn_term(last_turn, 7, 1, 0, True)
+        new_codes((0, 1, 2), "last_add", "aei7")
+        for b in (1, 2, 0):
             quantise(b, BOTH)
-        combine(5, HR, tag="turned3_0")
-        multiply(5, HI)
-        combine(5, HI)
-        project_relation(7)
-        score(0, 2, 0)
-        score(2, 2, 7)
-        turn_pairs(5, HR, 1)
+        turn_pairs(5, BOTH, 1)
+        product(7, 1, 1)
+        score(0, 2, 3)
+        turn_term(last_turn, 7, 1, 1, False)
+        nc.scalar.copy(new_turned(7, HI)[:, 0], last_turn[:].rearrange("p t j -> p j t"))
+        score(2, 1, 0, nc.vector.tensor_copy)
 
-        new_terms(6, "pause6")
-        for parts in (HR, HI):
-            multiply(6, parts)
-            combine(6, parts)
-        turn_pairs(5, HI, 6)
-        new_terms(7)
-        multiply(7, HR)
-        turn_pairs(6, HR, 1)
-        turn_terms(7, HR, (3,))
-        multiply(7, HI)
-        turn_terms(7, HI, (0,))
-
-        new_codes((4, 5, 6, 7), "pause6")
-        for b, parts in ((4, BOTH), (5, HR), (5, HI), (6, HR), (7, HR)):
+        new_codes((3, 4, 5, 6, 7), "turned2_0", "planes2")
+        for b, parts in ((3, BOTH), (4, BOTH), (6, BOTH), (5, BOTH), (7, HR)):
             quantise(b, parts)
-        turn_pairs(6, HI, 5, nc.vector.tensor_copy)
-        score(4, 2, 7)
-        last_sums = [bank(number, [P, P]) for number in (2, 1)]
+        score(3, 2, 2)
+        score(5, 2, 4, nc.vector.tensor_copy)
+        last_sums = [bank(number, [P, P]) for number in (5, 1)]
         for g in range(2):
             score_pass(last_sums[g][:], 7, g, 0)
         quantise(7, HI)
-        quantise(6, HI)
         last_result = keep.tile([P, 2, P], F32, name="result7")
         for g in range(2):
             score_pass(last_sums[g][:], 7, g, 1)
-        for g in range(2):
-            nc.scalar.copy(last_result[:, g], last_sums[g][:])
+        for g, copy in enumerate((nc.scalar.copy, nc.vector.tensor_copy)):
+            copy(last_result[:, g], last_sums[g][:])
         nc.sync.dma_start(out[:, 7 * P:8 * P].rearrange("(g n) j -> n g j", g=2), last_result[:])
-        score(6, 1, 6, nc.vector.tensor_copy)

@@ -25,11 +25,16 @@ HALF = J // 2
 HALF_COLS = HALF // 16
 EARLY = 4
 ON_TENSOR = (1, 2, 6, 7)
-HOLDING = (7,)
+HOLDING = (6, 7)
 HR, HI, BOTH = slice(0, 1), slice(1, 2), slice(0, 2)
 COL_WER, COL_WEI, COLS_ENT = J, J + 2 * R, J + 4 * R
 COL_WRR, COL_WRI, COLS_REL = J, J + R, J + 2 * R
-PLACE_WR, PLACE_GOT2, PLACE_GOT, PLACE_TAB2, PLACE_TAB = 0, 3 * J, 3 * J + J // 2, 4 * J, 4 * J + 4 * T
+PLACE_GOT2, PLACE_GOT, PLACE_WEI, PLACE_TAB2 = 0, 256, 512, 3 * J
+PLACE_WER = PLACE_TAB2 + 4 * T
+PLACE_ZEROS, PLACE_TAB = PLACE_WER + 3 * J // 2, PLACE_WER + 2 * J
+PLACE_LAST_PAIRS = PLACE_TAB + 4 * T
+PLACE_PAIRS = PLACE_LAST_PAIRS + 2 * J
+PLACE_GOT2_LATE, PLACE_WR = PLACE_PAIRS + 768, PLACE_PAIRS + J
 ENT_PIECES = (slice(0, 2 * P), slice(2 * P, 4 * P), slice(4 * P, J))
 REL_PIECES = (slice(0, 2 * P), slice(2 * P, J))
 COL_NI = PACK * N
@@ -48,9 +53,7 @@ def tile_list_ckg_none_kernel(
 
         list1 = keep.tile([P, J // 16], U16, name="list1")
         list2 = keep.tile([P, J // 16], U16, name="list2")
-        zeros = placed.tile([P, J // 4], I32, name="zeros", offset=PLACE_TAB, align_bytes=256)
-        wer_sb = keep.tile([P, 2, 2 * R], U8, name="wer_sb", align_bytes=256)
-        wei_sb = keep.tile([P, 2, 2 * R], U8, name="wei_sb", align_bytes=256)
+        zeros = placed.tile([P, J // 4], I32, name="zeros", offset=PLACE_ZEROS, align_bytes=256)
         tab_rows = keep.tile([P, T], U8, name="tab_rows", align_bytes=256)
         tab2_rows = keep.tile([P, T], U8, name="tab2_rows", align_bytes=256)
         ent_planes = keep.tile([P, COLS_ENT], U8, name="ent_planes", align_bytes=256)
@@ -65,9 +68,9 @@ def tile_list_ckg_none_kernel(
             nc.sync.dma_start(rows.bitcast(I32).rearrange("q (a n) -> q a n", a=scales.shape[0]),
                               scales.rearrange("a q n -> q a n").bitcast(I32))
 
+        nc.vector.memset(zeros[:], 0)
         nc.vector.memset(tab2_rows[:].bitcast(I32), 0)
         nc.vector.memset(rel_planes[:, J:COLS_REL].bitcast(I32), 0)
-        nc.vector.memset(zeros[:], 0)
         nc.vector.tensor_copy(ent_plane1[:].bitcast(I32), zeros[:])
         nc.vector.memset(tab_rows[32:64, :].bitcast(I32), 0)
         nc.vector.memset(tab_rows[64:P, :].bitcast(I32), 0)
@@ -76,8 +79,6 @@ def tile_list_ckg_none_kernel(
         nc.sync.dma_start(list1[:], offs)
         nc.sync.dma_start(tab_rows[0:2 * ROWS, :].bitcast(I32), tab_scales.rearrange("a q t -> (a q) t").bitcast(I32))
         nc.sync.dma_start(list2[:], offs2)
-        nc.sync.dma_start(wer_sb[:].bitcast(I32), wer_words.rearrange("a p n -> p a n").bitcast(I32))
-        nc.sync.dma_start(wei_sb[:].bitcast(I32), wei_words.rearrange("a p n -> p a n").bitcast(I32))
         load_scale_rows(ent_rows[0:ROWS, COL_WER:COL_WEI], wer_scales)
         load_scale_rows(ent_rows[0:ROWS, COL_WEI:COLS_ENT], wei_scales)
         nc.sync.dma_start(tab2_rows[0:P:8, :].bitcast(I32), tab2_scales[0].bitcast(I32))
@@ -85,39 +86,52 @@ def tile_list_ckg_none_kernel(
         load_scale_rows(rel_planes[0:P:8, COL_WRI:COLS_REL], wri_scales)
         tab_sb = placed.tile([P, T], I32, name="tab_sb", offset=PLACE_TAB, align_bytes=256)
         nc.sync.dma_start(tab_sb[:], words_view(tab_words))
+        wer_sb = placed.tile([P, 2, 2 * R], U8, name="wer_sb", offset=PLACE_WER, align_bytes=256)
+        nc.sync.dma_start(wer_sb[:].bitcast(I32), wer_words.rearrange("a p n -> p a n").bitcast(I32))
 
-        got_rows = placed.tile([P, J], U8, name="got_rows", offset=PLACE_GOT, align_bytes=256)
-        nc.vector.tensor_copy(got_rows[:], tab_rows[:].indirect(list1[:]))
-        nc.vector.tensor_copy(ent_rows[:, 0:J].bitcast(I32), got_rows[:].bitcast(I32))
+        got_rows = placed.tile([P, 3 * J], U8, name="got_rows", offset=PLACE_GOT, align_bytes=256)
+        nc.vector.tensor_copy(got_rows[:, 0:J], tab_rows[:].indirect(list1[:]))
+        nc.vector.tensor_copy(ent_rows[:, 0:J].bitcast(I32), got_rows[:, 0:J].bitcast(I32))
         for r in range(4):
             nc.sync.dma_start(ent_plane1[r:P:QUADRANT, :].bitcast(I32),
                               ent_rows[ROWS + r:2 * ROWS:4, 0:J].bitcast(I32))
+        wei_sb = placed.tile([P, 2, 2 * R], U8, name="wei_sb", offset=PLACE_WEI, align_bytes=256)
         for r in range(4):
+            if r == 2:
+                nc.sync.dma_start(wei_sb[:].bitcast(I32), wei_words.rearrange("a p n -> p a n").bitcast(I32))
             nc.sync.dma_start(ent_planes[r:P:QUADRANT, :].bitcast(I32), ent_rows[r:ROWS:4, :].bitcast(I32))
         tab2_sb = placed.tile([P, T], I32, name="tab2_sb", offset=PLACE_TAB2, align_bytes=256)
         nc.sync.dma_start(tab2_sb[:], words_view(tab2_words))
-        got2_rows = placed.tile([P, J], U8, name="got2_rows", offset=PLACE_GOT2, align_bytes=256)
-        nc.vector.tensor_copy(got2_rows[:], tab2_rows[:].indirect(list2[:]))
-        nc.vector.tensor_copy(rel_planes[:, 0:J].bitcast(I32), got2_rows[:].bitcast(I32))
-        for r in range(1, 4):
-            nc.sync.dma_start(rel_planes[r:P:QUADRANT, :].bitcast(I32), rel_planes[8 * r:P:QUADRANT, :].bitcast(I32))
+
+        def gather_rel_rows(h, place):
+            got2_rows = placed.tile([P, HALF], U8, name=f"got2_rows{h}", offset=place, align_bytes=256)
+            nc.vector.tensor_copy(got2_rows[:], tab2_rows[:].indirect(list2[:, HALF_COLS * h:HALF_COLS * (h + 1)]))
+            nc.vector.tensor_copy(rel_planes[:, HALF * h:HALF * (h + 1)].bitcast(I32), got2_rows[:].bitcast(I32))
+
+        gather_rel_rows(0, PLACE_GOT2)
 
         ent_words, rel_words = [], []
         for h, piece in enumerate(ENT_PIECES):
             n = piece.stop - piece.start
-            pairs = keep.tile([P, n], U32, name=f"pairs{h}", tag="pairs", align_bytes=256)
+            if h == 2:
+                gather_rel_rows(1, PLACE_GOT2_LATE)
+                for r in range(1, 4):
+                    nc.sync.dma_start(rel_planes[r:P:QUADRANT, :].bitcast(I32),
+                                      rel_planes[8 * r:P:QUADRANT, :].bitcast(I32))
+            pairs = placed.tile([P, n], U32, name=f"pairs{h}", offset=PLACE_LAST_PAIRS if h else PLACE_PAIRS,
+                                align_bytes=256)
             nc.vector.tensor_copy(
                 pairs[:], tab_sb[:].bitcast(U32).indirect(list1[:, piece.start // 16:piece.stop // 16]))
             parted = keep.tile([P, 2, n], U16, name=f"parted{h}", align_bytes=256)
             nc.vector.tensor_copy(parted[:], pairs[:].bitcast(U16).rearrange("p (j d) -> p d j", d=2))
             ent_words.extend(parted[:, :, j0:j0 + P] for j0 in range(0, n, P))
-        identity = keep.tile([P, P], F32, name="identity", tag="pairs", align_bytes=256)
+        identity = placed.tile([P, P], F32, name="identity", offset=PLACE_LAST_PAIRS + J, align_bytes=256)
         make_identity(nc, identity[:])
         wr_sb = placed.tile([P, 2, R], I32, name="wr_sb", offset=PLACE_WR, align_bytes=256)
         nc.sync.dma_start(wr_sb[:, 0, :], words_view(wrr_words))
         nc.sync.dma_start(wr_sb[:, 1, :], words_view(wri_words))
 
-        cand_sb = placed.tile([P, COL_NI + 2 * N], U8, name="cand_sb", offset=PLACE_TAB, align_bytes=256)
+        cand_sb = placed.tile([P, COL_NI + 2 * N], U8, name="cand_sb", offset=PLACE_LAST_PAIRS - J // 2, align_bytes=256)
         nc.sync.dma_start(cand_sb[:, 0:COL_NI].bitcast(I32), words_view(nr_words))
         nc.sync.dma_start(cand_sb[:, COL_NI:COL_NI + 2 * N].bitcast(I32), ni_words[0].bitcast(I32))
         cand_planes = placed.tile([P, 2, N], U8, name="cand_planes", offset=PLACE_TAB + 2 * J, align_bytes=256)
@@ -166,15 +180,15 @@ def tile_list_ckg_none_kernel(
                         start=(a == 0), stop=(a == 1))
                 nc.scalar.copy(as_placed(ent_parts[b][c], b), by_place(acc[:], b))
 
-        def project_relation(b, numbers):
-            rel[b] = []
-            for c, col in enumerate((COL_WRR, COL_WRI)):
+        def project_relation(b, numbers, parts=BOTH):
+            for c in range(parts.start, parts.stop):
+                col = (COL_WRR, COL_WRI)[c]
                 acc = bank(numbers[c], [P, R])
                 nc.tensor.matmul_mx(
                     out=acc[:], lhsT=rel_words[b].bitcast(FP8X4),
                     lhsT_scale=rel_planes[:, b * P:(b + 1) * P],
                     rhs=wr_sb[:, c, :].bitcast(FP8X4), rhs_scale=rel_planes[:, col:col + R], start=True, stop=True)
-                rel[b].append(by_place(acc[:], b))
+                rel.setdefault(b, []).append(by_place(acc[:], b))
 
         def products_on_gpsimd(b):
             arr_sb = keep.tile([P, R], F32, name=f"arr_sb{b}")
@@ -187,8 +201,8 @@ def tile_list_ckg_none_kernel(
                 for c in range(2):
                     product(b, c, term)
 
-        def new_terms(b, tag=None, last_tag=None):
-            with_arr = keep.tile([P, 2, R], F32, name=f"with_arr{b}")
+        def new_terms(b, tag=None, last_tag=None, arr_tag=None):
+            with_arr = keep.tile([P, 2, R], F32, name="with_arr", tag=arr_tag or f"with_arr{b}", align_bytes=256)
             with_ari = keep.tile([P, 2, R], F32, name="with_ari", tag=tag or f"with_ari{b}", align_bytes=256)
             terms[b] = (with_arr, with_ari)
             term_parts[b] = [[tile[:, c] for c in range(2)] for tile in terms[b]]
@@ -253,104 +267,115 @@ def tile_list_ckg_none_kernel(
                 nc.scalar.copy(target[:, i], acc[:].rearrange("p t j -> p j t"))
 
         def new_codes(blocks, tag, planes_tag):
-            codes = keep.tile([P, len(blocks), 2 * P], U32, name="codes", tag=tag, align_bytes=256)
-            planes = keep.tile([P, len(blocks), 2 * P], U8, name="planes", tag=planes_tag, align_bytes=256)
+            codes = keep.tile([P, 2, len(blocks) * P], U32, name="codes", tag=tag, align_bytes=256)
+            planes = keep.tile([P, 2, len(blocks) * P], U8, name="planes", tag=planes_tag, align_bytes=256)
             for i, b in enumerate(blocks):
-                quant[b] = (codes[:, i, :], planes[:, i, :])
+                quant[b] = (codes, planes, i * P)
 
         def quantise(b, parts):
-            codes, plane = quant[b]
-            cols = slice(parts.start * P, parts.stop * P)
-            nc.vector.quantize_mx(out=codes[:, cols].bitcast(FP8X4), scales=plane[:, cols],
-                                  in_=turned[b, parts.start][:].rearrange("p c j t -> p (c j t)"))
+            codes, planes, j0 = quant[b]
+            for c in range(parts.start, parts.stop):
+                nc.vector.quantize_mx(out=codes[:, c, j0:j0 + P].bitcast(FP8X4), scales=planes[:, c, j0:j0 + P],
+                                      in_=turned[b, parts.start][:, c - parts.start].rearrange("p j t -> p (j t)"))
 
-        def score_pass(acc, b, g, c):
-            codes, plane = quant[b]
+        def score_pass(acc, b, n, g, c):
+            codes, planes, j0 = quant[b]
             if c == 0:
                 words = cand_sb[:, PACK * P * g:PACK * P * (g + 1)].bitcast(FP8X4)
             else:
                 words = cand_sb[:, COL_NI + 2 * P * g:COL_NI + 2 * P * (g + 1)].bitcast(FP4X4)
             nc.tensor.matmul_mx(
                 out=acc, lhsT=words, lhsT_scale=cand_planes[:, c, g * P:(g + 1) * P],
-                rhs=codes[:, c * P:(c + 1) * P].bitcast(FP8X4), rhs_scale=plane[:, c * P:(c + 1) * P],
+                rhs=codes[:, c, j0:j0 + n * P].bitcast(FP8X4), rhs_scale=planes[:, c, j0:j0 + n * P],
                 start=(c == 0), stop=(c == 1))
 
         def score(first, n, number, copy=nc.scalar.copy):
-            acc = bank(number, [P, 2, n, P])
-            for i in range(n):
-                for g in range(2):
-                    for c in range(2):
-                        score_pass(acc[:, g, i, :], first + i, g, c)
+            acc = bank(number, [P, 2, n * P])
+            for g in range(2):
+                for c in range(2):
+                    score_pass(acc[:, g, :], first, n, g, c)
             result = keep.tile([P, 2, n * P], F32, name=f"result{first}")
-            copy(result[:], acc[:].rearrange("n g i j -> n g (i j)"))
+            copy(result[:], acc[:])
             nc.sync.dma_start(out[:, first * P:(first + n) * P].rearrange("(g n) j -> n g j", g=2), result[:])
 
-        EARLY_BANKS = ((6, 7), (0, 1), (2, 3), (4, 5))
-        for b in range(EARLY):
-            project_entity(b, EARLY_BANKS[b])
-        for b in range(EARLY):
-            project_relation(b, EARLY_BANKS[b])
+        ENT_BANKS = ((4, 5), (7, 2), (0, 1), (6, 3), (4, 5))
+        REL_BANKS = ((7, 2), (0, 1), (6, 3), (4, 5))
+        for b in range(5):
+            project_entity(b, ENT_BANKS[b])
+        for parts in (HR, HI):
+            for b in (0, 1):
+                project_relation(b, REL_BANKS[b], parts)
+        for b in (2, 3):
+            project_relation(b, REL_BANKS[b])
         products_on_gpsimd(1)
         products_on_gpsimd(2)
-        project_entity(4, (0, 2))
+        project_entity(5, (0, 6))
         new_terms(0)
         arr_first(0)
         combine(0, BOTH)
         for b in (1, 2):
             for c in range(2):
                 product(b, c, 1)
-        turn_terms(1, BOTH, (6, 7), (0, 1))
+        turn_terms(1, HR, (7,), (0, 1))
         project_relation(4, (1, 3))
-        project_entity(5, (0, 2))
+        turn_terms(1, HI, (2,), (0, 1))
+        project_entity(6, (7,), HR)
         new_terms(3)
         arr_first(3)
         combine(3, BOTH)
-        turn_terms(2, BOTH, (6, 7), (0, 1))
+        turn_terms(2, BOTH, (0, 6), (0, 1))
         project_relation(5, (4, 5))
-        project_entity(6, (0, 2))
-        new_terms(4)
+        project_entity(6, (0,), HI)
+        new_terms(4, "pause")
         arr_first(4)
         combine(4, BOTH)
-        turn_pairs(0, BOTH, 6)
+        turn_pairs(0, BOTH, 2)
         project_relation(6, (1, 3))
+        project_entity(7, (6,), HR)
         new_terms(5, "last_add")
         arr_first(5)
-        combine(5, BOTH)
-        project_entity(7, (0, 2))
-        project_relation(7, (4, 5))
         turn_pairs(3, BOTH, 7)
-        new_terms(6)
-        multiply(6, BOTH)
-        turn_terms(6, BOTH, (6, 0))
-        turn_pairs(4, BOTH, 2)
-        new_terms(7, None, "turned1_0")
+        project_entity(7, (2,), HI)
+        project_relation(7, (4, 5))
+        new_terms(6, None, "turned0_0")
         for c, term in ((0, 1), (1, 0), (0, 0)):
-            product(7, c, term)
-        turn_terms(7, HR, (7,), (1, 0))
-        last_turn = bank(6, [P, PACK, P])
-        turn_term(last_turn, 7, 1, 0, True)
-        new_codes((0, 1, 2), "last_add", "aei7")
-        for b in (1, 2, 0):
-            quantise(b, BOTH)
-        turn_pairs(5, BOTH, 1)
-        product(7, 1, 1)
-        score(0, 2, 3)
-        turn_term(last_turn, 7, 1, 1, False)
-        nc.scalar.copy(new_turned(7, HI)[:, 0], last_turn[:].rearrange("p t j -> p j t"))
-        score(2, 1, 0, nc.vector.tensor_copy)
-
-        new_codes((3, 4, 5, 6, 7), "turned2_0", "planes2")
-        for b, parts in ((3, BOTH), (4, BOTH), (6, BOTH), (5, BOTH), (7, HR)):
+            product(6, c, term)
+        turn_terms(6, HR, (0,), (1, 0))
+        turn_pairs(4, BOTH, 6)
+        new_codes((0, 1, 2, 3), "pause", "aei6")
+        for b, parts in ((0, BOTH), (1, HR), (1, HI), (2, BOTH), (3, BOTH)):
             quantise(b, parts)
-        score(3, 2, 2)
-        score(5, 2, 4, nc.vector.tensor_copy)
-        last_sums = [bank(number, [P, P]) for number in (5, 1)]
+        combine(5, BOTH, tag="turned3_0")
+        product(6, 1, 1)
+        score(0, 2, 1)
+        turn_terms(6, HI, (7,), (0, 1))
+        score(2, 2, 3)
+        new_terms(7, "turned2_0", None, "turned1_0")
+        arr_first(7)
+        last_turns = [bank(number, [P, PACK, P]) for number in (2, 0)]
+        for c in range(2):
+            turn_term(last_turns[c], 7, c, 0, True)
+        turn_term(last_turns[0], 7, 0, 1, False)
+        turn_pairs(5, BOTH, 4)
+        turn_term(last_turns[1], 7, 1, 1, False)
+
+        new_codes((4, 6, 5, 7), "last_add", "aei7")
+        for b, parts in ((4, BOTH), (6, HR), (6, HI)):
+            quantise(b, parts)
+        for c, (parts, copy) in enumerate(((HR, nc.vector.tensor_copy), (HI, nc.scalar.copy))):
+            copy(new_turned(7, parts)[:, 0], last_turns[c][:].rearrange("p t j -> p j t"))
+        score(4, 1, 6)
+        score(6, 1, 1)
+        for b, parts in ((5, BOTH), (7, HR)):
+            quantise(b, parts)
+        score(5, 1, 3)
+        last_sums = [bank(number, [P, P]) for number in (5, 7)]
         for g in range(2):
-            score_pass(last_sums[g][:], 7, g, 0)
+            score_pass(last_sums[g][:], 7, 1, g, 0)
         quantise(7, HI)
         last_result = keep.tile([P, 2, P], F32, name="result7")
         for g in range(2):
-            score_pass(last_sums[g][:], 7, g, 1)
+            score_pass(last_sums[g][:], 7, 1, g, 1)
         for g, copy in enumerate((nc.scalar.copy, nc.vector.tensor_copy)):
             copy(last_result[:, g], last_sums[g][:])
         nc.sync.dma_start(out[:, 7 * P:8 * P].rearrange("(g n) j -> n g j", g=2), last_result[:])

@@ -88,6 +88,11 @@ def tile_list_ckg_none_kernel(
         nc.sync.dma_start(tab_sb[:], words_view(tab_words))
         wer_sb = placed.tile([P, 2, 2 * R], U8, name="wer_sb", offset=PLACE_WER, align_bytes=256)
         nc.sync.dma_start(wer_sb[:].bitcast(I32), wer_words.rearrange("a p n -> p a n").bitcast(I32))
+        warm = psum.tile([P, R], F32, name="bank3", bufs=1)
+        for i in range(3):
+            nc.tensor.matmul_mx(
+                out=warm[:], lhsT=wer_sb[:, 0, 0:2 * P].bitcast(FP4X4), lhsT_scale=rel_planes[:, COL_WRR:COL_WRR + P],
+                rhs=wer_sb[:, 0, :].bitcast(FP4X4), rhs_scale=rel_planes[:, COL_WRR:COL_WRI], start=True, stop=True)
 
         got_rows = placed.tile([P, 3 * J], U8, name="got_rows", offset=PLACE_GOT, align_bytes=256)
         nc.vector.tensor_copy(got_rows[:, 0:J], tab_rows[:].indirect(list1[:]))

@@ -21,23 +21,27 @@ P = 128
 PACK = 4
 QUADRANT = 32
 ROWS = 16
+PER_COL = 16
 HALF = J // 2
-HALF_COLS = HALF // 16
-EARLY = 4
-ON_TENSOR = (1, 2, 6, 7)
-HOLDING = (6, 7)
+ALIGN = 256
 HR, HI, BOTH = slice(0, 1), slice(1, 2), slice(0, 2)
-COL_WER, COL_WEI, COLS_ENT = J, J + 2 * R, J + 4 * R
-COL_WRR, COL_WRI, COLS_REL = J, J + R, J + 2 * R
-PLACE_GOT2, PLACE_GOT, PLACE_WEI, PLACE_TAB2 = 0, 256, 512, 3 * J
-PLACE_WER = PLACE_TAB2 + 4 * T
-PLACE_ZEROS, PLACE_TAB = PLACE_WER + 3 * J // 2, PLACE_WER + 2 * J
-PLACE_LAST_PAIRS = PLACE_TAB + 4 * T
-PLACE_PAIRS = PLACE_LAST_PAIRS + 2 * J
-PLACE_GOT2_LATE, PLACE_WR = PLACE_PAIRS + 768, PLACE_PAIRS + J
+ON_TENSOR = (1, 2, 6, 7)
 ENT_PIECES = (slice(0, 2 * P), slice(2 * P, 4 * P), slice(4 * P, J))
 REL_PIECES = (slice(0, 2 * P), slice(2 * P, J))
+ENT_BANKS = ((4, 5), (7, 2), (0, 1), (6, 3), (4, 5))
+REL_BANKS = ((7, 2), (0, 1), (6, 3), (4, 5))
+WARM_UP = 3
+COL_WER, COL_WEI, COLS_ENT = J, J + 2 * R, J + 4 * R
+COL_WRR, COL_WRI, COLS_REL = J, J + R, J + 2 * R
 COL_NI = PACK * N
+AT_REL_ROWS0, AT_GOT, AT_WEI, AT_TAB2 = 0, ALIGN, 2 * ALIGN, 3 * J
+AT_WER = AT_TAB2 + 4 * T
+AT_ZEROS, AT_TAB = AT_WER + 3 * J // 2, AT_WER + 2 * J
+AT_PAIRS1 = AT_TAB + 4 * T
+AT_CAND, AT_IDENTITY = AT_PAIRS1 - HALF, AT_PAIRS1 + J
+AT_PAIRS0 = AT_PAIRS1 + 2 * J
+AT_REL_ROWS1, AT_WR = AT_PAIRS0 + J - ALIGN, AT_PAIRS0 + J
+AT_CAND_PLANES = AT_TAB + 2 * J
 
 
 def tile_list_ckg_none_kernel(
@@ -47,19 +51,17 @@ def tile_list_ckg_none_kernel(
     nc = tc.nc
     with ExitStack() as ctx:
         keep = ctx.enter_context(tc.tile_pool(name="keep", bufs=1))
-        ring = ctx.enter_context(tc.tile_pool(name="ring", bufs=3))
         placed = ctx.enter_context(tc.tile_pool(name="placed", bufs=1))
         psum = ctx.enter_context(tc.psum_pool(name="psum", bufs=1))
 
-        list1 = keep.tile([P, J // 16], U16, name="list1")
-        list2 = keep.tile([P, J // 16], U16, name="list2")
-        zeros = placed.tile([P, J // 4], I32, name="zeros", offset=PLACE_ZEROS, align_bytes=256)
-        tab_rows = keep.tile([P, T], U8, name="tab_rows", align_bytes=256)
-        tab2_rows = keep.tile([P, T], U8, name="tab2_rows", align_bytes=256)
-        ent_planes = keep.tile([P, COLS_ENT], U8, name="ent_planes", align_bytes=256)
-        ent_rows = keep.tile([P, COLS_ENT], U8, name="ent_rows", align_bytes=256)
-        ent_plane1 = keep.tile([P, J], U8, name="ent_plane1", align_bytes=256)
-        rel_planes = keep.tile([P, COLS_REL], U8, name="rel_planes", align_bytes=256)
+        def kept(shape, dtype, tag):
+            return keep.tile(shape, dtype, name=tag, tag=tag, align_bytes=ALIGN)
+
+        def at(offset, shape, dtype, name):
+            return placed.tile(shape, dtype, name=name, offset=offset, align_bytes=ALIGN)
+
+        def bank(number, shape):
+            return psum.tile(shape, F32, name=f"bank{number}", bufs=1)
 
         def words_view(words):
             return words.rearrange("a p n i -> p (a n i)").bitcast(I32)
@@ -68,12 +70,25 @@ def tile_list_ckg_none_kernel(
             nc.sync.dma_start(rows.bitcast(I32).rearrange("q (a n) -> q a n", a=scales.shape[0]),
                               scales.rearrange("a q n -> q a n").bitcast(I32))
 
+        def gather(target, window, offsets, piece):
+            nc.vector.tensor_copy(target, window.indirect(offsets[:, piece.start // PER_COL:piece.stop // PER_COL]))
+
+        list1 = keep.tile([P, J // PER_COL], U16, name="list1")
+        list2 = keep.tile([P, J // PER_COL], U16, name="list2")
+        zeros = at(AT_ZEROS, [P, J // 4], I32, "zeros")
+        tab_rows = kept([P, T], U8, "tab_rows")
+        tab2_rows = kept([P, T], U8, "tab2_rows")
+        ent_planes = kept([P, COLS_ENT], U8, "ent_planes")
+        ent_rows = kept([P, COLS_ENT], U8, "ent_rows")
+        ent_plane1 = kept([P, J], U8, "ent_plane1")
+        rel_planes = kept([P, COLS_REL], U8, "rel_planes")
+
         nc.vector.memset(zeros[:], 0)
         nc.vector.memset(tab2_rows[:].bitcast(I32), 0)
         nc.vector.memset(rel_planes[:, J:COLS_REL].bitcast(I32), 0)
         nc.vector.tensor_copy(ent_plane1[:].bitcast(I32), zeros[:])
-        nc.vector.memset(tab_rows[32:64, :].bitcast(I32), 0)
-        nc.vector.memset(tab_rows[64:P, :].bitcast(I32), 0)
+        nc.vector.memset(tab_rows[QUADRANT:2 * QUADRANT, :].bitcast(I32), 0)
+        nc.vector.memset(tab_rows[2 * QUADRANT:P, :].bitcast(I32), 0)
         nc.vector.memset(ent_planes[:].bitcast(I32), 0)
 
         nc.sync.dma_start(list1[:], offs)
@@ -84,75 +99,78 @@ def tile_list_ckg_none_kernel(
         nc.sync.dma_start(tab2_rows[0:P:8, :].bitcast(I32), tab2_scales[0].bitcast(I32))
         load_scale_rows(rel_planes[0:P:8, COL_WRR:COL_WRI], wrr_scales)
         load_scale_rows(rel_planes[0:P:8, COL_WRI:COLS_REL], wri_scales)
-        tab_sb = placed.tile([P, T], I32, name="tab_sb", offset=PLACE_TAB, align_bytes=256)
+        tab_sb = at(AT_TAB, [P, T], I32, "tab_sb")
         nc.sync.dma_start(tab_sb[:], words_view(tab_words))
-        wer_sb = placed.tile([P, 2, 2 * R], U8, name="wer_sb", offset=PLACE_WER, align_bytes=256)
+        wer_sb = at(AT_WER, [P, 2, 2 * R], U8, "wer_sb")
         nc.sync.dma_start(wer_sb[:].bitcast(I32), wer_words.rearrange("a p n -> p a n").bitcast(I32))
-        warm = psum.tile([P, R], F32, name="bank3", bufs=1)
-        for i in range(3):
+
+        warm = bank(3, [P, R])
+        for i in range(WARM_UP):
             nc.tensor.matmul_mx(
                 out=warm[:], lhsT=wer_sb[:, 0, 0:2 * P].bitcast(FP4X4), lhsT_scale=rel_planes[:, COL_WRR:COL_WRR + P],
                 rhs=wer_sb[:, 0, :].bitcast(FP4X4), rhs_scale=rel_planes[:, COL_WRR:COL_WRI], start=True, stop=True)
 
-        got_rows = placed.tile([P, 3 * J], U8, name="got_rows", offset=PLACE_GOT, align_bytes=256)
-        nc.vector.tensor_copy(got_rows[:, 0:J], tab_rows[:].indirect(list1[:]))
+        got_rows = at(AT_GOT, [P, 3 * J], U8, "got_rows")
+        gather(got_rows[:, 0:J], tab_rows[:], list1, slice(0, J))
         nc.vector.tensor_copy(ent_rows[:, 0:J].bitcast(I32), got_rows[:, 0:J].bitcast(I32))
+
+        def place_pass0(r):
+            nc.sync.dma_start(ent_planes[r:P:QUADRANT, :].bitcast(I32), ent_rows[r:ROWS:4, :].bitcast(I32))
+
         for r in range(4):
             nc.sync.dma_start(ent_plane1[r:P:QUADRANT, :].bitcast(I32),
                               ent_rows[ROWS + r:2 * ROWS:4, 0:J].bitcast(I32))
-        wei_sb = placed.tile([P, 2, 2 * R], U8, name="wei_sb", offset=PLACE_WEI, align_bytes=256)
-        for r in range(4):
-            if r == 2:
-                nc.sync.dma_start(wei_sb[:].bitcast(I32), wei_words.rearrange("a p n -> p a n").bitcast(I32))
-            nc.sync.dma_start(ent_planes[r:P:QUADRANT, :].bitcast(I32), ent_rows[r:ROWS:4, :].bitcast(I32))
-        tab2_sb = placed.tile([P, T], I32, name="tab2_sb", offset=PLACE_TAB2, align_bytes=256)
+        for r in (0, 1):
+            place_pass0(r)
+        wei_sb = at(AT_WEI, [P, 2, 2 * R], U8, "wei_sb")
+        nc.sync.dma_start(wei_sb[:].bitcast(I32), wei_words.rearrange("a p n -> p a n").bitcast(I32))
+        for r in (2, 3):
+            place_pass0(r)
+        tab2_sb = at(AT_TAB2, [P, T], I32, "tab2_sb")
         nc.sync.dma_start(tab2_sb[:], words_view(tab2_words))
 
-        def gather_rel_rows(h, place):
-            got2_rows = placed.tile([P, HALF], U8, name=f"got2_rows{h}", offset=place, align_bytes=256)
-            nc.vector.tensor_copy(got2_rows[:], tab2_rows[:].indirect(list2[:, HALF_COLS * h:HALF_COLS * (h + 1)]))
-            nc.vector.tensor_copy(rel_planes[:, HALF * h:HALF * (h + 1)].bitcast(I32), got2_rows[:].bitcast(I32))
-
-        gather_rel_rows(0, PLACE_GOT2)
+        def gather_rel_rows(h, offset):
+            piece = slice(HALF * h, HALF * (h + 1))
+            rel_rows = at(offset, [P, HALF], U8, f"rel_rows{h}")
+            gather(rel_rows[:], tab2_rows[:], list2, piece)
+            nc.vector.tensor_copy(rel_planes[:, piece].bitcast(I32), rel_rows[:].bitcast(I32))
 
         ent_words, rel_words = [], []
-        for h, piece in enumerate(ENT_PIECES):
-            n = piece.stop - piece.start
-            if h == 2:
-                gather_rel_rows(1, PLACE_GOT2_LATE)
-                for r in range(1, 4):
-                    nc.sync.dma_start(rel_planes[r:P:QUADRANT, :].bitcast(I32),
-                                      rel_planes[8 * r:P:QUADRANT, :].bitcast(I32))
-            pairs = placed.tile([P, n], U32, name=f"pairs{h}", offset=PLACE_LAST_PAIRS if h else PLACE_PAIRS,
-                                align_bytes=256)
-            nc.vector.tensor_copy(
-                pairs[:], tab_sb[:].bitcast(U32).indirect(list1[:, piece.start // 16:piece.stop // 16]))
-            parted = keep.tile([P, 2, n], U16, name=f"parted{h}", align_bytes=256)
+
+        def gather_ent_words(h, offset):
+            n = ENT_PIECES[h].stop - ENT_PIECES[h].start
+            pairs = at(offset, [P, n], U32, f"pairs{h}")
+            gather(pairs[:], tab_sb[:].bitcast(U32), list1, ENT_PIECES[h])
+            parted = kept([P, 2, n], U16, f"parted{h}")
             nc.vector.tensor_copy(parted[:], pairs[:].bitcast(U16).rearrange("p (j d) -> p d j", d=2))
             ent_words.extend(parted[:, :, j0:j0 + P] for j0 in range(0, n, P))
-        identity = placed.tile([P, P], F32, name="identity", offset=PLACE_LAST_PAIRS + J, align_bytes=256)
+
+        gather_rel_rows(0, AT_REL_ROWS0)
+        gather_ent_words(0, AT_PAIRS0)
+        gather_ent_words(1, AT_PAIRS1)
+        gather_rel_rows(1, AT_REL_ROWS1)
+        for r in range(1, 4):
+            nc.sync.dma_start(rel_planes[r:P:QUADRANT, :].bitcast(I32), rel_planes[8 * r:P:QUADRANT, :].bitcast(I32))
+        gather_ent_words(2, AT_PAIRS1)
+        identity = at(AT_IDENTITY, [P, P], F32, "identity")
         make_identity(nc, identity[:])
-        wr_sb = placed.tile([P, 2, R], I32, name="wr_sb", offset=PLACE_WR, align_bytes=256)
+        wr_sb = at(AT_WR, [P, 2, R], I32, "wr_sb")
         nc.sync.dma_start(wr_sb[:, 0, :], words_view(wrr_words))
         nc.sync.dma_start(wr_sb[:, 1, :], words_view(wri_words))
 
-        cand_sb = placed.tile([P, COL_NI + 2 * N], U8, name="cand_sb", offset=PLACE_LAST_PAIRS - J // 2, align_bytes=256)
+        cand_sb = at(AT_CAND, [P, COL_NI + 2 * N], U8, "cand_sb")
         nc.sync.dma_start(cand_sb[:, 0:COL_NI].bitcast(I32), words_view(nr_words))
         nc.sync.dma_start(cand_sb[:, COL_NI:COL_NI + 2 * N].bitcast(I32), ni_words[0].bitcast(I32))
-        cand_planes = placed.tile([P, 2, N], U8, name="cand_planes", offset=PLACE_TAB + 2 * J, align_bytes=256)
+        cand_planes = at(AT_CAND_PLANES, [P, 2, N], U8, "cand_planes")
         nc.vector.memset(cand_planes[:].bitcast(I32), 0)
         for c, cand_scales in enumerate((nr_scales, ni_scales)):
             for r in range(4):
                 nc.sync.dma_start(cand_planes[r:P:QUADRANT, c, :].bitcast(I32),
                                   cand_scales[0, r:ROWS:4, :].bitcast(I32))
         for h, piece in enumerate(REL_PIECES):
-            picked = keep.tile([P, piece.stop - piece.start], U32, name=f"picked{h}", align_bytes=256)
-            nc.vector.tensor_copy(
-                picked[:], tab2_sb[:].bitcast(U32).indirect(list2[:, piece.start // 16:piece.stop // 16]))
+            picked = kept([P, piece.stop - piece.start], U32, f"picked{h}")
+            gather(picked[:], tab2_sb[:].bitcast(U32), list2, piece)
             rel_words.extend(picked[:, j0:j0 + P] for j0 in range(0, piece.stop - piece.start, P))
-
-        def bank(number, shape):
-            return psum.tile(shape, F32, name=f"bank{number}", bufs=1)
 
         def by_place(view, b):
             if b in ON_TENSOR:
@@ -164,124 +182,110 @@ def tile_list_ckg_none_kernel(
                 return view.rearrange("j (t m) -> j t m", t=PACK)
             return view.rearrange("j (u m e) -> j u m e", u=2, e=2)
 
-        ent_parts, term_parts = {}, {}
-        ent, rel, terms, summed, turned, quant = {}, {}, {}, {}, {}, {}
+        ent, own_aei, rel, terms, own_term, summed, turned, quant = {}, {}, {}, {}, {}, {}, {}, {}
 
-        def project_entity(b, numbers, parts=BOTH):
-            if b not in ent:
-                ent[b] = keep.tile([P, 2, R], F32, name=f"ent{b}")
-                ent_parts[b] = [ent[b][:, c] for c in range(2)]
-                if b in HOLDING:
-                    aei = keep.tile([P, R], F32, name="aei", tag=f"aei{b}", align_bytes=256)
-                    ent_parts[b][1] = aei[:]
-            for c, number in zip(range(parts.start, parts.stop), numbers):
-                w_sb, col = ((wer_sb, COL_WER), (wei_sb, COL_WEI))[c]
-                acc = bank(number, [P, R])
-                for a in range(2):
-                    plane = (ent_planes, ent_plane1)[a][:, b * P:(b + 1) * P]
-                    nc.tensor.matmul_mx(
-                        out=acc[:], lhsT=ent_words[b][:, a].bitcast(FP4X4), lhsT_scale=plane,
-                        rhs=w_sb[:, a, :].bitcast(FP4X4), rhs_scale=ent_planes[:, col + a * R:col + (a + 1) * R],
-                        start=(a == 0), stop=(a == 1))
-                nc.scalar.copy(as_placed(ent_parts[b][c], b), by_place(acc[:], b))
+        def factor_of(b, e):
+            return own_aei[b][:] if e == 1 and b in own_aei else ent[b][:, e]
 
-        def project_relation(b, numbers, parts=BOTH):
-            for c in range(parts.start, parts.stop):
-                col = (COL_WRR, COL_WRI)[c]
-                acc = bank(numbers[c], [P, R])
+        def term_of(b, c, term):
+            return own_term[b][:] if (c, term) == (1, 1) and b in own_term else terms[b][term][:, c]
+
+        def project_entity(b, e, number):
+            w_sb, col = ((wer_sb, COL_WER), (wei_sb, COL_WEI))[e]
+            acc = bank(number, [P, R])
+            for a in range(2):
+                plane = (ent_planes, ent_plane1)[a][:, b * P:(b + 1) * P]
                 nc.tensor.matmul_mx(
-                    out=acc[:], lhsT=rel_words[b].bitcast(FP8X4),
-                    lhsT_scale=rel_planes[:, b * P:(b + 1) * P],
-                    rhs=wr_sb[:, c, :].bitcast(FP8X4), rhs_scale=rel_planes[:, col:col + R], start=True, stop=True)
-                rel.setdefault(b, []).append(by_place(acc[:], b))
+                    out=acc[:], lhsT=ent_words[b][:, a].bitcast(FP4X4), lhsT_scale=plane,
+                    rhs=w_sb[:, a, :].bitcast(FP4X4), rhs_scale=ent_planes[:, col + a * R:col + (a + 1) * R],
+                    start=(a == 0), stop=(a == 1))
+            nc.scalar.copy(as_placed(factor_of(b, e), b), by_place(acc[:], b))
 
-        def products_on_gpsimd(b):
-            arr_sb = keep.tile([P, R], F32, name=f"arr_sb{b}")
-            nc.scalar.copy(as_placed(arr_sb[:], b), rel[b][0])
-            new_terms(b)
-            nc.gpsimd.tensor_tensor(terms[b][0][:], ent[b][:], arr_sb[:].unsqueeze(1).to_broadcast([P, 2, R]), MULT)
+        def project_relation(b, term, number):
+            col = (COL_WRR, COL_WRI)[term]
+            acc = bank(number, [P, R])
+            nc.tensor.matmul_mx(
+                out=acc[:], lhsT=rel_words[b].bitcast(FP8X4), lhsT_scale=rel_planes[:, b * P:(b + 1) * P],
+                rhs=wr_sb[:, term, :].bitcast(FP8X4), rhs_scale=rel_planes[:, col:col + R], start=True, stop=True)
+            rel[b, term] = by_place(acc[:], b)
 
-        def arr_first(b):
+        def project_both(project, b, numbers):
+            for i, number in enumerate(numbers):
+                project(b, i, number)
+
+        def new_terms(b, arr_tag=None, ari_tag=None):
+            terms[b] = (kept([P, 2, R], F32, arr_tag or f"with_arr{b}"), kept([P, 2, R], F32, ari_tag or f"with_ari{b}"))
+
+        def product(b, c, term):
+            target = as_placed(term_of(b, c, term), b)
+            factor = as_placed(factor_of(b, (c + term) % 2), b)
+            if (c, term) != (0, 1):
+                nc.vector.tensor_tensor(target, factor, rel[b, term], MULT)
+            elif b in ON_TENSOR:
+                nc.vector.scalar_tensor_tensor(target, factor, -1.0, rel[b, term], MULT, MULT)
+            else:
+                for u in range(2):
+                    nc.vector.scalar_tensor_tensor(target[:, u], factor[:, u], -1.0, rel[b, term][:, u], MULT, MULT)
+
+        def multiply(b):
             for term in range(2):
                 for c in range(2):
                     product(b, c, term)
 
-        def new_terms(b, tag=None, last_tag=None, arr_tag=None):
-            with_arr = keep.tile([P, 2, R], F32, name="with_arr", tag=arr_tag or f"with_arr{b}", align_bytes=256)
-            with_ari = keep.tile([P, 2, R], F32, name="with_ari", tag=tag or f"with_ari{b}", align_bytes=256)
-            terms[b] = (with_arr, with_ari)
-            term_parts[b] = [[tile[:, c] for c in range(2)] for tile in terms[b]]
-            if last_tag is not None:
-                last_term = keep.tile([P, R], F32, name="last_term", tag=last_tag, align_bytes=256)
-                term_parts[b][1][1] = last_term[:]
+        def multiply_on_gpsimd(b):
+            arr_sb = kept([P, R], F32, f"arr_sb{b}")
+            nc.scalar.copy(as_placed(arr_sb[:], b), rel[b, 0])
+            new_terms(b)
+            nc.gpsimd.tensor_tensor(terms[b][0][:], ent[b][:], arr_sb[:].unsqueeze(1).to_broadcast([P, 2, R]), MULT)
 
-        def product(b, c, term):
-            target = as_placed(term_parts[b][term][c], b)
-            factor = as_placed(ent_parts[b][(c + term) % 2], b)
-            if (c, term) != (0, 1):
-                nc.vector.tensor_tensor(target, factor, rel[b][term], MULT)
-            elif b in ON_TENSOR:
-                nc.vector.scalar_tensor_tensor(target, factor, -1.0, rel[b][term], MULT, MULT)
-            else:
-                for u in range(2):
-                    nc.vector.scalar_tensor_tensor(target[:, u], factor[:, u], -1.0, rel[b][term][:, u], MULT, MULT)
-
-        def multiply(b, parts):
-            for c in range(parts.start, parts.stop):
-                for term in range(2):
-                    product(b, c, term)
-
-        def combine(b, parts, tag=None):
-            shape = [P, parts.stop - parts.start, R]
-            if tag is None:
-                total = ring.tile(shape, BF16, name="summed", align_bytes=64)
-            else:
-                total = keep.tile(shape, BF16, name="summed", tag=tag, align_bytes=256)
-            nc.gpsimd.tensor_tensor(total[:], terms[b][0][:, parts], terms[b][1][:, parts], ADD)
-            summed[b, parts.start] = total
+        def combine(b, tag=None):
+            summed[b] = kept([P, 2, R], BF16, tag or f"summed{b}")
+            nc.gpsimd.tensor_tensor(summed[b][:], terms[b][0][:], terms[b][1][:], ADD)
 
         def new_turned(b, parts):
-            turned[b, parts.start] = keep.tile([P, parts.stop - parts.start, P, PACK], BF16, name="turned",
-                                               tag=f"turned{b}_{parts.start}", align_bytes=256)
-            return turned[b, parts.start]
+            tile = kept([P, parts.stop - parts.start, P, PACK], BF16, f"turned{b}_{parts.start}")
+            for c in range(parts.start, parts.stop):
+                turned[b, c] = tile[:, c - parts.start]
+            return tile
 
-        def turn_pairs(b, parts, number, copy=nc.scalar.copy):
-            n = parts.stop - parts.start
-            target = new_turned(b, parts)
-            acc = bank(number, [P, n, 2, P])
-            words = summed[b, parts.start][:].rearrange("j c r -> j (c r)").bitcast(F32).rearrange(
-                "j (c u p) -> j c u p", c=n, u=2)
-            for i in range(n):
+        def turn_pairs(b, number):
+            target = new_turned(b, BOTH)
+            acc = bank(number, [P, 2, 2, P])
+            words = summed[b][:].rearrange("j c r -> j (c r)").bitcast(F32).rearrange("j (c u p) -> j c u p", c=2, u=2)
+            for c in range(2):
                 for u in range(2):
-                    nc.tensor.transpose(acc[:, i, u, :], words[:, i, u, :], identity[:])
-            copy(
-                target[:].rearrange("p c j t -> p (c j t)").bitcast(F32).rearrange("p (c j u) -> p c j u", c=n, u=2),
+                    nc.tensor.transpose(acc[:, c, u, :], words[:, c, u, :], identity[:])
+            nc.scalar.copy(
+                target[:].rearrange("p c j t -> p (c j t)").bitcast(F32).rearrange("p (c j u) -> p c j u", c=2, u=2),
                 acc[:].rearrange("p c u j -> p c j u"))
 
         def turn_term(acc, b, c, term, first):
             for t in range(PACK):
-                nc.tensor.matmul(acc[:, t, :], term_parts[b][term][c][:, t * P:(t + 1) * P], identity[:],
+                nc.tensor.matmul(acc[:, t, :], term_of(b, c, term)[:, t * P:(t + 1) * P], identity[:],
                                  start=(first and t == 0), stop=(not first and t == PACK - 1), is_transpose=True)
 
-        def turn_terms(b, parts, numbers, order=(1, 0)):
-            target = new_turned(b, parts)
-            for i, number in enumerate(numbers):
+        def round_turned(acc, b, c, copy=nc.scalar.copy):
+            copy(turned[b, c], acc[:].rearrange("p t j -> p j t"))
+
+        def turn_terms(b, parts, numbers, order=(0, 1)):
+            new_turned(b, parts)
+            for c, number in zip(range(parts.start, parts.stop), numbers):
                 acc = bank(number, [P, PACK, P])
                 for term in order:
-                    turn_term(acc, b, parts.start + i, term, term == order[0])
-                nc.scalar.copy(target[:, i], acc[:].rearrange("p t j -> p j t"))
+                    turn_term(acc, b, c, term, term == order[0])
+                round_turned(acc, b, c)
 
-        def new_codes(blocks, tag, planes_tag):
-            codes = keep.tile([P, 2, len(blocks) * P], U32, name="codes", tag=tag, align_bytes=256)
-            planes = keep.tile([P, 2, len(blocks) * P], U8, name="planes", tag=planes_tag, align_bytes=256)
+        def new_codes(blocks, codes_tag, planes_tag):
+            codes = kept([P, 2, len(blocks) * P], U32, codes_tag)
+            planes = kept([P, 2, len(blocks) * P], U8, planes_tag)
             for i, b in enumerate(blocks):
                 quant[b] = (codes, planes, i * P)
 
-        def quantise(b, parts):
+        def quantise(b, parts=BOTH):
             codes, planes, j0 = quant[b]
             for c in range(parts.start, parts.stop):
                 nc.vector.quantize_mx(out=codes[:, c, j0:j0 + P].bitcast(FP8X4), scales=planes[:, c, j0:j0 + P],
-                                      in_=turned[b, parts.start][:, c - parts.start].rearrange("p j t -> p (j t)"))
+                                      in_=turned[b, c].rearrange("p j t -> p (j t)"))
 
         def score_pass(acc, b, n, g, c):
             codes, planes, j0 = quant[b]
@@ -294,93 +298,104 @@ def tile_list_ckg_none_kernel(
                 rhs=codes[:, c, j0:j0 + n * P].bitcast(FP8X4), rhs_scale=planes[:, c, j0:j0 + n * P],
                 start=(c == 0), stop=(c == 1))
 
-        def score(first, n, number, copy=nc.scalar.copy):
+        def store(b, n, result):
+            nc.sync.dma_start(out[:, b * P:(b + n) * P].rearrange("(g n) j -> n g j", g=2), result[:])
+
+        def score(b, n, number):
             acc = bank(number, [P, 2, n * P])
             for g in range(2):
                 for c in range(2):
-                    score_pass(acc[:, g, :], first, n, g, c)
-            result = keep.tile([P, 2, n * P], F32, name=f"result{first}")
-            copy(result[:], acc[:])
-            nc.sync.dma_start(out[:, first * P:(first + n) * P].rearrange("(g n) j -> n g j", g=2), result[:])
+                    score_pass(acc[:, g, :], b, n, g, c)
+            result = kept([P, 2, n * P], F32, f"result{b}")
+            nc.scalar.copy(result[:], acc[:])
+            store(b, n, result)
 
-        ENT_BANKS = ((4, 5), (7, 2), (0, 1), (6, 3), (4, 5))
-        REL_BANKS = ((7, 2), (0, 1), (6, 3), (4, 5))
-        for b in range(5):
-            project_entity(b, ENT_BANKS[b])
-        for parts in (HR, HI):
+        for b in range(J // P):
+            ent[b] = kept([P, 2, R], F32, f"ent{b}")
+        for b in (6, 7):
+            own_aei[b] = kept([P, R], F32, f"aei{b}")
+
+        for b, numbers in enumerate(ENT_BANKS):
+            project_both(project_entity, b, numbers)
+        for term in range(2):
             for b in (0, 1):
-                project_relation(b, REL_BANKS[b], parts)
+                project_relation(b, term, REL_BANKS[b][term])
         for b in (2, 3):
-            project_relation(b, REL_BANKS[b])
-        products_on_gpsimd(1)
-        products_on_gpsimd(2)
-        project_entity(5, (0, 6))
+            project_both(project_relation, b, REL_BANKS[b])
+        for b in (1, 2):
+            multiply_on_gpsimd(b)
+        project_both(project_entity, 5, (0, 6))
         new_terms(0)
-        arr_first(0)
-        combine(0, BOTH)
+        multiply(0)
+        combine(0)
         for b in (1, 2):
             for c in range(2):
                 product(b, c, 1)
-        turn_terms(1, HR, (7,), (0, 1))
-        project_relation(4, (1, 3))
-        turn_terms(1, HI, (2,), (0, 1))
-        project_entity(6, (7,), HR)
+
+        project_entity(6, 0, 7)
+        turn_terms(1, HR, (2,))
+        turn_terms(1, HI, (0,))
+        project_both(project_relation, 4, (1, 3))
+        project_entity(6, 1, 6)
         new_terms(3)
-        arr_first(3)
-        combine(3, BOTH)
-        turn_terms(2, BOTH, (0, 6), (0, 1))
-        project_relation(5, (4, 5))
-        project_entity(6, (0,), HI)
-        new_terms(4, "pause")
-        arr_first(4)
-        combine(4, BOTH)
-        turn_pairs(0, BOTH, 2)
-        project_relation(6, (1, 3))
-        project_entity(7, (6,), HR)
-        new_terms(5, "last_add")
-        arr_first(5)
-        turn_pairs(3, BOTH, 7)
-        project_entity(7, (2,), HI)
-        project_relation(7, (4, 5))
-        new_terms(6, None, "turned0_0")
+        multiply(3)
+        combine(3)
+        turn_terms(2, BOTH, (7, 2))
+        project_both(project_relation, 5, (4, 5))
+        project_entity(7, 0, 0)
+        new_terms(4, ari_tag="before_pause")
+        multiply(4)
+        combine(4)
+        turn_pairs(0, 6)
+        project_both(project_relation, 6, (1, 3))
+        turn_pairs(3, 7)
+        project_entity(7, 1, 2)
+        new_terms(5, ari_tag="last_add")
+        multiply(5)
+        project_both(project_relation, 7, (4, 5))
+
+        new_terms(6)
+        own_term[6] = kept([P, R], F32, "turned0_0")
         for c, term in ((0, 1), (1, 0), (0, 0)):
             product(6, c, term)
         turn_terms(6, HR, (0,), (1, 0))
-        turn_pairs(4, BOTH, 6)
-        new_codes((0, 1, 2, 3), "pause", "aei6")
-        for b, parts in ((0, BOTH), (1, HR), (1, HI), (2, BOTH), (3, BOTH)):
-            quantise(b, parts)
-        combine(5, BOTH, tag="turned3_0")
+        turn_pairs(4, 6)
+        new_codes((0, 1, 2, 3), "before_pause", "aei6")
+        for b in range(4):
+            quantise(b)
+        combine(5, tag="turned3_0")
         product(6, 1, 1)
         score(0, 2, 1)
-        turn_terms(6, HI, (7,), (0, 1))
+        turn_terms(6, HI, (7,))
         score(2, 2, 3)
-        new_terms(7, "turned2_0", None, "turned1_0")
-        arr_first(7)
+
+        new_terms(7, arr_tag="turned1_0", ari_tag="turned2_0")
+        multiply(7)
         last_turns = [bank(number, [P, PACK, P]) for number in (2, 0)]
         for c in range(2):
             turn_term(last_turns[c], 7, c, 0, True)
         turn_term(last_turns[0], 7, 0, 1, False)
-        turn_pairs(5, BOTH, 4)
+        turn_pairs(5, 4)
         turn_term(last_turns[1], 7, 1, 1, False)
 
         new_codes((4, 6, 5, 7), "last_add", "aei7")
-        for b, parts in ((4, BOTH), (6, HR), (6, HI)):
-            quantise(b, parts)
-        for c, (parts, copy) in enumerate(((HR, nc.vector.tensor_copy), (HI, nc.scalar.copy))):
-            copy(new_turned(7, parts)[:, 0], last_turns[c][:].rearrange("p t j -> p j t"))
+        for b in (4, 6):
+            quantise(b)
+        for parts, copy in ((HR, nc.vector.tensor_copy), (HI, nc.scalar.copy)):
+            new_turned(7, parts)
+            round_turned(last_turns[parts.start], 7, parts.start, copy)
         score(4, 1, 6)
         score(6, 1, 1)
-        for b, parts in ((5, BOTH), (7, HR)):
-            quantise(b, parts)
+        quantise(5)
+        quantise(7, HR)
         score(5, 1, 3)
         last_sums = [bank(number, [P, P]) for number in (5, 7)]
         for g in range(2):
             score_pass(last_sums[g][:], 7, 1, g, 0)
         quantise(7, HI)
-        last_result = keep.tile([P, 2, P], F32, name="result7")
         for g in range(2):
             score_pass(last_sums[g][:], 7, 1, g, 1)
+        last_result = kept([P, 2, P], F32, "result7")
         for g, copy in enumerate((nc.scalar.copy, nc.vector.tensor_copy)):
             copy(last_result[:, g], last_sums[g][:])
-        nc.sync.dma_start(out[:, 7 * P:8 * P].rearrange("(g n) j -> n g j", g=2), last_result[:])
+        store(7, 1, last_result)

@@ -30,7 +30,6 @@ ENT_PIECES = (slice(0, 2 * P), slice(2 * P, 4 * P), slice(4 * P, J))
 REL_PIECES = (slice(0, 2 * P), slice(2 * P, J))
 ENT_BANKS = ((4, 5), (7, 2), (0, 1), (6, 3), (4, 5))
 REL_BANKS = ((7, 2), (0, 1), (6, 3), (4, 5))
-WARM_UP = 3
 COL_WER, COL_WEI, COLS_ENT = J, J + 2 * R, J + 4 * R
 COL_WRR, COL_WRI, COLS_REL = J, J + R, J + 2 * R
 COL_NI = PACK * N
@@ -103,12 +102,6 @@ def tile_list_ckg_none_kernel(
         nc.sync.dma_start(tab_sb[:], words_view(tab_words))
         wer_sb = at(AT_WER, [P, 2, 2 * R], U8, "wer_sb")
         nc.sync.dma_start(wer_sb[:].bitcast(I32), wer_words.rearrange("a p n -> p a n").bitcast(I32))
-
-        warm = bank(3, [P, R])
-        for i in range(WARM_UP):
-            nc.tensor.matmul_mx(
-                out=warm[:], lhsT=wer_sb[:, 0, 0:2 * P].bitcast(FP4X4), lhsT_scale=rel_planes[:, COL_WRR:COL_WRR + P],
-                rhs=wer_sb[:, 0, :].bitcast(FP4X4), rhs_scale=rel_planes[:, COL_WRR:COL_WRI], start=True, stop=True)
 
         got_rows = at(AT_GOT, [P, 3 * J], U8, "got_rows")
         gather(got_rows[:, 0:J], tab_rows[:], list1, slice(0, J))

@@ -23,24 +23,24 @@ QUADRANT = 32
 ROWS = 16
 PER_COL = 16
 HALF = J // 2
+PIECE = 2 * P
 ALIGN = 256
 HR, HI, BOTH = slice(0, 1), slice(1, 2), slice(0, 2)
-ON_TENSOR = (1, 2, 6, 7)
-ENT_PIECES = (slice(0, 2 * P), slice(2 * P, 4 * P), slice(4 * P, J))
+ON_TENSOR = (3, 4, 6, 7)
 REL_PIECES = (slice(0, 2 * P), slice(2 * P, J))
-ENT_BANKS = ((4, 5), (7, 2), (0, 1), (6, 3), (4, 5))
-REL_BANKS = ((7, 2), (0, 1), (6, 3), (4, 5))
-COL_WER, COL_WEI, COLS_ENT = J, J + 2 * R, J + 4 * R
+COL_WER, COL_WEI, COLS_ENT = J, J + R, J + 2 * R
 COL_WRR, COL_WRI, COLS_REL = J, J + R, J + 2 * R
 COL_NI = PACK * N
-AT_REL_ROWS0, AT_GOT, AT_WEI, AT_TAB2 = 0, ALIGN, 2 * ALIGN, 3 * J
-AT_WER = AT_TAB2 + 4 * T
-AT_ZEROS, AT_TAB = AT_WER + 3 * J // 2, AT_WER + 2 * J
-AT_PAIRS1 = AT_TAB + 4 * T
-AT_CAND, AT_IDENTITY = AT_PAIRS1 - HALF, AT_PAIRS1 + J
-AT_PAIRS0 = AT_PAIRS1 + 2 * J
-AT_REL_ROWS1, AT_WR = AT_PAIRS0 + J - ALIGN, AT_PAIRS0 + J
-AT_CAND_PLANES = AT_TAB + 2 * J
+AT_TAB2 = 0
+AT_REL_ROWS0 = AT_TAB2 + 4 * T
+AT_GOT = AT_REL_ROWS0 + ALIGN - J
+AT_PAIRS_B = AT_REL_ROWS0 + HALF
+AT_PAIRS_A = AT_PAIRS_B + 4 * PIECE
+AT_LATE = AT_PAIRS_A + 4 * PIECE
+AT_REL_ROWS1 = AT_LATE - ALIGN
+AT_CAND = AT_PAIRS_A + HALF - (COL_NI + 2 * N)
+AT_IDENTITY = AT_PAIRS_A + HALF
+LATE_WRR, LATE_WEI, LATE_WRI, COLS_LATE = 0, 4 * R, 8 * R, 12 * R
 
 
 def tile_list_ckg_none_kernel(
@@ -65,60 +65,51 @@ def tile_list_ckg_none_kernel(
         def words_view(words):
             return words.rearrange("a p n i -> p (a n i)").bitcast(I32)
 
-        def load_scale_rows(rows, scales):
-            nc.sync.dma_start(rows.bitcast(I32).rearrange("q (a n) -> q a n", a=scales.shape[0]),
-                              scales.rearrange("a q n -> q a n").bitcast(I32))
-
         def gather(target, window, offsets, piece):
             nc.vector.tensor_copy(target, window.indirect(offsets[:, piece.start // PER_COL:piece.stop // PER_COL]))
 
+        def clear(view):
+            nc.vector.memset(view.bitcast(I32), 0)
+
         list1 = keep.tile([P, J // PER_COL], U16, name="list1")
         list2 = keep.tile([P, J // PER_COL], U16, name="list2")
-        zeros = at(AT_ZEROS, [P, J // 4], I32, "zeros")
         tab_rows = kept([P, T], U8, "tab_rows")
         tab2_rows = kept([P, T], U8, "tab2_rows")
-        ent_planes = kept([P, COLS_ENT], U8, "ent_planes")
-        ent_rows = kept([P, COLS_ENT], U8, "ent_rows")
-        ent_plane1 = kept([P, J], U8, "ent_plane1")
+        ent_planes = [kept([P, COLS_ENT], U8, "ent_planes0")]
         rel_planes = kept([P, COLS_REL], U8, "rel_planes")
 
-        nc.vector.memset(zeros[:], 0)
-        nc.vector.memset(tab2_rows[:].bitcast(I32), 0)
-        nc.vector.memset(rel_planes[:, J:COLS_REL].bitcast(I32), 0)
-        nc.vector.tensor_copy(ent_plane1[:].bitcast(I32), zeros[:])
-        nc.vector.memset(tab_rows[QUADRANT:2 * QUADRANT, :].bitcast(I32), 0)
-        nc.vector.memset(tab_rows[2 * QUADRANT:P, :].bitcast(I32), 0)
-        nc.vector.memset(ent_planes[:].bitcast(I32), 0)
+        clear(tab2_rows[:])
+        clear(rel_planes[:, J:COLS_REL])
+        for rows in (slice(QUADRANT, 2 * QUADRANT), slice(2 * QUADRANT, P)):
+            clear(tab_rows[rows, :])
+        for rows in (slice(QUADRANT, 2 * QUADRANT), slice(2 * QUADRANT, P)):
+            clear(ent_planes[0][rows, J:COLS_ENT])
+
+        def both_passes(scales):
+            return scales.rearrange("a q n -> (a q) n").bitcast(I32)
 
         nc.sync.dma_start(list1[:], offs)
-        nc.sync.dma_start(tab_rows[0:2 * ROWS, :].bitcast(I32), tab_scales.rearrange("a q t -> (a q) t").bitcast(I32))
+        nc.sync.dma_start(tab_rows[0:2 * ROWS, :].bitcast(I32), both_passes(tab_scales))
+        nc.sync.dma_start(ent_planes[0][0:2 * ROWS, COL_WER:COL_WEI].bitcast(I32), both_passes(wer_scales))
+        nc.sync.dma_start(ent_planes[0][0:2 * ROWS, COL_WEI:COLS_ENT].bitcast(I32), both_passes(wei_scales))
         nc.sync.dma_start(list2[:], offs2)
-        load_scale_rows(ent_rows[0:ROWS, COL_WER:COL_WEI], wer_scales)
-        load_scale_rows(ent_rows[0:ROWS, COL_WEI:COLS_ENT], wei_scales)
-        nc.sync.dma_start(tab2_rows[0:P:8, :].bitcast(I32), tab2_scales[0].bitcast(I32))
-        load_scale_rows(rel_planes[0:P:8, COL_WRR:COL_WRI], wrr_scales)
-        load_scale_rows(rel_planes[0:P:8, COL_WRI:COLS_REL], wri_scales)
-        tab_sb = at(AT_TAB, [P, T], I32, "tab_sb")
+        tab_sb = kept([P, T], I32, "tab_sb")
         nc.sync.dma_start(tab_sb[:], words_view(tab_words))
-        wer_sb = at(AT_WER, [P, 2, 2 * R], U8, "wer_sb")
+        wer_sb = kept([P, 2, 2 * R], U8, "wer_sb")
         nc.sync.dma_start(wer_sb[:].bitcast(I32), wer_words.rearrange("a p n -> p a n").bitcast(I32))
+        nc.scalar.dma_start(tab2_rows[0:P:8, :].bitcast(I32), tab2_scales[0].bitcast(I32))
+        nc.scalar.dma_start(rel_planes[0:P:8, COL_WRR:COL_WRI].bitcast(I32), wrr_scales[0].bitcast(I32))
+        nc.scalar.dma_start(rel_planes[0:P:8, COL_WRI:COLS_REL].bitcast(I32), wri_scales[0].bitcast(I32))
 
-        got_rows = at(AT_GOT, [P, 3 * J], U8, "got_rows")
-        gather(got_rows[:, 0:J], tab_rows[:], list1, slice(0, J))
-        nc.vector.tensor_copy(ent_rows[:, 0:J].bitcast(I32), got_rows[:, 0:J].bitcast(I32))
-
-        def place_pass0(r):
-            nc.sync.dma_start(ent_planes[r:P:QUADRANT, :].bitcast(I32), ent_rows[r:ROWS:4, :].bitcast(I32))
-
-        for r in range(4):
-            nc.sync.dma_start(ent_plane1[r:P:QUADRANT, :].bitcast(I32),
-                              ent_rows[ROWS + r:2 * ROWS:4, 0:J].bitcast(I32))
-        for r in (0, 1):
-            place_pass0(r)
-        wei_sb = at(AT_WEI, [P, 2, 2 * R], U8, "wei_sb")
-        nc.sync.dma_start(wei_sb[:].bitcast(I32), wei_words.rearrange("a p n -> p a n").bitcast(I32))
-        for r in (2, 3):
-            place_pass0(r)
+        got_rows = at(AT_GOT, [P, J], U8, "got_rows")
+        gather(got_rows[:], tab_rows[:], list1, slice(0, J))
+        nc.vector.tensor_copy(ent_planes[0][:, 0:J].bitcast(I32), got_rows[:].bitcast(I32))
+        ent_planes.append(kept([P, COLS_ENT], U8, "tab_rows"))
+        for a in (1, 0):
+            for q in range(1 - a, 4):
+                row = ROWS * a + 4 * q
+                nc.sync.dma_start(ent_planes[a][QUADRANT * q:QUADRANT * q + 4, :].bitcast(I32),
+                                  ent_planes[0][row:row + 4, :].bitcast(I32))
         tab2_sb = at(AT_TAB2, [P, T], I32, "tab2_sb")
         nc.sync.dma_start(tab2_sb[:], words_view(tab2_words))
 
@@ -131,31 +122,32 @@ def tile_list_ckg_none_kernel(
         ent_words, rel_words = [], []
 
         def gather_ent_words(h, offset):
-            n = ENT_PIECES[h].stop - ENT_PIECES[h].start
-            pairs = at(offset, [P, n], U32, f"pairs{h}")
-            gather(pairs[:], tab_sb[:].bitcast(U32), list1, ENT_PIECES[h])
-            parted = kept([P, 2, n], U16, f"parted{h}")
+            pairs = at(offset, [P, PIECE], U32, f"pairs{h}")
+            gather(pairs[:], tab_sb[:].bitcast(U32), list1, slice(h * PIECE, (h + 1) * PIECE))
+            parted = kept([P, 2, PIECE], U16, f"parted{h}")
             nc.vector.tensor_copy(parted[:], pairs[:].bitcast(U16).rearrange("p (j d) -> p d j", d=2))
-            ent_words.extend(parted[:, :, j0:j0 + P] for j0 in range(0, n, P))
+            ent_words.extend(parted[:, :, j0:j0 + P] for j0 in range(0, PIECE, P))
 
         gather_rel_rows(0, AT_REL_ROWS0)
-        gather_ent_words(0, AT_PAIRS0)
-        gather_ent_words(1, AT_PAIRS1)
+        gather_ent_words(0, AT_PAIRS_A)
+        gather_ent_words(1, AT_PAIRS_B)
         gather_rel_rows(1, AT_REL_ROWS1)
         for r in range(1, 4):
             nc.sync.dma_start(rel_planes[r:P:QUADRANT, :].bitcast(I32), rel_planes[8 * r:P:QUADRANT, :].bitcast(I32))
-        gather_ent_words(2, AT_PAIRS1)
+        late = at(AT_LATE, [P, COLS_LATE], U8, "late")
+        nc.sync.dma_start(late[:, LATE_WRR:LATE_WEI].bitcast(I32), words_view(wrr_words))
+        nc.sync.dma_start(late[:, LATE_WEI:LATE_WRI].bitcast(I32).rearrange("p (a n) -> p a n", a=2),
+                          wei_words.rearrange("a p n -> p a n").bitcast(I32))
+        nc.sync.dma_start(late[:, LATE_WRI:COLS_LATE].bitcast(I32), words_view(wri_words))
+        gather_ent_words(2, AT_PAIRS_B)
+        gather_ent_words(3, AT_PAIRS_A)
         identity = at(AT_IDENTITY, [P, P], F32, "identity")
         make_identity(nc, identity[:])
-        wr_sb = at(AT_WR, [P, 2, R], I32, "wr_sb")
-        nc.sync.dma_start(wr_sb[:, 0, :], words_view(wrr_words))
-        nc.sync.dma_start(wr_sb[:, 1, :], words_view(wri_words))
 
         cand_sb = at(AT_CAND, [P, COL_NI + 2 * N], U8, "cand_sb")
         nc.sync.dma_start(cand_sb[:, 0:COL_NI].bitcast(I32), words_view(nr_words))
         nc.sync.dma_start(cand_sb[:, COL_NI:COL_NI + 2 * N].bitcast(I32), ni_words[0].bitcast(I32))
-        cand_planes = at(AT_CAND_PLANES, [P, 2, N], U8, "cand_planes")
-        nc.vector.memset(cand_planes[:].bitcast(I32), 0)
+        cand_planes = kept([P, 2, N], U8, "tab_sb")
         for c, cand_scales in enumerate((nr_scales, ni_scales)):
             for r in range(4):
                 nc.sync.dma_start(cand_planes[r:P:QUADRANT, c, :].bitcast(I32),
@@ -184,27 +176,26 @@ def tile_list_ckg_none_kernel(
             return own_term[b][:] if (c, term) == (1, 1) and b in own_term else terms[b][term][:, c]
 
         def project_entity(b, e, number):
-            w_sb, col = ((wer_sb, COL_WER), (wei_sb, COL_WEI))[e]
+            col = (COL_WER, COL_WEI)[e]
             acc = bank(number, [P, R])
             for a in range(2):
-                plane = (ent_planes, ent_plane1)[a][:, b * P:(b + 1) * P]
+                words = wer_sb[:, a, :] if e == 0 else late[:, LATE_WEI + 2 * R * a:LATE_WEI + 2 * R * (a + 1)]
                 nc.tensor.matmul_mx(
-                    out=acc[:], lhsT=ent_words[b][:, a].bitcast(FP4X4), lhsT_scale=plane,
-                    rhs=w_sb[:, a, :].bitcast(FP4X4), rhs_scale=ent_planes[:, col + a * R:col + (a + 1) * R],
+                    out=acc[:], lhsT=ent_words[b][:, a].bitcast(FP4X4),
+                    lhsT_scale=ent_planes[a][:, b * P:(b + 1) * P],
+                    rhs=words.bitcast(FP4X4), rhs_scale=ent_planes[a][:, col:col + R],
                     start=(a == 0), stop=(a == 1))
             nc.scalar.copy(as_placed(factor_of(b, e), b), by_place(acc[:], b))
 
         def project_relation(b, term, number):
             col = (COL_WRR, COL_WRI)[term]
+            start = (LATE_WRR, LATE_WRI)[term]
             acc = bank(number, [P, R])
             nc.tensor.matmul_mx(
                 out=acc[:], lhsT=rel_words[b].bitcast(FP8X4), lhsT_scale=rel_planes[:, b * P:(b + 1) * P],
-                rhs=wr_sb[:, term, :].bitcast(FP8X4), rhs_scale=rel_planes[:, col:col + R], start=True, stop=True)
+                rhs=late[:, start:start + 4 * R].bitcast(FP8X4), rhs_scale=rel_planes[:, col:col + R],
+                start=True, stop=True)
             rel[b, term] = by_place(acc[:], b)
-
-        def project_both(project, b, numbers):
-            for i, number in enumerate(numbers):
-                project(b, i, number)
 
         def new_terms(b, arr_tag=None, ari_tag=None):
             terms[b] = (kept([P, 2, R], F32, arr_tag or f"with_arr{b}"), kept([P, 2, R], F32, ari_tag or f"with_ari{b}"))
@@ -220,16 +211,22 @@ def tile_list_ckg_none_kernel(
                 for u in range(2):
                     nc.vector.scalar_tensor_tensor(target[:, u], factor[:, u], -1.0, rel[b, term][:, u], MULT, MULT)
 
-        def multiply(b):
-            for term in range(2):
+        def multiply(b, which=(0, 1)):
+            for term in which:
                 for c in range(2):
                     product(b, c, term)
 
-        def multiply_on_gpsimd(b):
-            arr_sb = kept([P, R], F32, f"arr_sb{b}")
-            nc.scalar.copy(as_placed(arr_sb[:], b), rel[b, 0])
+        arr_sb = {}
+
+        def copy_arr(b):
+            arr_sb[b] = kept([P, R], F32, f"arr_sb{b}")
+            nc.scalar.copy(as_placed(arr_sb[b][:], b), rel[b, 0])
             new_terms(b)
-            nc.gpsimd.tensor_tensor(terms[b][0][:], ent[b][:], arr_sb[:].unsqueeze(1).to_broadcast([P, 2, R]), MULT)
+
+        def multiply_on_gpsimd(b, parts):
+            n = parts.stop - parts.start
+            nc.gpsimd.tensor_tensor(terms[b][0][:, parts], ent[b][:, parts],
+                                    arr_sb[b][:].unsqueeze(1).to_broadcast([P, n, R]), MULT)
 
         def combine(b, tag=None):
             summed[b] = kept([P, 2, R], BF16, tag or f"summed{b}")
@@ -305,84 +302,91 @@ def tile_list_ckg_none_kernel(
 
         for b in range(J // P):
             ent[b] = kept([P, 2, R], F32, f"ent{b}")
-        for b in (6, 7):
-            own_aei[b] = kept([P, R], F32, f"aei{b}")
 
-        for b, numbers in enumerate(ENT_BANKS):
-            project_both(project_entity, b, numbers)
-        for term in range(2):
-            for b in (0, 1):
-                project_relation(b, term, REL_BANKS[b][term])
-        for b in (2, 3):
-            project_both(project_relation, b, REL_BANKS[b])
-        for b in (1, 2):
-            multiply_on_gpsimd(b)
-        project_both(project_entity, 5, (0, 6))
+        for b in range(J // P):
+            project_entity(b, 0, (b + 6) % 8)
+        project_relation(1, 0, 7)
+        copy_arr(1)
+        multiply_on_gpsimd(1, HR)
+        project_relation(0, 0, 6)
+        project_entity(1, 1, 0)
+        multiply_on_gpsimd(1, HI)
+        project_relation(0, 1, 2)
+        project_relation(1, 1, 3)
+        project_entity(0, 1, 1)
+        project_relation(2, 0, 4)
+        copy_arr(2)
+        project_entity(2, 1, 5)
+        multiply_on_gpsimd(2, BOTH)
+        project_relation(2, 1, 7)
         new_terms(0)
-        multiply(0)
+        for b, c, term in ((0, 0, 0), (0, 1, 1), (1, 1, 1), (0, 1, 0), (0, 0, 1)):
+            product(b, c, term)
         combine(0)
-        for b in (1, 2):
-            for c in range(2):
-                product(b, c, 1)
+        project_relation(3, 0, 6)
+        project_entity(3, 1, 0)
+        project_relation(3, 1, 2)
+        product(1, 0, 1)
+        combine(1)
+        project_relation(4, 0, 4)
+        project_entity(4, 1, 5)
+        multiply(2, (1,))
+        combine(2)
+        project_relation(4, 1, 3)
+        project_entity(5, 1, 1)
 
-        project_entity(6, 0, 7)
-        turn_terms(1, HR, (2,))
-        turn_terms(1, HI, (0,))
-        project_both(project_relation, 4, (1, 3))
-        project_entity(6, 1, 6)
         new_terms(3)
         multiply(3)
-        combine(3)
-        turn_terms(2, BOTH, (7, 2))
-        project_both(project_relation, 5, (4, 5))
-        project_entity(7, 0, 0)
-        new_terms(4, ari_tag="before_pause")
+        project_relation(5, 0, 6)
+        project_relation(5, 1, 2)
+        turn_terms(3, BOTH, (7, 0))
+        turn_pairs(0, 5)
+        project_entity(6, 1, 1)
+        new_terms(4)
         multiply(4)
-        combine(4)
-        turn_pairs(0, 6)
-        project_both(project_relation, 6, (1, 3))
-        turn_pairs(3, 7)
-        project_entity(7, 1, 2)
+        project_relation(6, 0, 4)
+        project_relation(6, 1, 3)
+        turn_terms(4, BOTH, (7, 0))
+        turn_pairs(1, 5)
         new_terms(5, ari_tag="last_add")
         multiply(5)
-        project_both(project_relation, 7, (4, 5))
+        project_relation(7, 0, 6)
+        project_entity(7, 1, 5)
+        project_relation(7, 1, 2)
+        turn_pairs(2, 1)
 
-        new_terms(6)
-        own_term[6] = kept([P, R], F32, "turned0_0")
-        for c, term in ((0, 1), (1, 0), (0, 0)):
-            product(6, c, term)
-        turn_terms(6, HR, (0,), (1, 0))
-        turn_pairs(4, 6)
-        new_codes((0, 1, 2, 3), "before_pause", "aei6")
-        for b in range(4):
+        new_codes((0, 1, 3, 4), "with_ari2", "planes0")
+        for b in (0, 3, 4, 1):
             quantise(b)
-        combine(5, tag="turned3_0")
-        product(6, 1, 1)
-        score(0, 2, 1)
-        turn_terms(6, HI, (7,))
-        score(2, 2, 3)
+        combine(5, tag="turned1_0")
+        new_terms(6)
+        for c, term in ((0, 0), (0, 1), (1, 0), (1, 1)):
+            product(6, c, term)
+        score(0, 2, 7)
+        turn_terms(6, HR, (5,))
+        score(3, 2, 0)
+        turn_terms(6, HI, (1,))
 
-        new_terms(7, arr_tag="turned1_0", ari_tag="turned2_0")
+        new_terms(7)
         multiply(7)
-        last_turns = [bank(number, [P, PACK, P]) for number in (2, 0)]
+        last_turns = [bank(number, [P, PACK, P]) for number in (4, 3)]
+        turn_pairs(5, 7)
         for c in range(2):
             turn_term(last_turns[c], 7, c, 0, True)
         turn_term(last_turns[0], 7, 0, 1, False)
-        turn_pairs(5, 4)
         turn_term(last_turns[1], 7, 1, 1, False)
 
-        new_codes((4, 6, 5, 7), "last_add", "aei7")
-        for b in (4, 6):
+        new_codes((2, 6, 5, 7), "last_add", "planes1")
+        for b in (2, 6, 5):
             quantise(b)
         for parts, copy in ((HR, nc.vector.tensor_copy), (HI, nc.scalar.copy)):
             new_turned(7, parts)
             round_turned(last_turns[parts.start], 7, parts.start, copy)
-        score(4, 1, 6)
-        score(6, 1, 1)
-        quantise(5)
+        score(2, 1, 0)
+        score(6, 1, 5)
         quantise(7, HR)
-        score(5, 1, 3)
-        last_sums = [bank(number, [P, P]) for number in (5, 7)]
+        score(5, 1, 1)
+        last_sums = [bank(number, [P, P]) for number in (6, 2)]
         for g in range(2):
             score_pass(last_sums[g][:], 7, 1, g, 0)
         quantise(7, HI)

@@ -26,21 +26,23 @@ HALF = J // 2
 PIECE = 2 * P
 ALIGN = 256
 HR, HI, BOTH = slice(0, 1), slice(1, 2), slice(0, 2)
-ON_TENSOR = (3, 4, 6, 7)
-REL_PIECES = (slice(0, 2 * P), slice(2 * P, J))
-COL_WER, COL_WEI, COLS_ENT = J, J + R, J + 2 * R
-COL_WRR, COL_WRI, COLS_REL = J, J + R, J + 2 * R
+ON_TENSOR = (1, 3, 5, 7)
+REL_PIECES = (slice(0, 2 * P), slice(2 * P, 4 * P), slice(4 * P, J))
+COL_WER, COL_PASS1, COLS_ENT = J, J + 2 * R, 2 * J + 2 * R
+COL_WRR, COL_WRI, COL_WEI, COLS_REL = J, J + R, J + 2 * R, J + 4 * R
 COL_NI = PACK * N
-AT_TAB2 = 0
+AT_TAB = 0
+AT_ZEROS = AT_TAB + 4 * T - ALIGN
+AT_TAB2 = AT_ZEROS + J
+AT_GOT = AT_TAB2 + 4 * T - 3 * ALIGN
 AT_REL_ROWS0 = AT_TAB2 + 4 * T
-AT_GOT = AT_REL_ROWS0 + ALIGN - J
 AT_PAIRS_B = AT_REL_ROWS0 + HALF
 AT_PAIRS_A = AT_PAIRS_B + 4 * PIECE
 AT_LATE = AT_PAIRS_A + 4 * PIECE
 AT_REL_ROWS1 = AT_LATE - ALIGN
 AT_CAND = AT_PAIRS_A + HALF - (COL_NI + 2 * N)
 AT_IDENTITY = AT_PAIRS_A + HALF
-LATE_WRR, LATE_WEI, LATE_WRI, COLS_LATE = 0, 4 * R, 8 * R, 12 * R
+LATE_WRR, LATE_WRI, LATE_WEI, COLS_LATE = 0, 4 * R, 8 * R, 12 * R
 
 
 def tile_list_ckg_none_kernel(
@@ -75,41 +77,45 @@ def tile_list_ckg_none_kernel(
         list2 = keep.tile([P, J // PER_COL], U16, name="list2")
         tab_rows = kept([P, T], U8, "tab_rows")
         tab2_rows = kept([P, T], U8, "tab2_rows")
-        ent_planes = [kept([P, COLS_ENT], U8, "ent_planes0")]
+        ent_planes = kept([P, COLS_ENT], U8, "ent_planes")
         rel_planes = kept([P, COLS_REL], U8, "rel_planes")
+        zeros = at(AT_ZEROS, [P, J // 4], I32, "zeros")
 
+        clear(tab_rows[:])
+        nc.vector.memset(zeros[:], 0)
         clear(tab2_rows[:])
+        nc.vector.tensor_copy(ent_planes[:, J:COLS_ENT].bitcast(I32).rearrange("p (h n) -> p h n", h=2),
+                              zeros[:].unsqueeze(1).to_broadcast([P, 2, J // 4]))
         clear(rel_planes[:, J:COLS_REL])
-        for rows in (slice(QUADRANT, 2 * QUADRANT), slice(2 * QUADRANT, P)):
-            clear(tab_rows[rows, :])
-        for rows in (slice(QUADRANT, 2 * QUADRANT), slice(2 * QUADRANT, P)):
-            clear(ent_planes[0][rows, J:COLS_ENT])
 
-        def both_passes(scales):
-            return scales.rearrange("a q n -> (a q) n").bitcast(I32)
+        def load_scale_rows(queue, rows, scales):
+            queue.dma_start(rows.bitcast(I32).rearrange("q (a n) -> q a n", a=scales.shape[0]),
+                            scales.rearrange("a q n -> q a n").bitcast(I32))
 
         nc.sync.dma_start(list1[:], offs)
-        nc.sync.dma_start(tab_rows[0:2 * ROWS, :].bitcast(I32), both_passes(tab_scales))
-        nc.sync.dma_start(ent_planes[0][0:2 * ROWS, COL_WER:COL_WEI].bitcast(I32), both_passes(wer_scales))
-        nc.sync.dma_start(ent_planes[0][0:2 * ROWS, COL_WEI:COLS_ENT].bitcast(I32), both_passes(wei_scales))
         nc.sync.dma_start(list2[:], offs2)
-        tab_sb = kept([P, T], I32, "tab_sb")
-        nc.sync.dma_start(tab_sb[:], words_view(tab_words))
         wer_sb = kept([P, 2, 2 * R], U8, "wer_sb")
         nc.sync.dma_start(wer_sb[:].bitcast(I32), wer_words.rearrange("a p n -> p a n").bitcast(I32))
-        nc.scalar.dma_start(tab2_rows[0:P:8, :].bitcast(I32), tab2_scales[0].bitcast(I32))
-        nc.scalar.dma_start(rel_planes[0:P:8, COL_WRR:COL_WRI].bitcast(I32), wrr_scales[0].bitcast(I32))
-        nc.scalar.dma_start(rel_planes[0:P:8, COL_WRI:COLS_REL].bitcast(I32), wri_scales[0].bitcast(I32))
+        for a in range(2):
+            nc.sync.dma_start(tab_rows[4 * a:P:8, :].bitcast(I32), tab_scales[a].bitcast(I32))
+        load_scale_rows(nc.sync, tab2_rows[0:P:8, :], tab2_scales)
+        load_scale_rows(nc.sync, ent_planes[0:P:8, COL_WER:COL_PASS1], wer_scales)
+        tab_sb = at(AT_TAB, [P, T], I32, "tab_sb")
+        nc.sync.dma_start(tab_sb[:], words_view(tab_words))
+        load_scale_rows(nc.gpsimd, rel_planes[0:P:8, COL_WRR:COL_WRI], wrr_scales)
+        load_scale_rows(nc.gpsimd, rel_planes[0:P:8, COL_WRI:COL_WEI], wri_scales)
+        load_scale_rows(nc.gpsimd, rel_planes[0:P:8, COL_WEI:COLS_REL], wei_scales)
 
-        got_rows = at(AT_GOT, [P, J], U8, "got_rows")
-        gather(got_rows[:], tab_rows[:], list1, slice(0, J))
-        nc.vector.tensor_copy(ent_planes[0][:, 0:J].bitcast(I32), got_rows[:].bitcast(I32))
-        ent_planes.append(kept([P, COLS_ENT], U8, "tab_rows"))
-        for a in (1, 0):
-            for q in range(1 - a, 4):
-                row = ROWS * a + 4 * q
-                nc.sync.dma_start(ent_planes[a][QUADRANT * q:QUADRANT * q + 4, :].bitcast(I32),
-                                  ent_planes[0][row:row + 4, :].bitcast(I32))
+        got_rows = at(AT_GOT, [P, AT_PAIRS_A + ALIGN - AT_GOT], U8, "got_rows")
+        gather(got_rows[:, 0:J], tab_rows[:], list1, slice(0, J))
+        nc.vector.tensor_copy(ent_planes[:, 0:J].bitcast(I32), got_rows[:, 0:J].bitcast(I32))
+        for r in range(4):
+            queue = nc.gpsimd if r == 0 else nc.sync
+            queue.dma_start(ent_planes[r:P:QUADRANT, COL_PASS1:COLS_ENT].bitcast(I32),
+                            ent_planes[8 * r + 4:P:QUADRANT, 0:J].bitcast(I32))
+        for r in range(1, 4):
+            nc.sync.dma_start(ent_planes[r:P:QUADRANT, 0:COL_PASS1].bitcast(I32),
+                              ent_planes[8 * r:P:QUADRANT, 0:COL_PASS1].bitcast(I32))
         tab2_sb = at(AT_TAB2, [P, T], I32, "tab2_sb")
         nc.sync.dma_start(tab2_sb[:], words_view(tab2_words))
 
@@ -135,10 +141,10 @@ def tile_list_ckg_none_kernel(
         for r in range(1, 4):
             nc.sync.dma_start(rel_planes[r:P:QUADRANT, :].bitcast(I32), rel_planes[8 * r:P:QUADRANT, :].bitcast(I32))
         late = at(AT_LATE, [P, COLS_LATE], U8, "late")
-        nc.sync.dma_start(late[:, LATE_WRR:LATE_WEI].bitcast(I32), words_view(wrr_words))
-        nc.sync.dma_start(late[:, LATE_WEI:LATE_WRI].bitcast(I32).rearrange("p (a n) -> p a n", a=2),
+        nc.sync.dma_start(late[:, LATE_WRR:LATE_WRI].bitcast(I32), words_view(wrr_words))
+        nc.sync.dma_start(late[:, LATE_WRI:LATE_WEI].bitcast(I32), words_view(wri_words))
+        nc.sync.dma_start(late[:, LATE_WEI:COLS_LATE].bitcast(I32).rearrange("p (a n) -> p a n", a=2),
                           wei_words.rearrange("a p n -> p a n").bitcast(I32))
-        nc.sync.dma_start(late[:, LATE_WRI:COLS_LATE].bitcast(I32), words_view(wri_words))
         gather_ent_words(2, AT_PAIRS_B)
         gather_ent_words(3, AT_PAIRS_A)
         identity = at(AT_IDENTITY, [P, P], F32, "identity")
@@ -147,7 +153,7 @@ def tile_list_ckg_none_kernel(
         cand_sb = at(AT_CAND, [P, COL_NI + 2 * N], U8, "cand_sb")
         nc.sync.dma_start(cand_sb[:, 0:COL_NI].bitcast(I32), words_view(nr_words))
         nc.sync.dma_start(cand_sb[:, COL_NI:COL_NI + 2 * N].bitcast(I32), ni_words[0].bitcast(I32))
-        cand_planes = kept([P, 2, N], U8, "tab_sb")
+        cand_planes = at(AT_TAB, [P, 2, N], U8, "cand_planes")
         for c, cand_scales in enumerate((nr_scales, ni_scales)):
             for r in range(4):
                 nc.sync.dma_start(cand_planes[r:P:QUADRANT, c, :].bitcast(I32),
@@ -168,6 +174,7 @@ def tile_list_ckg_none_kernel(
             return view.rearrange("j (u m e) -> j u m e", u=2, e=2)
 
         ent, own_aei, rel, terms, own_term, summed, turned, quant = {}, {}, {}, {}, {}, {}, {}, {}
+        group = {}
 
         def factor_of(b, e):
             return own_aei[b][:] if e == 1 and b in own_aei else ent[b][:, e]
@@ -176,15 +183,17 @@ def tile_list_ckg_none_kernel(
             return own_term[b][:] if (c, term) == (1, 1) and b in own_term else terms[b][term][:, c]
 
         def project_entity(b, e, number):
-            col = (COL_WER, COL_WEI)[e]
             acc = bank(number, [P, R])
             for a in range(2):
-                words = wer_sb[:, a, :] if e == 0 else late[:, LATE_WEI + 2 * R * a:LATE_WEI + 2 * R * (a + 1)]
+                if e == 0:
+                    words, scales = wer_sb[:, a, :], ent_planes[:, COL_WER + a * R:COL_WER + (a + 1) * R]
+                else:
+                    words = late[:, LATE_WEI + 2 * R * a:LATE_WEI + 2 * R * (a + 1)]
+                    scales = rel_planes[:, COL_WEI + a * R:COL_WEI + (a + 1) * R]
+                col = COL_PASS1 * a + b * P
                 nc.tensor.matmul_mx(
-                    out=acc[:], lhsT=ent_words[b][:, a].bitcast(FP4X4),
-                    lhsT_scale=ent_planes[a][:, b * P:(b + 1) * P],
-                    rhs=words.bitcast(FP4X4), rhs_scale=ent_planes[a][:, col:col + R],
-                    start=(a == 0), stop=(a == 1))
+                    out=acc[:], lhsT=ent_words[b][:, a].bitcast(FP4X4), lhsT_scale=ent_planes[:, col:col + P],
+                    rhs=words.bitcast(FP4X4), rhs_scale=scales, start=(a == 0), stop=(a == 1))
             nc.scalar.copy(as_placed(factor_of(b, e), b), by_place(acc[:], b))
 
         def project_relation(b, term, number):
@@ -232,21 +241,28 @@ def tile_list_ckg_none_kernel(
             summed[b] = kept([P, 2, R], BF16, tag or f"summed{b}")
             nc.gpsimd.tensor_tensor(summed[b][:], terms[b][0][:], terms[b][1][:], ADD)
 
-        def new_turned(b, parts):
-            tile = kept([P, parts.stop - parts.start, P, PACK], BF16, f"turned{b}_{parts.start}")
-            for c in range(parts.start, parts.stop):
-                turned[b, c] = tile[:, c - parts.start]
-            return tile
-
-        def turn_pairs(b, number):
-            target = new_turned(b, BOTH)
-            acc = bank(number, [P, 2, 2, P])
-            words = summed[b][:].rearrange("j c r -> j (c r)").bitcast(F32).rearrange("j (c u p) -> j c u p", c=2, u=2)
+        def combine_parts(b, tag):
+            summed[b] = kept([P, 2, R], BF16, tag)
             for c in range(2):
+                nc.gpsimd.tensor_tensor(summed[b][:, c], term_of(b, c, 0), term_of(b, c, 1), ADD)
+
+        def new_turned(first, n):
+            group[first] = kept([P, 2, n, P, PACK], BF16, f"turned{first}")
+            for b in range(first, first + n):
+                for c in range(2):
+                    turned[b, c] = group[first][:, c, b - first]
+
+        def turn_pairs(b, number, parts=BOTH):
+            n = parts.stop - parts.start
+            first = max(f for f in group if f <= b)
+            target = group[first][:, parts, b - first]
+            acc = bank(number, [P, n, 2, P])
+            words = summed[b][:].rearrange("j c r -> j (c r)").bitcast(F32).rearrange("j (c u p) -> j c u p", c=2, u=2)
+            for c in range(n):
                 for u in range(2):
-                    nc.tensor.transpose(acc[:, c, u, :], words[:, c, u, :], identity[:])
+                    nc.tensor.transpose(acc[:, c, u, :], words[:, parts.start + c, u, :], identity[:])
             nc.scalar.copy(
-                target[:].rearrange("p c j t -> p (c j t)").bitcast(F32).rearrange("p (c j u) -> p c j u", c=2, u=2),
+                target.rearrange("p c j t -> p c (j t)").bitcast(F32).rearrange("p c (j u) -> p c j u", u=2),
                 acc[:].rearrange("p c u j -> p c j u"))
 
         def turn_term(acc, b, c, term, first):
@@ -258,7 +274,6 @@ def tile_list_ckg_none_kernel(
             copy(turned[b, c], acc[:].rearrange("p t j -> p j t"))
 
         def turn_terms(b, parts, numbers, order=(0, 1)):
-            new_turned(b, parts)
             for c, number in zip(range(parts.start, parts.stop), numbers):
                 acc = bank(number, [P, PACK, P])
                 for term in order:
@@ -271,11 +286,12 @@ def tile_list_ckg_none_kernel(
             for i, b in enumerate(blocks):
                 quant[b] = (codes, planes, i * P)
 
-        def quantise(b, parts=BOTH):
+        def quantise(b, n, parts=BOTH):
             codes, planes, j0 = quant[b]
             for c in range(parts.start, parts.stop):
-                nc.vector.quantize_mx(out=codes[:, c, j0:j0 + P].bitcast(FP8X4), scales=planes[:, c, j0:j0 + P],
-                                      in_=turned[b, c].rearrange("p j t -> p (j t)"))
+                nc.vector.quantize_mx(out=codes[:, c, j0:j0 + n * P].bitcast(FP8X4),
+                                      scales=planes[:, c, j0:j0 + n * P],
+                                      in_=group[b][:, c].rearrange("p b j t -> p (b j t)"))
 
         def score_pass(acc, b, n, g, c):
             codes, planes, j0 = quant[b]
@@ -302,94 +318,104 @@ def tile_list_ckg_none_kernel(
 
         for b in range(J // P):
             ent[b] = kept([P, 2, R], F32, f"ent{b}")
+        own_aei[6] = kept([P, R], F32, "aei6")
+        for first, n in ((0, 4), (4, 2), (6, 1), (7, 1)):
+            new_turned(first, n)
 
-        for b in range(J // P):
-            project_entity(b, 0, (b + 6) % 8)
-        project_relation(1, 0, 7)
+        for b in range(4):
+            project_entity(b, 0, b)
+        project_relation(1, 0, 6)
         copy_arr(1)
         multiply_on_gpsimd(1, HR)
-        project_relation(0, 0, 6)
-        project_entity(1, 1, 0)
-        multiply_on_gpsimd(1, HI)
+        project_relation(0, 0, 7)
+        project_relation(2, 0, 0)
+        copy_arr(2)
+        multiply_on_gpsimd(2, HR)
+        for b, number in ((4, 4), (5, 5), (6, 1)):
+            project_entity(b, 0, number)
         project_relation(0, 1, 2)
         project_relation(1, 1, 3)
-        project_entity(0, 1, 1)
-        project_relation(2, 0, 4)
-        copy_arr(2)
-        project_entity(2, 1, 5)
-        multiply_on_gpsimd(2, BOTH)
-        project_relation(2, 1, 7)
+        project_relation(2, 1, 5)
+        project_entity(0, 1, 4)
+        project_entity(1, 1, 6)
+        multiply_on_gpsimd(1, HI)
+        project_entity(2, 1, 0)
+        multiply_on_gpsimd(2, HI)
+        project_relation(3, 0, 1)
+
+        def multiply_block(b):
+            for c, term in ((0, 0), (1, 0), (0, 1), (1, 1)):
+                product(b, c, term)
+
         new_terms(0)
-        for b, c, term in ((0, 0, 0), (0, 1, 1), (1, 1, 1), (0, 1, 0), (0, 0, 1)):
+        for b, c, term in ((0, 0, 0), (0, 1, 1), (1, 1, 1), (2, 1, 1), (0, 1, 0), (0, 0, 1), (1, 0, 1), (2, 0, 1)):
             product(b, c, term)
         combine(0)
-        project_relation(3, 0, 6)
-        project_entity(3, 1, 0)
-        project_relation(3, 1, 2)
-        product(1, 0, 1)
-        combine(1)
-        project_relation(4, 0, 4)
-        project_entity(4, 1, 5)
-        multiply(2, (1,))
         combine(2)
+        project_entity(3, 1, 4)
+        project_relation(3, 1, 2)
+        project_entity(4, 1, 7)
+        project_relation(4, 0, 4)
         project_relation(4, 1, 3)
-        project_entity(5, 1, 1)
-
+        turn_terms(1, HR, (6,))
+        project_entity(5, 1, 7)
+        turn_terms(1, HI, (5,))
         new_terms(3)
-        multiply(3)
-        project_relation(5, 0, 6)
+        multiply_block(3)
+        project_relation(5, 0, 1)
+        turn_terms(3, HR, (6,), (1, 0))
         project_relation(5, 1, 2)
-        turn_terms(3, BOTH, (7, 0))
-        turn_pairs(0, 5)
-        project_entity(6, 1, 1)
-        new_terms(4)
-        multiply(4)
+        project_entity(6, 1, 7)
+        new_terms(4, ari_tag="before_pause")
+        multiply_block(4)
+        combine(4)
         project_relation(6, 0, 4)
+        turn_terms(3, HI, (5,), (1, 0))
+        turn_pairs(0, 0)
         project_relation(6, 1, 3)
-        turn_terms(4, BOTH, (7, 0))
-        turn_pairs(1, 5)
-        new_terms(5, ari_tag="last_add")
-        multiply(5)
-        project_relation(7, 0, 6)
-        project_entity(7, 1, 5)
+        project_entity(7, 0, 6)
+        turn_pairs(2, 7)
+        new_terms(5)
+        new_terms(6, ari_tag="last_add")
+        multiply_block(5)
+        project_relation(7, 0, 1)
+        turn_terms(5, HR, (5,), (1, 0))
         project_relation(7, 1, 2)
-        turn_pairs(2, 1)
-
-        new_codes((0, 1, 3, 4), "with_ari2", "planes0")
-        for b in (0, 3, 4, 1):
-            quantise(b)
-        combine(5, tag="turned1_0")
-        new_terms(6)
-        for c, term in ((0, 0), (0, 1), (1, 0), (1, 1)):
+        project_entity(7, 1, 0)
+        turn_terms(5, HI, (6,), (1, 0))
+        for c, term in ((0, 0), (0, 1), (1, 0)):
             product(6, c, term)
-        score(0, 2, 7)
-        turn_terms(6, HR, (5,))
-        score(3, 2, 0)
-        turn_terms(6, HI, (1,))
+        turn_pairs(4, 7)
+
+        new_codes((0, 1, 2, 3), "before_pause", "aei6")
+        quantise(0, 4)
+        product(6, 1, 1)
+        combine_parts(6, "turned0")
+        score(0, 2, 5)
 
         new_terms(7)
-        multiply(7)
+        multiply_block(7)
         last_turns = [bank(number, [P, PACK, P]) for number in (4, 3)]
-        turn_pairs(5, 7)
-        for c in range(2):
-            turn_term(last_turns[c], 7, c, 0, True)
+        turn_term(last_turns[0], 7, 0, 0, True)
+        score(2, 2, 1)
+        turn_term(last_turns[1], 7, 1, 0, True)
+        turn_pairs(6, 0, HR)
         turn_term(last_turns[0], 7, 0, 1, False)
+        turn_pairs(6, 6, HI)
         turn_term(last_turns[1], 7, 1, 1, False)
 
-        new_codes((2, 6, 5, 7), "last_add", "planes1")
-        for b in (2, 6, 5):
-            quantise(b)
-        for parts, copy in ((HR, nc.vector.tensor_copy), (HI, nc.scalar.copy)):
-            new_turned(7, parts)
-            round_turned(last_turns[parts.start], 7, parts.start, copy)
-        score(2, 1, 0)
+        new_codes((4, 5, 6, 7), "last_add", "planes_end")
+        quantise(4, 2)
+        for c, copy in enumerate((nc.vector.tensor_copy, nc.scalar.copy)):
+            round_turned(last_turns[c], 7, c, copy)
+        score(4, 2, 7)
+        quantise(6, 1)
         score(6, 1, 5)
-        quantise(7, HR)
-        score(5, 1, 1)
-        last_sums = [bank(number, [P, P]) for number in (6, 2)]
+        quantise(7, 1, HR)
+        last_sums = [bank(number, [P, P]) for number in (2, 1)]
         for g in range(2):
             score_pass(last_sums[g][:], 7, 1, g, 0)
-        quantise(7, HI)
+        quantise(7, 1, HI)
         for g in range(2):
             score_pass(last_sums[g][:], 7, 1, g, 1)
         last_result = kept([P, 2, P], F32, "result7")

@@ -28,21 +28,21 @@ ALIGN = 256
 HR, HI, BOTH = slice(0, 1), slice(1, 2), slice(0, 2)
 ON_TENSOR = (1, 3, 5, 7)
 REL_PIECES = (slice(0, 2 * P), slice(2 * P, 4 * P), slice(4 * P, J))
-COL_WER, COL_PASS1, COLS_ENT = J, J + 2 * R, 2 * J + 2 * R
+COL_WER, COLS_ENT = J, J + R
 COL_WRR, COL_WRI, COL_WEI, COLS_REL = J, J + R, J + 2 * R, J + 4 * R
 COL_NI = PACK * N
 AT_TAB = 0
-AT_ZEROS = AT_TAB + 4 * T - ALIGN
-AT_TAB2 = AT_ZEROS + J
+AT_TAB2 = AT_TAB + 4 * T
 AT_GOT = AT_TAB2 + 4 * T - 3 * ALIGN
-AT_REL_ROWS0 = AT_TAB2 + 4 * T
+AT_WRR = AT_TAB2 + 4 * T
+AT_REL_ROWS0 = AT_WRR + 4 * R
 AT_PAIRS_B = AT_REL_ROWS0 + HALF
 AT_PAIRS_A = AT_PAIRS_B + 4 * PIECE
 AT_LATE = AT_PAIRS_A + 4 * PIECE
 AT_REL_ROWS1 = AT_LATE - ALIGN
 AT_CAND = AT_PAIRS_A + HALF - (COL_NI + 2 * N)
 AT_IDENTITY = AT_PAIRS_A + HALF
-LATE_WRR, LATE_WRI, LATE_WEI, COLS_LATE = 0, 4 * R, 8 * R, 12 * R
+LATE_WRI, LATE_WEI, COLS_LATE = 0, 4 * R, 8 * R
 
 
 def tile_list_ckg_none_kernel(
@@ -77,47 +77,49 @@ def tile_list_ckg_none_kernel(
         list2 = keep.tile([P, J // PER_COL], U16, name="list2")
         tab_rows = kept([P, T], U8, "tab_rows")
         tab2_rows = kept([P, T], U8, "tab2_rows")
-        ent_planes = kept([P, COLS_ENT], U8, "ent_planes")
+        planes0 = kept([P, COLS_ENT], U8, "planes0")
         rel_planes = kept([P, COLS_REL], U8, "rel_planes")
-        zeros = at(AT_ZEROS, [P, J // 4], I32, "zeros")
 
-        clear(tab_rows[:])
-        nc.vector.memset(zeros[:], 0)
         clear(tab2_rows[:])
-        nc.vector.tensor_copy(ent_planes[:, J:COLS_ENT].bitcast(I32).rearrange("p (h n) -> p h n", h=2),
-                              zeros[:].unsqueeze(1).to_broadcast([P, 2, J // 4]))
         clear(rel_planes[:, J:COLS_REL])
+        for rows in (slice(QUADRANT, 2 * QUADRANT), slice(2 * QUADRANT, P)):
+            clear(tab_rows[rows, :])
+            clear(planes0[rows, J:COLS_ENT])
 
-        def load_scale_rows(queue, rows, scales):
-            queue.dma_start(rows.bitcast(I32).rearrange("q (a n) -> q a n", a=scales.shape[0]),
-                            scales.rearrange("a q n -> q a n").bitcast(I32))
+        def both_passes(scales):
+            return scales.rearrange("a q n -> (a q) n").bitcast(I32)
+
+        def load_scale_rows(rows, scales):
+            nc.gpsimd.dma_start(rows.bitcast(I32).rearrange("q (a n) -> q a n", a=scales.shape[0]),
+                                scales.rearrange("a q n -> q a n").bitcast(I32))
 
         nc.sync.dma_start(list1[:], offs)
+        nc.sync.dma_start(tab_rows[0:2 * ROWS, :].bitcast(I32), both_passes(tab_scales))
+        nc.sync.dma_start(planes0[0:2 * ROWS, COL_WER:COLS_ENT].bitcast(I32), both_passes(wer_scales))
         nc.sync.dma_start(list2[:], offs2)
         wer_sb = kept([P, 2, 2 * R], U8, "wer_sb")
         nc.sync.dma_start(wer_sb[:].bitcast(I32), wer_words.rearrange("a p n -> p a n").bitcast(I32))
-        for a in range(2):
-            nc.sync.dma_start(tab_rows[4 * a:P:8, :].bitcast(I32), tab_scales[a].bitcast(I32))
-        load_scale_rows(nc.sync, tab2_rows[0:P:8, :], tab2_scales)
-        load_scale_rows(nc.sync, ent_planes[0:P:8, COL_WER:COL_PASS1], wer_scales)
         tab_sb = at(AT_TAB, [P, T], I32, "tab_sb")
         nc.sync.dma_start(tab_sb[:], words_view(tab_words))
-        load_scale_rows(nc.gpsimd, rel_planes[0:P:8, COL_WRR:COL_WRI], wrr_scales)
-        load_scale_rows(nc.gpsimd, rel_planes[0:P:8, COL_WRI:COL_WEI], wri_scales)
-        load_scale_rows(nc.gpsimd, rel_planes[0:P:8, COL_WEI:COLS_REL], wei_scales)
+        nc.scalar.dma_start(tab2_rows[0:P:8, :].bitcast(I32), tab2_scales[0].bitcast(I32))
+        load_scale_rows(rel_planes[0:P:8, COL_WRR:COL_WRI], wrr_scales)
+        load_scale_rows(rel_planes[0:P:8, COL_WRI:COL_WEI], wri_scales)
+        load_scale_rows(rel_planes[0:P:8, COL_WEI:COLS_REL], wei_scales)
 
         got_rows = at(AT_GOT, [P, AT_PAIRS_A + ALIGN - AT_GOT], U8, "got_rows")
         gather(got_rows[:, 0:J], tab_rows[:], list1, slice(0, J))
-        nc.vector.tensor_copy(ent_planes[:, 0:J].bitcast(I32), got_rows[:, 0:J].bitcast(I32))
+        nc.vector.tensor_copy(planes0[:, 0:J].bitcast(I32), got_rows[:, 0:J].bitcast(I32))
+        planes1 = kept([P, COLS_ENT], U8, "tab_rows")
+        for q in (2, 1, 3):
+            nc.sync.dma_start(planes0[QUADRANT * q:QUADRANT * q + 4, :].bitcast(I32),
+                              planes0[4 * q:4 * q + 4, :].bitcast(I32))
         for r in range(4):
-            queue = nc.gpsimd if r == 0 else nc.sync
-            queue.dma_start(ent_planes[r:P:QUADRANT, COL_PASS1:COLS_ENT].bitcast(I32),
-                            ent_planes[8 * r + 4:P:QUADRANT, 0:J].bitcast(I32))
-        for r in range(1, 4):
-            nc.sync.dma_start(ent_planes[r:P:QUADRANT, 0:COL_PASS1].bitcast(I32),
-                              ent_planes[8 * r:P:QUADRANT, 0:COL_PASS1].bitcast(I32))
+            queue = nc.gpsimd if r < 2 else nc.sync
+            queue.dma_start(planes1[r:P:QUADRANT, :].bitcast(I32), planes0[ROWS + r:2 * ROWS:4, :].bitcast(I32))
         tab2_sb = at(AT_TAB2, [P, T], I32, "tab2_sb")
         nc.sync.dma_start(tab2_sb[:], words_view(tab2_words))
+        wrr_sb = at(AT_WRR, [P, 4 * R], U8, "wrr_sb")
+        nc.sync.dma_start(wrr_sb[:].bitcast(I32), words_view(wrr_words))
 
         def gather_rel_rows(h, offset):
             piece = slice(HALF * h, HALF * (h + 1))
@@ -141,7 +143,6 @@ def tile_list_ckg_none_kernel(
         for r in range(1, 4):
             nc.sync.dma_start(rel_planes[r:P:QUADRANT, :].bitcast(I32), rel_planes[8 * r:P:QUADRANT, :].bitcast(I32))
         late = at(AT_LATE, [P, COLS_LATE], U8, "late")
-        nc.sync.dma_start(late[:, LATE_WRR:LATE_WRI].bitcast(I32), words_view(wrr_words))
         nc.sync.dma_start(late[:, LATE_WRI:LATE_WEI].bitcast(I32), words_view(wri_words))
         nc.sync.dma_start(late[:, LATE_WEI:COLS_LATE].bitcast(I32).rearrange("p (a n) -> p a n", a=2),
                           wei_words.rearrange("a p n -> p a n").bitcast(I32))
@@ -182,27 +183,31 @@ def tile_list_ckg_none_kernel(
         def term_of(b, c, term):
             return own_term[b][:] if (c, term) == (1, 1) and b in own_term else terms[b][term][:, c]
 
+        def entity_pass(acc, b, e, a):
+            planes = (planes0, planes1)[a]
+            if e == 0:
+                words, scales = wer_sb[:, a, :], planes[:, COL_WER:COLS_ENT]
+            else:
+                words = late[:, LATE_WEI + 2 * R * a:LATE_WEI + 2 * R * (a + 1)]
+                scales = rel_planes[:, COL_WEI + a * R:COL_WEI + (a + 1) * R]
+            nc.tensor.matmul_mx(
+                out=acc[:], lhsT=ent_words[b][:, a].bitcast(FP4X4), lhsT_scale=planes[:, b * P:(b + 1) * P],
+                rhs=words.bitcast(FP4X4), rhs_scale=scales, start=(a == 0), stop=(a == 1))
+            if a == 1:
+                nc.scalar.copy(as_placed(factor_of(b, e), b), by_place(acc[:], b))
+
         def project_entity(b, e, number):
             acc = bank(number, [P, R])
             for a in range(2):
-                if e == 0:
-                    words, scales = wer_sb[:, a, :], ent_planes[:, COL_WER + a * R:COL_WER + (a + 1) * R]
-                else:
-                    words = late[:, LATE_WEI + 2 * R * a:LATE_WEI + 2 * R * (a + 1)]
-                    scales = rel_planes[:, COL_WEI + a * R:COL_WEI + (a + 1) * R]
-                col = COL_PASS1 * a + b * P
-                nc.tensor.matmul_mx(
-                    out=acc[:], lhsT=ent_words[b][:, a].bitcast(FP4X4), lhsT_scale=ent_planes[:, col:col + P],
-                    rhs=words.bitcast(FP4X4), rhs_scale=scales, start=(a == 0), stop=(a == 1))
-            nc.scalar.copy(as_placed(factor_of(b, e), b), by_place(acc[:], b))
+                entity_pass(acc, b, e, a)
 
         def project_relation(b, term, number):
             col = (COL_WRR, COL_WRI)[term]
-            start = (LATE_WRR, LATE_WRI)[term]
+            words = (wrr_sb[:], late[:, LATE_WRI:LATE_WEI])[term]
             acc = bank(number, [P, R])
             nc.tensor.matmul_mx(
                 out=acc[:], lhsT=rel_words[b].bitcast(FP8X4), lhsT_scale=rel_planes[:, b * P:(b + 1) * P],
-                rhs=late[:, start:start + 4 * R].bitcast(FP8X4), rhs_scale=rel_planes[:, col:col + R],
+                rhs=words.bitcast(FP8X4), rhs_scale=rel_planes[:, col:col + R],
                 start=True, stop=True)
             rel[b, term] = by_place(acc[:], b)
 
@@ -322,8 +327,10 @@ def tile_list_ckg_none_kernel(
         for first, n in ((0, 4), (4, 2), (6, 1), (7, 1)):
             new_turned(first, n)
 
-        for b in range(4):
-            project_entity(b, 0, b)
+        first_banks = [bank(b, [P, R]) for b in range(4)]
+        for a in range(2):
+            for b in range(4):
+                entity_pass(first_banks[b], b, 0, a)
         project_relation(1, 0, 6)
         copy_arr(1)
         multiply_on_gpsimd(1, HR)

@@ -28,20 +28,19 @@ ALIGN = 256
 HR, HI, BOTH = slice(0, 1), slice(1, 2), slice(0, 2)
 ON_TENSOR = (1, 3, 5, 7)
 REL_PIECES = (slice(0, 2 * P), slice(2 * P, 4 * P), slice(4 * P, J))
-COL_WER, COLS_ENT = J, J + R
-COL_WRR, COL_WRI, COL_WEI, COLS_REL = J, J + R, J + 2 * R, J + 4 * R
+COL_WER, COL_WEI, COLS_ENT = J, J + R, J + 2 * R
+COL_WRR, COL_WRI, COLS_REL = J, J + R, J + 2 * R
 COL_NI = PACK * N
 AT_TAB = 0
-AT_TAB2 = AT_TAB + 4 * T
+AT_ZEROS = AT_TAB + 4 * T - ALIGN
+AT_TAB2 = AT_ZEROS + J
 AT_GOT = AT_TAB2 + 4 * T - 3 * ALIGN
 AT_WRR = AT_TAB2 + 4 * T
-AT_REL_ROWS0 = AT_WRR + 4 * R
-AT_PAIRS_B = AT_REL_ROWS0 + HALF
-AT_PAIRS_A = AT_PAIRS_B + 4 * PIECE
-AT_LATE = AT_PAIRS_A + 4 * PIECE
-AT_REL_ROWS1 = AT_LATE - ALIGN
-AT_CAND = AT_PAIRS_A + HALF - (COL_NI + 2 * N)
-AT_IDENTITY = AT_PAIRS_A + HALF
+AT_PAIRS = AT_WRR + 4 * R
+AT_PAIRS_B = AT_PAIRS + 4 * PIECE
+AT_REL_ROWS = AT_PAIRS_B + 4 * PIECE
+AT_LATE = AT_REL_ROWS + J
+AT_IDENTITY, AT_CAND = AT_PAIRS, AT_PAIRS + HALF
 LATE_WRI, LATE_WEI, COLS_LATE = 0, 4 * R, 8 * R
 
 
@@ -80,10 +79,13 @@ def tile_list_ckg_none_kernel(
         planes0 = kept([P, COLS_ENT], U8, "planes0")
         rel_planes = kept([P, COLS_REL], U8, "rel_planes")
 
+        zeros = at(AT_ZEROS, [P, J // 4], I32, "zeros")
         clear(tab2_rows[:])
-        clear(rel_planes[:, J:COLS_REL])
+        nc.vector.memset(zeros[:], 0)
+        clear(tab_rows[QUADRANT:2 * QUADRANT, :])
+        nc.vector.tensor_copy(rel_planes[:, J:COLS_REL].bitcast(I32), zeros[:])
+        clear(tab_rows[2 * QUADRANT:P, :])
         for rows in (slice(QUADRANT, 2 * QUADRANT), slice(2 * QUADRANT, P)):
-            clear(tab_rows[rows, :])
             clear(planes0[rows, J:COLS_ENT])
 
         def both_passes(scales):
@@ -95,18 +97,18 @@ def tile_list_ckg_none_kernel(
 
         nc.sync.dma_start(list1[:], offs)
         nc.sync.dma_start(tab_rows[0:2 * ROWS, :].bitcast(I32), both_passes(tab_scales))
-        nc.sync.dma_start(planes0[0:2 * ROWS, COL_WER:COLS_ENT].bitcast(I32), both_passes(wer_scales))
+        nc.sync.dma_start(planes0[0:2 * ROWS, COL_WER:COL_WEI].bitcast(I32), both_passes(wer_scales))
+        nc.sync.dma_start(planes0[0:2 * ROWS, COL_WEI:COLS_ENT].bitcast(I32), both_passes(wei_scales))
         nc.sync.dma_start(list2[:], offs2)
         wer_sb = kept([P, 2, 2 * R], U8, "wer_sb")
         nc.sync.dma_start(wer_sb[:].bitcast(I32), wer_words.rearrange("a p n -> p a n").bitcast(I32))
+        nc.sync.dma_start(tab2_rows[0:P:8, :].bitcast(I32), tab2_scales[0].bitcast(I32))
         tab_sb = at(AT_TAB, [P, T], I32, "tab_sb")
         nc.sync.dma_start(tab_sb[:], words_view(tab_words))
-        nc.scalar.dma_start(tab2_rows[0:P:8, :].bitcast(I32), tab2_scales[0].bitcast(I32))
         load_scale_rows(rel_planes[0:P:8, COL_WRR:COL_WRI], wrr_scales)
-        load_scale_rows(rel_planes[0:P:8, COL_WRI:COL_WEI], wri_scales)
-        load_scale_rows(rel_planes[0:P:8, COL_WEI:COLS_REL], wei_scales)
+        load_scale_rows(rel_planes[0:P:8, COL_WRI:COLS_REL], wri_scales)
 
-        got_rows = at(AT_GOT, [P, AT_PAIRS_A + ALIGN - AT_GOT], U8, "got_rows")
+        got_rows = at(AT_GOT, [P, AT_REL_ROWS + ALIGN - AT_GOT], U8, "got_rows")
         gather(got_rows[:, 0:J], tab_rows[:], list1, slice(0, J))
         nc.vector.tensor_copy(planes0[:, 0:J].bitcast(I32), got_rows[:, 0:J].bitcast(I32))
         planes1 = kept([P, COLS_ENT], U8, "tab_rows")
@@ -114,40 +116,33 @@ def tile_list_ckg_none_kernel(
             nc.sync.dma_start(planes0[QUADRANT * q:QUADRANT * q + 4, :].bitcast(I32),
                               planes0[4 * q:4 * q + 4, :].bitcast(I32))
         for r in range(4):
-            queue = nc.gpsimd if r < 2 else nc.sync
-            queue.dma_start(planes1[r:P:QUADRANT, :].bitcast(I32), planes0[ROWS + r:2 * ROWS:4, :].bitcast(I32))
+            nc.sync.dma_start(planes1[r:P:QUADRANT, :].bitcast(I32), planes0[ROWS + r:2 * ROWS:4, :].bitcast(I32))
         tab2_sb = at(AT_TAB2, [P, T], I32, "tab2_sb")
         nc.sync.dma_start(tab2_sb[:], words_view(tab2_words))
         wrr_sb = at(AT_WRR, [P, 4 * R], U8, "wrr_sb")
         nc.sync.dma_start(wrr_sb[:].bitcast(I32), words_view(wrr_words))
 
-        def gather_rel_rows(h, offset):
-            piece = slice(HALF * h, HALF * (h + 1))
-            rel_rows = at(offset, [P, HALF], U8, f"rel_rows{h}")
-            gather(rel_rows[:], tab2_rows[:], list2, piece)
-            nc.vector.tensor_copy(rel_planes[:, piece].bitcast(I32), rel_rows[:].bitcast(I32))
-
         ent_words, rel_words = [], []
 
-        def gather_ent_words(h, offset):
-            pairs = at(offset, [P, PIECE], U32, f"pairs{h}")
-            gather(pairs[:], tab_sb[:].bitcast(U32), list1, slice(h * PIECE, (h + 1) * PIECE))
+        def gather_ent_words(h, offset, width=PIECE):
+            pairs = at(offset, [P, width], U32, f"pairs{h}")[:, 0:PIECE]
+            gather(pairs, tab_sb[:].bitcast(U32), list1, slice(h * PIECE, (h + 1) * PIECE))
             parted = kept([P, 2, PIECE], U16, f"parted{h}")
-            nc.vector.tensor_copy(parted[:], pairs[:].bitcast(U16).rearrange("p (j d) -> p d j", d=2))
+            nc.vector.tensor_copy(parted[:], pairs.bitcast(U16).rearrange("p (j d) -> p d j", d=2))
             ent_words.extend(parted[:, :, j0:j0 + P] for j0 in range(0, PIECE, P))
 
-        gather_rel_rows(0, AT_REL_ROWS0)
-        gather_ent_words(0, AT_PAIRS_A)
-        gather_ent_words(1, AT_PAIRS_B)
-        gather_rel_rows(1, AT_REL_ROWS1)
+        rel_rows = at(AT_REL_ROWS, [P, J + ALIGN], U8, "rel_rows")
+        gather(rel_rows[:, 0:J], tab2_rows[:], list2, slice(0, J))
+        nc.vector.tensor_copy(rel_planes[:, 0:J].bitcast(I32), rel_rows[:, 0:J].bitcast(I32))
         for r in range(1, 4):
             nc.sync.dma_start(rel_planes[r:P:QUADRANT, :].bitcast(I32), rel_planes[8 * r:P:QUADRANT, :].bitcast(I32))
         late = at(AT_LATE, [P, COLS_LATE], U8, "late")
         nc.sync.dma_start(late[:, LATE_WRI:LATE_WEI].bitcast(I32), words_view(wri_words))
         nc.sync.dma_start(late[:, LATE_WEI:COLS_LATE].bitcast(I32).rearrange("p (a n) -> p a n", a=2),
                           wei_words.rearrange("a p n -> p a n").bitcast(I32))
-        gather_ent_words(2, AT_PAIRS_B)
-        gather_ent_words(3, AT_PAIRS_A)
+        gather_ent_words(0, AT_PAIRS, 2 * PIECE)
+        for h, offset in ((1, AT_PAIRS), (2, AT_PAIRS_B), (3, AT_PAIRS)):
+            gather_ent_words(h, offset)
         identity = at(AT_IDENTITY, [P, P], F32, "identity")
         make_identity(nc, identity[:])
 
@@ -186,19 +181,19 @@ def tile_list_ckg_none_kernel(
         def entity_pass(acc, b, e, a):
             planes = (planes0, planes1)[a]
             if e == 0:
-                words, scales = wer_sb[:, a, :], planes[:, COL_WER:COLS_ENT]
+                words = wer_sb[:, a, :]
             else:
                 words = late[:, LATE_WEI + 2 * R * a:LATE_WEI + 2 * R * (a + 1)]
-                scales = rel_planes[:, COL_WEI + a * R:COL_WEI + (a + 1) * R]
+            col = (COL_WER, COL_WEI)[e]
             nc.tensor.matmul_mx(
                 out=acc[:], lhsT=ent_words[b][:, a].bitcast(FP4X4), lhsT_scale=planes[:, b * P:(b + 1) * P],
-                rhs=words.bitcast(FP4X4), rhs_scale=scales, start=(a == 0), stop=(a == 1))
-            if a == 1:
+                rhs=words.bitcast(FP4X4), rhs_scale=planes[:, col:col + R], start=(a == 1), stop=(a == 0))
+            if a == 0:
                 nc.scalar.copy(as_placed(factor_of(b, e), b), by_place(acc[:], b))
 
         def project_entity(b, e, number):
             acc = bank(number, [P, R])
-            for a in range(2):
+            for a in (1, 0):
                 entity_pass(acc, b, e, a)
 
         def project_relation(b, term, number):
@@ -327,10 +322,8 @@ def tile_list_ckg_none_kernel(
         for first, n in ((0, 4), (4, 2), (6, 1), (7, 1)):
             new_turned(first, n)
 
-        first_banks = [bank(b, [P, R]) for b in range(4)]
-        for a in range(2):
-            for b in range(4):
-                entity_pass(first_banks[b], b, 0, a)
+        for b in range(4):
+            project_entity(b, 0, b)
         project_relation(1, 0, 6)
         copy_arr(1)
         multiply_on_gpsimd(1, HR)
@@ -364,7 +357,7 @@ def tile_list_ckg_none_kernel(
         project_entity(4, 1, 7)
         project_relation(4, 0, 4)
         project_relation(4, 1, 3)
-        turn_terms(1, HR, (6,))
+        turn_terms(1, HR, (6,), (1, 0))
         project_entity(5, 1, 7)
         turn_terms(1, HI, (5,))
         new_terms(3)
@@ -380,8 +373,8 @@ def tile_list_ckg_none_kernel(
         turn_terms(3, HI, (5,), (1, 0))
         turn_pairs(0, 0)
         project_relation(6, 1, 3)
-        project_entity(7, 0, 6)
         turn_pairs(2, 7)
+        project_entity(7, 0, 6)
         new_terms(5)
         new_terms(6, ari_tag="last_add")
         multiply_block(5)

@@ -25,6 +25,7 @@ PER_COL = 16
 HALF = J // 2
 PIECE = 2 * P
 ALIGN = 256
+TAB2_FIRST = 3 * T // 8
 HR, HI, BOTH = slice(0, 1), slice(1, 2), slice(0, 2)
 ON_TENSOR = (1, 3, 5, 7)
 REL_PIECES = (slice(0, 2 * P), slice(2 * P, 4 * P), slice(4 * P, J))
@@ -112,13 +113,14 @@ def tile_list_ckg_none_kernel(
         gather(got_rows[:, 0:J], tab_rows[:], list1, slice(0, J))
         nc.vector.tensor_copy(planes0[:, 0:J].bitcast(I32), got_rows[:, 0:J].bitcast(I32))
         planes1 = kept([P, COLS_ENT], U8, "tab_rows")
-        for q in (2, 1, 3):
-            nc.sync.dma_start(planes0[QUADRANT * q:QUADRANT * q + 4, :].bitcast(I32),
-                              planes0[4 * q:4 * q + 4, :].bitcast(I32))
         for r in range(4):
             nc.sync.dma_start(planes1[r:P:QUADRANT, :].bitcast(I32), planes0[ROWS + r:2 * ROWS:4, :].bitcast(I32))
         tab2_sb = at(AT_TAB2, [P, T], I32, "tab2_sb")
-        nc.sync.dma_start(tab2_sb[:], words_view(tab2_words))
+        nc.sync.dma_start(tab2_sb[:, 0:TAB2_FIRST], words_view(tab2_words)[:, 0:TAB2_FIRST])
+        for q in (2, 1, 3):
+            nc.sync.dma_start(planes0[QUADRANT * q:QUADRANT * q + 4, :].bitcast(I32),
+                              planes0[4 * q:4 * q + 4, :].bitcast(I32))
+        nc.sync.dma_start(tab2_sb[:, TAB2_FIRST:T], words_view(tab2_words)[:, TAB2_FIRST:T])
         wrr_sb = at(AT_WRR, [P, 4 * R], U8, "wrr_sb")
         nc.sync.dma_start(wrr_sb[:].bitcast(I32), words_view(wrr_words))
 
@@ -178,7 +180,7 @@ def tile_list_ckg_none_kernel(
         def term_of(b, c, term):
             return own_term[b][:] if (c, term) == (1, 1) and b in own_term else terms[b][term][:, c]
 
-        def entity_pass(acc, b, e, a):
+        def entity_pass(acc, b, e, a, first):
             planes = (planes0, planes1)[a]
             if e == 0:
                 words = wer_sb[:, a, :]
@@ -187,14 +189,14 @@ def tile_list_ckg_none_kernel(
             col = (COL_WER, COL_WEI)[e]
             nc.tensor.matmul_mx(
                 out=acc[:], lhsT=ent_words[b][:, a].bitcast(FP4X4), lhsT_scale=planes[:, b * P:(b + 1) * P],
-                rhs=words.bitcast(FP4X4), rhs_scale=planes[:, col:col + R], start=(a == 1), stop=(a == 0))
-            if a == 0:
+                rhs=words.bitcast(FP4X4), rhs_scale=planes[:, col:col + R], start=first, stop=not first)
+            if not first:
                 nc.scalar.copy(as_placed(factor_of(b, e), b), by_place(acc[:], b))
 
         def project_entity(b, e, number):
             acc = bank(number, [P, R])
-            for a in (1, 0):
-                entity_pass(acc, b, e, a)
+            for a in range(2):
+                entity_pass(acc, b, e, a, a == 0)
 
         def project_relation(b, term, number):
             col = (COL_WRR, COL_WRI)[term]
@@ -322,7 +324,11 @@ def tile_list_ckg_none_kernel(
         for first, n in ((0, 4), (4, 2), (6, 1), (7, 1)):
             new_turned(first, n)
 
-        for b in range(4):
+        first_banks = [bank(b, [P, R]) for b in range(2)]
+        for a in (1, 0):
+            for b in range(2):
+                entity_pass(first_banks[b], b, 0, a, a == 1)
+        for b in (2, 3):
             project_entity(b, 0, b)
         project_relation(1, 0, 6)
         copy_arr(1)

@@ -93,8 +93,7 @@ def tile_list_ckg_none_kernel(
             return scales.rearrange("a q n -> (a q) n").bitcast(I32)
 
         def load_scale_rows(rows, scales):
-            nc.gpsimd.dma_start(rows.bitcast(I32).rearrange("q (a n) -> q a n", a=scales.shape[0]),
-                                scales.rearrange("a q n -> q a n").bitcast(I32))
+            nc.sync.dma_start(rows.bitcast(I32), scales[0].bitcast(I32))
 
         nc.sync.dma_start(list1[:], offs)
         nc.sync.dma_start(tab_rows[0:2 * ROWS, :].bitcast(I32), both_passes(tab_scales))

@@ -253,7 +253,7 @@ def tile_list_ckg_none_kernel(
                 for c in range(2):
                     turned[b, c] = group[first][:, c, b - first]
 
-        def turn_pairs(b, number, parts=BOTH):
+        def turn_pairs(b, number, parts=BOTH, copy=nc.scalar.copy):
             n = parts.stop - parts.start
             first = max(f for f in group if f <= b)
             target = group[first][:, parts, b - first]
@@ -262,7 +262,7 @@ def tile_list_ckg_none_kernel(
             for c in range(n):
                 for u in range(2):
                     nc.tensor.transpose(acc[:, c, u, :], words[:, parts.start + c, u, :], identity[:])
-            nc.scalar.copy(
+            copy(
                 target.rearrange("p c j t -> p c (j t)").bitcast(F32).rearrange("p c (j u) -> p c j u", u=2),
                 acc[:].rearrange("p c u j -> p c j u"))
 
@@ -308,13 +308,13 @@ def tile_list_ckg_none_kernel(
         def store(b, n, result):
             nc.sync.dma_start(out[:, b * P:(b + n) * P].rearrange("(g n) j -> n g j", g=2), result[:])
 
-        def score(b, n, number):
+        def score(b, n, number, copy=nc.scalar.copy):
             acc = bank(number, [P, 2, n * P])
             for g in range(2):
                 for c in range(2):
                     score_pass(acc[:, g, :], b, n, g, c)
             result = kept([P, 2, n * P], F32, f"result{b}")
-            nc.scalar.copy(result[:], acc[:])
+            copy(result[:], acc[:])
             store(b, n, result)
 
         for b in range(J // P):
@@ -336,7 +336,7 @@ def tile_list_ckg_none_kernel(
         project_relation(2, 0, 0)
         copy_arr(2)
         multiply_on_gpsimd(2, HR)
-        for b, number in ((4, 4), (5, 5), (6, 1)):
+        for b, number in ((4, 4), (5, 5)):
             project_entity(b, 0, number)
         project_relation(0, 1, 2)
         project_relation(1, 1, 3)
@@ -362,64 +362,64 @@ def tile_list_ckg_none_kernel(
         project_entity(4, 1, 7)
         project_relation(4, 0, 4)
         project_relation(4, 1, 3)
-        turn_terms(1, HR, (6,), (1, 0))
-        project_entity(5, 1, 7)
-        turn_terms(1, HI, (5,))
+        turn_terms(1, HR, (0,), (1, 0))
+        project_entity(5, 1, 5)
+        turn_terms(1, HI, (7,))
         new_terms(3)
         multiply_block(3)
         project_relation(5, 0, 1)
+        project_entity(6, 0, 0)
         turn_terms(3, HR, (6,), (1, 0))
+        turn_pairs(0, 5)
         project_relation(5, 1, 2)
         project_entity(6, 1, 7)
         new_terms(4, ari_tag="before_pause")
         multiply_block(4)
         combine(4)
         project_relation(6, 0, 4)
-        turn_terms(3, HI, (5,), (1, 0))
-        turn_pairs(0, 0)
+        turn_terms(3, HI, (0,), (1, 0))
+        turn_pairs(2, 5)
         project_relation(6, 1, 3)
-        turn_pairs(2, 7)
         project_entity(7, 0, 6)
         new_terms(5)
         new_terms(6, ari_tag="last_add")
         multiply_block(5)
         project_relation(7, 0, 1)
-        turn_terms(5, HR, (5,), (1, 0))
+        turn_terms(5, HR, (7,), (1, 0))
         project_relation(7, 1, 2)
         project_entity(7, 1, 0)
         turn_terms(5, HI, (6,), (1, 0))
         for c, term in ((0, 0), (0, 1), (1, 0)):
             product(6, c, term)
-        turn_pairs(4, 7)
+        turn_pairs(4, 5)
 
         new_codes((0, 1, 2, 3), "before_pause", "aei6")
         quantise(0, 4)
         product(6, 1, 1)
         combine_parts(6, "turned0")
-        score(0, 2, 5)
+        score(0, 2, 7)
+        score(2, 2, 0)
 
         new_terms(7)
         multiply_block(7)
         last_turns = [bank(number, [P, PACK, P]) for number in (4, 3)]
         turn_term(last_turns[0], 7, 0, 0, True)
-        score(2, 2, 1)
         turn_term(last_turns[1], 7, 1, 0, True)
-        turn_pairs(6, 0, HR)
+        turn_pairs(6, 6, HR)
         turn_term(last_turns[0], 7, 0, 1, False)
-        turn_pairs(6, 6, HI)
-        turn_term(last_turns[1], 7, 1, 1, False)
-
+        round_turned(last_turns[0], 7, 0)
         new_codes((4, 5, 6, 7), "last_add", "planes_end")
         quantise(4, 2)
-        for c, copy in enumerate((nc.vector.tensor_copy, nc.scalar.copy)):
-            round_turned(last_turns[c], 7, c, copy)
-        score(4, 2, 7)
-        quantise(6, 1)
-        score(6, 1, 5)
+        turn_term(last_turns[1], 7, 1, 1, False)
+        round_turned(last_turns[1], 7, 1)
+        turn_pairs(6, 1, HI, nc.vector.tensor_copy)
+        score(4, 2, 5)
         quantise(7, 1, HR)
-        last_sums = [bank(number, [P, P]) for number in (2, 1)]
+        quantise(6, 1)
+        last_sums = [bank(number, [P, P]) for number in (2, 6)]
         for g in range(2):
             score_pass(last_sums[g][:], 7, 1, g, 0)
+        score(6, 1, 7, nc.vector.tensor_copy)
         quantise(7, 1, HI)
         for g in range(2):
             score_pass(last_sums[g][:], 7, 1, g, 1)

@@ -25,6 +25,7 @@ PER_COL = 16
 HALF = J // 2
 PIECE = 2 * P
 ALIGN = 256
+WARM_UPS = 3
 TAB2_FIRST = 3 * T // 8
 HR, HI, BOTH = slice(0, 1), slice(1, 2), slice(0, 2)
 ON_TENSOR = (1, 3, 5, 7)
@@ -135,6 +136,11 @@ def tile_list_ckg_none_kernel(
         rel_rows = at(AT_REL_ROWS, [P, J + ALIGN], U8, "rel_rows")
         gather(rel_rows[:, 0:J], tab2_rows[:], list2, slice(0, J))
         nc.vector.tensor_copy(rel_planes[:, 0:J].bitcast(I32), rel_rows[:, 0:J].bitcast(I32))
+        warm = bank(7, [P, R])
+        for _ in range(WARM_UPS):
+            nc.tensor.matmul_mx(
+                out=warm[:], lhsT=wer_sb[:, 0, 0:2 * P].bitcast(FP4X4), lhsT_scale=rel_planes[:, HALF:HALF + P],
+                rhs=wer_sb[:, 1, :].bitcast(FP4X4), rhs_scale=rel_planes[:, 0:R], start=True, stop=True)
         for r in range(1, 4):
             nc.sync.dma_start(rel_planes[r:P:QUADRANT, :].bitcast(I32), rel_planes[8 * r:P:QUADRANT, :].bitcast(I32))
         late = at(AT_LATE, [P, COLS_LATE], U8, "late")
@@ -336,7 +342,7 @@ def tile_list_ckg_none_kernel(
         project_relation(2, 0, 0)
         copy_arr(2)
         multiply_on_gpsimd(2, HR)
-        for b, number in ((4, 4), (5, 5)):
+        for b, number in ((4, 4), (5, 5), (6, 1)):
             project_entity(b, 0, number)
         project_relation(0, 1, 2)
         project_relation(1, 1, 3)
@@ -368,7 +374,6 @@ def tile_list_ckg_none_kernel(
         new_terms(3)
         multiply_block(3)
         project_relation(5, 0, 1)
-        project_entity(6, 0, 0)
         turn_terms(3, HR, (6,), (1, 0))
         turn_pairs(0, 5)
         project_relation(5, 1, 2)

@@ -25,7 +25,6 @@ PER_COL = 16
 HALF = J // 2
 PIECE = 2 * P
 ALIGN = 256
-WARM_UPS = 3
 TAB2_FIRST = 3 * T // 8
 HR, HI, BOTH = slice(0, 1), slice(1, 2), slice(0, 2)
 ON_TENSOR = (1, 3, 5, 7)
@@ -136,11 +135,6 @@ def tile_list_ckg_none_kernel(
         rel_rows = at(AT_REL_ROWS, [P, J + ALIGN], U8, "rel_rows")
         gather(rel_rows[:, 0:J], tab2_rows[:], list2, slice(0, J))
         nc.vector.tensor_copy(rel_planes[:, 0:J].bitcast(I32), rel_rows[:, 0:J].bitcast(I32))
-        warm = bank(7, [P, R])
-        for _ in range(WARM_UPS):
-            nc.tensor.matmul_mx(
-                out=warm[:], lhsT=wer_sb[:, 0, 0:2 * P].bitcast(FP4X4), lhsT_scale=rel_planes[:, HALF:HALF + P],
-                rhs=wer_sb[:, 1, :].bitcast(FP4X4), rhs_scale=rel_planes[:, 0:R], start=True, stop=True)
         for r in range(1, 4):
             nc.sync.dma_start(rel_planes[r:P:QUADRANT, :].bitcast(I32), rel_planes[8 * r:P:QUADRANT, :].bitcast(I32))
         late = at(AT_LATE, [P, COLS_LATE], U8, "late")

@@ -16,6 +16,7 @@ FP8X4 = mybir.dt.float8_e4m3fn_x4
 FP4X4 = mybir.dt.float4_e2m1fn_x4
 MULT = mybir.AluOpType.mult
 ADD = mybir.AluOpType.add
+SUBTRACT = mybir.AluOpType.subtract
 
 P = 128
 PACK = 4
@@ -28,13 +29,13 @@ ALIGN = 256
 TAB2_FIRST = 3 * T // 8
 HR, HI, BOTH = slice(0, 1), slice(1, 2), slice(0, 2)
 ON_TENSOR = (1, 3, 5, 7)
+IN_HALVES = 6
 REL_PIECES = (slice(0, 2 * P), slice(2 * P, 4 * P), slice(4 * P, J))
 COL_WER, COL_WEI, COLS_ENT = J, J + R, J + 2 * R
 COL_WRR, COL_WRI, COLS_REL = J, J + R, J + 2 * R
 COL_NI = PACK * N
 AT_TAB = 0
-AT_ZEROS = AT_TAB + 4 * T - ALIGN
-AT_TAB2 = AT_ZEROS + J
+AT_TAB2 = AT_TAB + 4 * T
 AT_GOT = AT_TAB2 + 4 * T - 3 * ALIGN
 AT_WRR = AT_TAB2 + 4 * T
 AT_PAIRS = AT_WRR + 4 * R
@@ -80,14 +81,9 @@ def tile_list_ckg_none_kernel(
         planes0 = kept([P, COLS_ENT], U8, "planes0")
         rel_planes = kept([P, COLS_REL], U8, "rel_planes")
 
-        zeros = at(AT_ZEROS, [P, J // 4], I32, "zeros")
         clear(tab2_rows[:])
-        nc.vector.memset(zeros[:], 0)
         clear(tab_rows[QUADRANT:2 * QUADRANT, :])
-        nc.vector.tensor_copy(rel_planes[:, J:COLS_REL].bitcast(I32), zeros[:])
         clear(tab_rows[2 * QUADRANT:P, :])
-        for rows in (slice(QUADRANT, 2 * QUADRANT), slice(2 * QUADRANT, P)):
-            clear(planes0[rows, J:COLS_ENT])
 
         def both_passes(scales):
             return scales.rearrange("a q n -> (a q) n").bitcast(I32)
@@ -213,7 +209,7 @@ def tile_list_ckg_none_kernel(
         def product(b, c, term):
             target = as_placed(term_of(b, c, term), b)
             factor = as_placed(factor_of(b, (c + term) % 2), b)
-            if (c, term) != (0, 1):
+            if (c, term) != (0, 1) or b == IN_HALVES:
                 nc.vector.tensor_tensor(target, factor, rel[b, term], MULT)
             elif b in ON_TENSOR:
                 nc.vector.scalar_tensor_tensor(target, factor, -1.0, rel[b, term], MULT, MULT)
@@ -245,7 +241,7 @@ def tile_list_ckg_none_kernel(
         def combine_parts(b, tag):
             summed[b] = kept([P, 2, R], BF16, tag)
             for c in range(2):
-                nc.gpsimd.tensor_tensor(summed[b][:, c], term_of(b, c, 0), term_of(b, c, 1), ADD)
+                nc.gpsimd.tensor_tensor(summed[b][:, c], term_of(b, c, 0), term_of(b, c, 1), (SUBTRACT, ADD)[c])
 
         def new_turned(first, n):
             group[first] = kept([P, 2, n, P, PACK], BF16, f"turned{first}")

from contextlib import ExitStack

import concourse.mybir as mybir
from concourse.masks import make_identity

K, L, R, N, T, J = 1024, 512, 512, 256, 4096, 1024
FLOPS = 2 * J * (2 * K * R + 2 * L * R + 2 * R * N)

F32 = mybir.dt.float32
BF16 = mybir.dt.bfloat16
I32 = mybir.dt.int32
U32 = mybir.dt.uint32
U16 = mybir.dt.uint16
U8 = mybir.dt.uint8
FP8X4 = mybir.dt.float8_e4m3fn_x4
FP4X4 = mybir.dt.float4_e2m1fn_x4
MULT = mybir.AluOpType.mult
ADD = mybir.AluOpType.add
SUBTRACT = mybir.AluOpType.subtract

P = 128
PACK = 4
QUADRANT = 32
ROWS = 16
PER_COL = 16
HALF = J // 2
PIECE = 2 * P
ALIGN = 256
TAB2_FIRST = 3 * T // 8
HR, HI, BOTH = slice(0, 1), slice(1, 2), slice(0, 2)
ON_TENSOR = (1, 3, 5, 7)
IN_HALVES = 6
REL_PIECES = (slice(0, 2 * P), slice(2 * P, 4 * P), slice(4 * P, J))
COL_WER, COL_WEI, COLS_ENT = J, J + R, J + 2 * R
COL_WRR, COL_WRI, COLS_REL = J, J + R, J + 2 * R
COL_NI = PACK * N
AT_TAB = 0
AT_TAB2 = AT_TAB + 4 * T
AT_GOT = AT_TAB2 + 4 * T - 3 * ALIGN
AT_WRR = AT_TAB2 + 4 * T
AT_PAIRS = AT_WRR + 4 * R
AT_PAIRS_B = AT_PAIRS + 4 * PIECE
AT_REL_ROWS = AT_PAIRS_B + 4 * PIECE
AT_LATE = AT_REL_ROWS + J
AT_IDENTITY, AT_CAND = AT_PAIRS, AT_PAIRS + HALF
LATE_WRI, LATE_WEI, COLS_LATE = 0, 4 * R, 8 * R


def tile_list_ckg_none_kernel(
    tc, tab_words, tab_scales, tab2_words, tab2_scales, wer_words, wer_scales, wei_words, wei_scales,
    wrr_words, wrr_scales, wri_words, wri_scales, nr_words, nr_scales, ni_words, ni_scales, offs, offs2, out,
):
    nc = tc.nc
    with ExitStack() as ctx:
        keep = ctx.enter_context(tc.tile_pool(name="keep", bufs=1))
        placed = ctx.enter_context(tc.tile_pool(name="placed", bufs=1))
        psum = ctx.enter_context(tc.psum_pool(name="psum", bufs=1))

        def kept(shape, dtype, tag):
            return keep.tile(shape, dtype, name=tag, tag=tag, align_bytes=ALIGN)

        def at(offset, shape, dtype, name):
            return placed.tile(shape, dtype, name=name, offset=offset, align_bytes=ALIGN)

        def bank(number, shape):
            return psum.tile(shape, F32, name=f"bank{number}", bufs=1)

        def words_view(words):
            return words.rearrange("a p n i -> p (a n i)").bitcast(I32)

        def gather(target, window, offsets, piece):
            nc.vector.tensor_copy(target, window.indirect(offsets[:, piece.start // PER_COL:piece.stop // PER_COL]))

        def clear(view):
            nc.vector.memset(view.bitcast(I32), 0)

        list1 = keep.tile([P, J // PER_COL], U16, name="list1")
        list2 = keep.tile([P, J // PER_COL], U16, name="list2")
        tab_rows = kept([P, T], U8, "tab_rows")
        tab2_rows = kept([P, T], U8, "tab2_rows")
        planes0 = kept([P, COLS_ENT], U8, "planes0")
        rel_planes = kept([P, COLS_REL], U8, "rel_planes")

        clear(tab2_rows[:])
        clear(tab_rows[QUADRANT:2 * QUADRANT, :])
        clear(tab_rows[2 * QUADRANT:P, :])

        def both_passes(scales):
            return scales.rearrange("a q n -> (a q) n").bitcast(I32)

        def load_scale_rows(rows, scales):
            nc.sync.dma_start(rows.bitcast(I32), scales[0].bitcast(I32))

        nc.sync.dma_start(list1[:], offs)
        nc.sync.dma_start(tab_rows[0:2 * ROWS, :].bitcast(I32), both_passes(tab_scales))
        nc.sync.dma_start(planes0[0:2 * ROWS, COL_WER:COL_WEI].bitcast(I32), both_passes(wer_scales))
        nc.sync.dma_start(planes0[0:2 * ROWS, COL_WEI:COLS_ENT].bitcast(I32), both_passes(wei_scales))
        nc.sync.dma_start(list2[:], offs2)
        wer_sb = kept([P, 2, 2 * R], U8, "wer_sb")
        nc.sync.dma_start(wer_sb[:].bitcast(I32), wer_words.rearrange("a p n -> p a n").bitcast(I32))
        nc.sync.dma_start(tab2_rows[0:P:8, :].bitcast(I32), tab2_scales[0].bitcast(I32))
        tab_sb = at(AT_TAB, [P, T], I32, "tab_sb")
        nc.sync.dma_start(tab_sb[:], words_view(tab_words))
        load_scale_rows(rel_planes[0:P:8, COL_WRR:COL_WRI], wrr_scales)
        load_scale_rows(rel_planes[0:P:8, COL_WRI:COLS_REL], wri_scales)

        got_rows = at(AT_GOT, [P, AT_REL_ROWS + ALIGN - AT_GOT], U8, "got_rows")
        gather(got_rows[:, 0:J], tab_rows[:], list1, slice(0, J))
        nc.vector.tensor_copy(planes0[:, 0:J].bitcast(I32), got_rows[:, 0:J].bitcast(I32))
        planes1 = kept([P, COLS_ENT], U8, "tab_rows")
        for r in range(4):
            nc.sync.dma_start(planes1[r:P:QUADRANT, :].bitcast(I32), planes0[ROWS + r:2 * ROWS:4, :].bitcast(I32))
        tab2_sb = at(AT_TAB2, [P, T], I32, "tab2_sb")
        nc.sync.dma_start(tab2_sb[:, 0:TAB2_FIRST], words_view(tab2_words)[:, 0:TAB2_FIRST])
        for q in (2, 1, 3):
            nc.sync.dma_start(planes0[QUADRANT * q:QUADRANT * q + 4, :].bitcast(I32),
                              planes0[4 * q:4 * q + 4, :].bitcast(I32))
        nc.sync.dma_start(tab2_sb[:, TAB2_FIRST:T], words_view(tab2_words)[:, TAB2_FIRST:T])
        wrr_sb = at(AT_WRR, [P, 4 * R], U8, "wrr_sb")
        nc.sync.dma_start(wrr_sb[:].bitcast(I32), words_view(wrr_words))

        ent_words, rel_words = [], []

        def gather_ent_words(h, offset, width=PIECE):
            pairs = at(offset, [P, width], U32, f"pairs{h}")[:, 0:PIECE]
            gather(pairs, tab_sb[:].bitcast(U32), list1, slice(h * PIECE, (h + 1) * PIECE))
            parted = kept([P, 2, PIECE], U16, f"parted{h}")
            nc.vector.tensor_copy(parted[:], pairs.bitcast(U16).rearrange("p (j d) -> p d j", d=2))
            ent_words.extend(parted[:, :, j0:j0 + P] for j0 in range(0, PIECE, P))

        rel_rows = at(AT_REL_ROWS, [P, J + ALIGN], U8, "rel_rows")
        gather(rel_rows[:, 0:J], tab2_rows[:], list2, slice(0, J))
        nc.vector.tensor_copy(rel_planes[:, 0:J].bitcast(I32), rel_rows[:, 0:J].bitcast(I32))
        for r in range(1, 4):
            nc.sync.dma_start(rel_planes[r:P:QUADRANT, :].bitcast(I32), rel_planes[8 * r:P:QUADRANT, :].bitcast(I32))
        late = at(AT_LATE, [P, COLS_LATE], U8, "late")
        nc.sync.dma_start(late[:, LATE_WRI:LATE_WEI].bitcast(I32), words_view(wri_words))
        nc.sync.dma_start(late[:, LATE_WEI:COLS_LATE].bitcast(I32).rearrange("p (a n) -> p a n", a=2),
                          wei_words.rearrange("a p n -> p a n").bitcast(I32))
        gather_ent_words(0, AT_PAIRS, 2 * PIECE)
        for h, offset in ((1, AT_PAIRS), (2, AT_PAIRS_B), (3, AT_PAIRS)):
            gather_ent_words(h, offset)
        identity = at(AT_IDENTITY, [P, P], F32, "identity")
        make_identity(nc, identity[:])

        cand_sb = at(AT_CAND, [P, COL_NI + 2 * N], U8, "cand_sb")
        nc.sync.dma_start(cand_sb[:, 0:COL_NI].bitcast(I32), words_view(nr_words))
        nc.sync.dma_start(cand_sb[:, COL_NI:COL_NI + 2 * N].bitcast(I32), ni_words[0].bitcast(I32))
        cand_planes = at(AT_TAB, [P, 2, N], U8, "cand_planes")
        for c, cand_scales in enumerate((nr_scales, ni_scales)):
            for r in range(4):
                nc.sync.dma_start(cand_planes[r:P:QUADRANT, c, :].bitcast(I32),
                                  cand_scales[0, r:ROWS:4, :].bitcast(I32))
        for h, piece in enumerate(REL_PIECES):
            picked = kept([P, piece.stop - piece.start], U32, f"picked{h}")
            gather(picked[:], tab2_sb[:].bitcast(U32), list2, piece)
            rel_words.extend(picked[:, j0:j0 + P] for j0 in range(0, piece.stop - piece.start, P))

        def by_place(view, b):
            if b in ON_TENSOR:
                return view.rearrange("j (m t) -> j t m", t=PACK)
            return view.rearrange("j (m u e) -> j u m e", u=2, e=2)

        def as_placed(view, b):
            if b in ON_TENSOR:
                return view.rearrange("j (t m) -> j t m", t=PACK)
            return view.rearrange("j (u m e) -> j u m e", u=2, e=2)

        ent, own_aei, rel, terms, own_term, summed, turned, quant = {}, {}, {}, {}, {}, {}, {}, {}
        group = {}

        def factor_of(b, e):
            return own_aei[b][:] if e == 1 and b in own_aei else ent[b][:, e]

        def term_of(b, c, term):
            return own_term[b][:] if (c, term) == (1, 1) and b in own_term else terms[b][term][:, c]

        def entity_pass(acc, b, e, a, first):
            planes = (planes0, planes1)[a]
            if e == 0:
                words = wer_sb[:, a, :]
            else:
                words = late[:, LATE_WEI + 2 * R * a:LATE_WEI + 2 * R * (a + 1)]
            col = (COL_WER, COL_WEI)[e]
            nc.tensor.matmul_mx(
                out=acc[:], lhsT=ent_words[b][:, a].bitcast(FP4X4), lhsT_scale=planes[:, b * P:(b + 1) * P],
                rhs=words.bitcast(FP4X4), rhs_scale=planes[:, col:col + R], start=first, stop=not first)
            if not first:
                nc.scalar.copy(as_placed(factor_of(b, e), b), by_place(acc[:], b))

        def project_entity(b, e, number):
            acc = bank(number, [P, R])
            for a in range(2):
                entity_pass(acc, b, e, a, a == 0)

        def project_relation(b, term, number):
            col = (COL_WRR, COL_WRI)[term]
            words = (wrr_sb[:], late[:, LATE_WRI:LATE_WEI])[term]
            acc = bank(number, [P, R])
            nc.tensor.matmul_mx(
                out=acc[:], lhsT=rel_words[b].bitcast(FP8X4), lhsT_scale=rel_planes[:, b * P:(b + 1) * P],
                rhs=words.bitcast(FP8X4), rhs_scale=rel_planes[:, col:col + R],
                start=True, stop=True)
            rel[b, term] = by_place(acc[:], b)

        def new_terms(b, arr_tag=None, ari_tag=None):
            terms[b] = (kept([P, 2, R], F32, arr_tag or f"with_arr{b}"), kept([P, 2, R], F32, ari_tag or f"with_ari{b}"))

        def product(b, c, term):
            target = as_placed(term_of(b, c, term), b)
            factor = as_placed(factor_of(b, (c + term) % 2), b)
            if (c, term) != (0, 1) or b == IN_HALVES:
                nc.vector.tensor_tensor(target, factor, rel[b, term], MULT)
            elif b in ON_TENSOR:
                nc.vector.scalar_tensor_tensor(target, factor, -1.0, rel[b, term], MULT, MULT)
            else:
                for u in range(2):
                    nc.vector.scalar_tensor_tensor(target[:, u], factor[:, u], -1.0, rel[b, term][:, u], MULT, MULT)

        def multiply(b, which=(0, 1)):
            for term in which:
                for c in range(2):
                    product(b, c, term)

        arr_sb = {}

        def copy_arr(b):
            arr_sb[b] = kept([P, R], F32, f"arr_sb{b}")
            nc.scalar.copy(as_placed(arr_sb[b][:], b), rel[b, 0])
            new_terms(b)

        def multiply_on_gpsimd(b, parts):
            n = parts.stop - parts.start
            nc.gpsimd.tensor_tensor(terms[b][0][:, parts], ent[b][:, parts],
                                    arr_sb[b][:].unsqueeze(1).to_broadcast([P, n, R]), MULT)

        def combine(b, tag=None):
            summed[b] = kept([P, 2, R], BF16, tag or f"summed{b}")
            nc.gpsimd.tensor_tensor(summed[b][:], terms[b][0][:], terms[b][1][:], ADD)

        def combine_parts(b, tag):
            summed[b] = kept([P, 2, R], BF16, tag)
            for c in range(2):
                nc.gpsimd.tensor_tensor(summed[b][:, c], term_of(b, c, 0), term_of(b, c, 1), (SUBTRACT, ADD)[c])

        def new_turned(first, n):
            group[first] = kept([P, 2, n, P, PACK], BF16, f"turned{first}")
            for b in range(first, first + n):
                for c in range(2):
                    turned[b, c] = group[first][:, c, b - first]

        def turn_pairs(b, number, parts=BOTH, copy=nc.scalar.copy):
            n = parts.stop - parts.start
            first = max(f for f in group if f <= b)
            target = group[first][:, parts, b - first]
            acc = bank(number, [P, n, 2, P])
            words = summed[b][:].rearrange("j c r -> j (c r)").bitcast(F32).rearrange("j (c u p) -> j c u p", c=2, u=2)
            for c in range(n):
                for u in range(2):
                    nc.tensor.transpose(acc[:, c, u, :], words[:, parts.start + c, u, :], identity[:])
            copy(
                target.rearrange("p c j t -> p c (j t)").bitcast(F32).rearrange("p c (j u) -> p c j u", u=2),
                acc[:].rearrange("p c u j -> p c j u"))

        def turn_term(acc, b, c, term, first):
            for t in range(PACK):
                nc.tensor.matmul(acc[:, t, :], term_of(b, c, term)[:, t * P:(t + 1) * P], identity[:],
                                 start=(first and t == 0), stop=(not first and t == PACK - 1), is_transpose=True)

        def round_turned(acc, b, c, copy=nc.scalar.copy):
            copy(turned[b, c], acc[:].rearrange("p t j -> p j t"))

        def turn_terms(b, parts, numbers, order=(0, 1)):
            for c, number in zip(range(parts.start, parts.stop), numbers):
                acc = bank(number, [P, PACK, P])
                for term in order:
                    turn_term(acc, b, c, term, term == order[0])
                round_turned(acc, b, c)

        def new_codes(blocks, codes_tag, planes_tag):
            codes = kept([P, 2, len(blocks) * P], U32, codes_tag)
            planes = kept([P, 2, len(blocks) * P], U8, planes_tag)
            for i, b in enumerate(blocks):
                quant[b] = (codes, planes, i * P)

        def quantise(b, n, parts=BOTH):
            codes, planes, j0 = quant[b]
            for c in range(parts.start, parts.stop):
                nc.vector.quantize_mx(out=codes[:, c, j0:j0 + n * P].bitcast(FP8X4),
                                      scales=planes[:, c, j0:j0 + n * P],
                                      in_=group[b][:, c].rearrange("p b j t -> p (b j t)"))

        def score_pass(acc, b, n, g, c):
            codes, planes, j0 = quant[b]
            if c == 0:
                words = cand_sb[:, PACK * P * g:PACK * P * (g + 1)].bitcast(FP8X4)
            else:
                words = cand_sb[:, COL_NI + 2 * P * g:COL_NI + 2 * P * (g + 1)].bitcast(FP4X4)
            nc.tensor.matmul_mx(
                out=acc, lhsT=words, lhsT_scale=cand_planes[:, c, g * P:(g + 1) * P],
                rhs=codes[:, c, j0:j0 + n * P].bitcast(FP8X4), rhs_scale=planes[:, c, j0:j0 + n * P],
                start=(c == 0), stop=(c == 1))

        def store(b, n, result):
            nc.sync.dma_start(out[:, b * P:(b + n) * P].rearrange("(g n) j -> n g j", g=2), result[:])

        def score(b, n, number, copy=nc.scalar.copy):
            acc = bank(number, [P, 2, n * P])
            for g in range(2):
                for c in range(2):
                    score_pass(acc[:, g, :], b, n, g, c)
            result = kept([P, 2, n * P], F32, f"result{b}")
            copy(result[:], acc[:])
            store(b, n, result)

        for b in range(J // P):
            ent[b] = kept([P, 2, R], F32, f"ent{b}")
        own_aei[6] = kept([P, R], F32, "aei6")
        for first, n in ((0, 4), (4, 2), (6, 1), (7, 1)):
            new_turned(first, n)

        first_banks = [bank(b, [P, R]) for b in range(2)]
        for a in (1, 0):
            for b in range(2):
                entity_pass(first_banks[b], b, 0, a, a == 1)
        for b in (2, 3):
            project_entity(b, 0, b)
        project_relation(1, 0, 6)
        copy_arr(1)
        multiply_on_gpsimd(1, HR)
        project_relation(0, 0, 7)
        project_relation(2, 0, 0)
        copy_arr(2)
        multiply_on_gpsimd(2, HR)
        for b, number in ((4, 4), (5, 5), (6, 1)):
            project_entity(b, 0, number)
        project_relation(0, 1, 2)
        project_relation(1, 1, 3)
        project_relation(2, 1, 5)
        project_entity(0, 1, 4)
        project_entity(1, 1, 6)
        multiply_on_gpsimd(1, HI)
        project_entity(2, 1, 0)
        multiply_on_gpsimd(2, HI)
        project_relation(3, 0, 1)

        def multiply_block(b):
            for c, term in ((0, 0), (1, 0), (0, 1), (1, 1)):
                product(b, c, term)

        new_terms(0)
        for b, c, term in ((0, 0, 0), (0, 1, 1), (1, 1, 1), (2, 1, 1), (0, 1, 0), (0, 0, 1), (1, 0, 1), (2, 0, 1)):
            product(b, c, term)
        combine(0)
        combine(2)
        project_entity(3, 1, 4)
        project_relation(3, 1, 2)
        project_entity(4, 1, 7)
        project_relation(4, 0, 4)
        project_relation(4, 1, 3)
        turn_terms(1, HR, (0,), (1, 0))
        project_entity(5, 1, 5)
        turn_terms(1, HI, (7,))
        new_terms(3)
        multiply_block(3)
        project_relation(5, 0, 1)
        turn_terms(3, HR, (6,), (1, 0))
        turn_pairs(0, 5)
        project_relation(5, 1, 2)
        project_entity(6, 1, 7)
        new_terms(4, ari_tag="before_pause")
        multiply_block(4)
        combine(4)
        project_relation(6, 0, 4)
        turn_terms(3, HI, (0,), (1, 0))
        turn_pairs(2, 5)
        project_relation(6, 1, 3)
        project_entity(7, 0, 6)
        new_terms(5)
        new_terms(6, ari_tag="last_add")
        multiply_block(5)
        project_relation(7, 0, 1)
        turn_terms(5, HR, (7,), (1, 0))
        project_relation(7, 1, 2)
        project_entity(7, 1, 0)
        turn_terms(5, HI, (6,), (1, 0))
        for c, term in ((0, 0), (0, 1), (1, 0)):
            product(6, c, term)
        turn_pairs(4, 5)

        new_codes((0, 1, 2, 3), "before_pause", "aei6")
        quantise(0, 4)
        product(6, 1, 1)
        combine_parts(6, "turned0")
        score(0, 2, 7)
        score(2, 2, 0)

        new_terms(7)
        multiply_block(7)
        last_turns = [bank(number, [P, PACK, P]) for number in (4, 3)]
        turn_term(last_turns[0], 7, 0, 0, True)
        turn_term(last_turns[1], 7, 1, 0, True)
        turn_pairs(6, 6, HR)
        turn_term(last_turns[0], 7, 0, 1, False)
        round_turned(last_turns[0], 7, 0)
        new_codes((4, 5, 6, 7), "last_add", "planes_end")
        quantise(4, 2)
        turn_term(last_turns[1], 7, 1, 1, False)
        round_turned(last_turns[1], 7, 1)
        turn_pairs(6, 1, HI, nc.vector.tensor_copy)
        score(4, 2, 5)
        quantise(7, 1, HR)
        quantise(6, 1)
        last_sums = [bank(number, [P, P]) for number in (2, 6)]
        for g in range(2):
            score_pass(last_sums[g][:], 7, 1, g, 0)
        score(6, 1, 7, nc.vector.tensor_copy)
        quantise(7, 1, HI)
        for g in range(2):
            score_pass(last_sums[g][:], 7, 1, g, 1)
        last_result = kept([P, 2, P], F32, "result7")
        for g, copy in enumerate((nc.scalar.copy, nc.vector.tensor_copy)):
            copy(last_result[:, g], last_sums[g][:])
        store(7, 1, last_result)
